import numpy as np, ml_dtypes
CORES = [6,15,38,47]
N = 4
import mx_ref
BF = ml_dtypes.bfloat16
def gentries(a):
    return np.ascontiguousarray(a.reshape(8, 16, -1).transpose(0, 2, 1)).reshape(8, -1)
def gtable(e):
    e = np.asarray(e); return np.ascontiguousarray(e.reshape(8, -1, 16).transpose(0, 2, 1)).reshape(128, -1).astype(np.int32)
def gcols(t, e):
    v = np.concatenate([t.reshape(8, 16, -1, 4), np.zeros((8, 16, 1, 4), BF)], axis=2)
    return np.ascontiguousarray(np.stack([v[g][:, e[g]] for g in range(8)])).reshape(128, -1)
def tile(rs):
    return np.stack(rs, axis=2).reshape(128, -1).astype(BF)
def pick(q, e):
    c = np.concatenate([q[0].reshape(128, -1, 4), np.zeros((128, 1, 4), np.uint8)], axis=1); s = np.concatenate([q[1], np.ones((16, 1), np.uint8)], axis=1)
    return (np.ascontiguousarray(c[:, e].reshape(128, -1)), np.ascontiguousarray(s[:, e]))
def join(*qs):
    return (np.concatenate([q[0] for q in qs], axis=1), np.concatenate([q[1] for q in qs], axis=1))
def put(q, e, v):
    c, s = q[0].reshape(128, -1, 4).copy(), q[1].copy(); c[:, e] = v[0].reshape(128, -1, 4); s[:, e] = v[1]
    return (c.reshape(128, -1), s)
def pk(c, s):
    return (np.ascontiguousarray(c), mx_ref.live(s))
def emit(q):
    return q[0], q[1]
def packed(v, rng):
    q = [mx_ref.quantize(np.ascontiguousarray(v[r])) for r in range(N)]
    return np.stack([a for a, b in q]), np.stack([mx_ref.plane(b, rng) for a, b in q])
def values_of_codes():
    e, c = np.zeros((128, 128, 4), np.float32), np.zeros((128, 2, 4), np.uint8)
    e[np.arange(128), np.arange(128), 0] = 1
    c[:127, :, 0] = np.arange(256).reshape(2, 128).T[:127]
    return mx_ref.matmul(mx_ref.quantize(e.reshape(128, 512).astype(BF)), (c.reshape(128, 8), np.full((16, 2), 127, np.uint8))).T.reshape(-1).astype(np.float64)
CODE_VALUE, SCALE_VALUE = values_of_codes(), 2.0 ** (np.arange(256) - 127.0)
def decode(q):
    return (CODE_VALUE[q[0]].reshape(16, 8, -1, 4) * SCALE_VALUE[q[1]][:, None, :, None] + 0.0).reshape(128, -1).astype(np.float32)
def f(rng, *shape):
    return mx_ref.flush((rng.standard_normal(shape, dtype=np.float32) * np.exp2(rng.integers(-2, 3, shape[:-1] + (1,)))).astype(BF))
def wide(rng, *shape, cols=0):
    v = rng.standard_normal(shape, dtype=np.float32) * np.exp2(rng.integers(-12, 13, shape)).astype(np.float32)
    if cols: v *= np.repeat(np.exp2(rng.integers(-cols, cols + 1, shape[:-2] + (1, shape[-1] // 4))) * (rng.random(shape[:-2] + (1, shape[-1] // 4)) > 0.0625), 4, axis=-1).astype(np.float32)
    return mx_ref.flush(v.astype(BF))
C, A, R = 320, 256, 3
STEP = [1, 2, 3]
def nearest(s, a, b):
    at = lambda e: np.abs(s - np.take_along_axis(s, e, axis=1))
    return np.where(at(b) < at(a), b, a)
def depths(b):
    k = np.zeros((8, C), int)
    for i in range(1, C): k[:, i] = (k[np.arange(8), b[:, i]] + 1) % 4
    return k
def gput(t, e, h):
    a, b = t.reshape(8, 16, -1, 4).copy(), h.reshape(8, 16, -1, 4)
    for g in range(8): a[g][:, e[g]] = b[g]
    return a.reshape(128, -1)
def big(v):
    v = v.astype(np.float32)
    v[np.abs(v) < np.float32(2.0 ** -16)] = 0
    return v.astype(BF)
def numbers_of(rng):
    return {"x": big(f(rng, N, 128, 4 * C)), "u": np.array(f(rng, N, 128, 512)), "v": np.array(f(rng, N, 128, 512))}
def layers(rng):
    return big(f(rng, N, 128, 2048)).reshape(N, 8, 16, 4, 8, 16, 4)
def weights(rng, w):
    c, p = packed(np.ascontiguousarray(w).reshape(N, 128, 2048), rng)
    return {"wc": c, "ws": p}
def listed(a, b):
    return np.stack([gtable(np.concatenate([a[r], b[r]], axis=1)) for r in range(N)])
def candidates(rng):
    reach = np.stack([np.where(rng.permutation(8) < 4, C, 8) for r in range(N)])[:, :, None]
    n = np.minimum(np.maximum(np.arange(C), 1), reach)
    a, b = [np.maximum(np.arange(C) - 1 - rng.integers(0, n), 0) for k in range(2)]
    return {"cd": listed(a, b)}
def signs(rng):
    return np.stack([rng.permutation(8) % 2 * 2.0 - 1.0 for r in range(N)])
def setup_inputs(rng):
    return {**numbers_of(rng), **weights(rng, layers(rng)), **candidates(rng)}
def setup_inputs_ties(rng):
    d = numbers_of(rng)
    e = rng.permutation(N)
    x = d["x"].reshape(N, 8, 16, C, 4)
    for r in range(N):
        k = np.zeros(C, int) if r == e[0] else rng.permutation(C) % 3
        a = x[r][:, :8, :3].copy()
        a[:, :, 2] = 0
        x[r][:, :8] = a[:, :, k]
    x[e[1]] = 0
    u = d["u"].reshape(N, 8, 16, 128, 4)
    u[:, :, 8:, ::16] = 0
    w = layers(rng)
    w[:, :, :, :, :, :8] = 0
    return {"x": x.reshape(N, 128, 4 * C), "u": u.reshape(N, 128, 512), "v": d["v"], **weights(rng, w), **candidates(rng)}
def setup_inputs_near(rng):
    d = numbers_of(rng)
    x = np.zeros((N, 8, 16, C, 4), np.float32)
    u = d["u"].reshape(N, 128, 128, 4)
    u[:, :, ::16] = 0
    o, c = rng.permutation(N) % 4, signs(rng)
    for r in range(N):
        m = np.full((8, 1), 256)
        m[np.argsort(c[r], kind="stable")[::2]] = 4
        s = rng.integers(0, m, (8, C))
        size = 1.0 if o[r] < 2 else 2.0 ** -7
        g = ((s[:, :, None] >> np.arange(8)) & 1) * np.exp2(np.arange(8) - 23.0) * size
        if o[r] < 3: x[r, :, 0, :, 0] = c[r][:, None] * rng.integers(0, 2, (8, C)) * size
        x[r, :, 8] = g[:, :, :4]
        x[r, :, 9] = g[:, :, 4:]
        x[r, :, 10:] = rng.integers(4, 8, (8, 6, C, 4)) * 2.0 ** -22 * size
        k = 1.0 if o[r] == 0 else 2.0 ** -30
        for h in range(0, 128, 16):
            u[r, h, h, 0] = k
            u[r, h + 8:h + 10, h] = k
    w = layers(rng)
    w[:, :, :10] = 0
    w[:, :, :, :, :, :10] = 0
    return {"x": x.reshape(N, 128, 4 * C).astype(BF), "u": u.reshape(N, 128, 512), "v": d["v"], **weights(rng, w), **candidates(rng)}
def setup_inputs_huge(rng):
    d = numbers_of(rng)
    z = rng.permutation(N) < N // 2
    k = np.stack([rng.choice([-1.0, -0.25] if z[r] else [-1.0, -0.5, 0.5, 1.0], C) for r in range(N)])
    x = 2.0 ** 28 * (0.8 + 0.2 * rng.random((N, 128, C, 4))) * k[:, None, :, None]
    u = d["u"].reshape(N, 128, 128, 4)
    a = 2.0 ** 30 * (1 - 0.25 * rng.random((N, 128, 8, 4))) * signs(rng)[:, None, :, None]
    u[:, :, ::16] = a.astype(np.float32).astype(BF)
    w = np.zeros((N, 128, 4, 128, 4), np.float32)
    i = np.arange(128)
    for b in range(4): w[:, i, b, i, b] = -1
    return {"x": x.astype(np.float32).reshape(N, 128, 4 * C).astype(BF), "u": u.reshape(N, 128, 512), "v": d["v"], **weights(rng, w.astype(BF)), **candidates(rng)}
def shape(rng, k):
    if k == 0: return np.maximum(np.arange(C) - 1, 0)
    if k == 1: return np.zeros(C, int)
    if k == 8:
        b = np.full(C, 1)
        b[:2] = 0
        return b
    if k == 9:
        n = A - 24
        b = np.full(C, 3)
        b[:4] = 0, 0, 1, 2
        b[n + 3:n + 11] = n - 5 + rng.permutation(8)
        b[n + 11:n + 19] = n + 3 + rng.permutation(8)
        b[n + 19:] = n + 11 + rng.integers(0, 8, C - n - 19)
        return b
    n = [C - 3, A, A - 1, A + 1, A - 2, 1][k - 2]
    b = rng.integers(0, 3, C) if k in (3, 4, 5) else np.full(C, 2)
    b[:4] = 0, 0, 1, 2
    b[4 + rng.permutation(C - 4)[:n - 1]] = 3
    return b
def setup_inputs_trees(rng):
    d = setup_inputs(rng)
    m = rng.permutation(10)
    b = np.stack([np.stack([shape(rng, k) for k in rng.permutation(np.delete(np.arange(10), [m[r], m[r - 1]]))]) for r in range(N)])
    d["cd"] = listed(b, b)
    return d
def setup_inputs_spread(rng):
    d = setup_inputs(rng)
    d["x"] = big(wide(rng, N, 128, 4 * C, cols=6))
    return d
def check_inputs(d):
    b = []
    for k in ("x", "u", "v"):
        a = np.abs(d[k].astype(np.float32))
        if not (np.isfinite(a).all() and ((a == 0) | (a >= 2.0 ** -30) & (a <= 2.0 ** 30)).all()): b.append("a value of " + k)
    none, least, most = [emit(mx_ref.quantize(np.full((128, 16), k, np.float32).astype(BF)))[1][0, 0] for k in (0.0, 2.0 ** -30, 2.0 ** 30)]
    for r in range(N):
        if ((d["wc"][r] == 0x7F) | (d["wc"][r] == 0xFF)).any(): b.append("wc: a code that is no number")
        s = mx_ref.live(d["ws"][r])
        if ((s != none) & ((s < least) | (s > most))).any(): b.append("ws: a scale out of range")
        e = gentries(d["cd"][r]).reshape(8, 2, C)
        if ((e < 0) | (e > np.maximum(np.arange(C) - 1, 0))).any(): b.append("cd: a candidate that isn't lower")
    return b
def reference(x, u, v, wc, ws, cd):
    qu = [mx_ref.quantize(u[r]) for r in range(N)]
    lay = [pk(wc[r], ws[r]) for r in range(N)]
    can = [gentries(cd[r]) for r in range(N)]
    now = [x[r] for r in range(N)]
    for t in range(R):
        held, took, depth, base, sent = [], [], [], [], []
        for r in range(N):
            q = mx_ref.quantize(now[r])
            b = nearest(mx_ref.matmul(qu[r], q)[::16], can[r][:, :C], can[r][:, C:])
            k = depths(b)
            o = np.argsort(k, axis=1, kind="stable")[:, :A]
            place = np.zeros((8, C), int)
            np.put_along_axis(place, o, np.arange(A)[None], axis=1)
            k, b = np.take_along_axis(k, o, axis=1), np.take_along_axis(b, o, axis=1)
            h = decode(q).astype(BF)
            p = gcols(h, o).astype(np.float32) - gcols(h, np.where(k > 0, b, -1)).astype(np.float32)
            sent.append(mx_ref.quantize(p.astype(BF)))
            held.append(h)
            took.append(o)
            depth.append(k)
            base.append(np.take_along_axis(place, b, axis=1))
        made = []
        for r in range(N):
            e = (r - STEP[t]) % N
            m = decode(sent[e]).astype(BF)
            for k in (1, 2, 3): m = (m.astype(np.float32) + gcols(m, np.where(depth[e] == k, base[e], -1)).astype(np.float32)).astype(BF)
            q = mx_ref.quantize(m)
            z = gcols(held[r], took[r])
            h = tile([mx_ref.matmul(pick(lay[r], np.arange(128 * b, 128 * b + 128)), q) * np.float32(0.015625) + z[:, b::4].astype(np.float32) for b in range(4)])
            made.append(gput(held[r], took[r], h))
        now = made
    y = np.zeros((N, 128, C), np.float32)
    oc, osc = np.zeros((N, 128, 4 * C), np.uint8), np.zeros((N, 16, C), np.uint8)
    for r in range(N):
        q = mx_ref.quantize(now[r])
        y[r] = mx_ref.matmul(mx_ref.quantize(v[r]), q)
        oc[r], osc[r] = emit(q)
    return {"y": y, "oc": oc, "osc": osc}

@@ -1,0 +1,497 @@
+from concourse.mybir import dt, AluOpType as ALU, ActivationFunctionType as ACT
+
+C, A, R = 320, 256, 3
+STEP = [1, 2, 3]
+CODE = "float8_e4m3fn_x4"
+H16 = "float16"
+Z = 16
+PW = Z + C
+SH = PW // 2
+KEEP = 1024.0
+MWW = 272
+LOW = 128
+RUNS = [(0, 32), (32, 64), (64, 96), (96, 128), (128, 192), (192, 256), (256, 320)]
+
+
+def _sb(n, d):
+    return ("sbuf", [128, n], d)
+
+
+SCRATCH = {
+    "xs": _sb(4 * C, "bfloat16"), "us": _sb(512, "bfloat16"), "vs": _sb(512, "bfloat16"),
+    "wq": _sb(512, CODE), "wsc": _sb(512, "uint8"), "cdi": _sb(40, "int32"), "cdo": _sb(48, "uint16"),
+    "qu": _sb(128, CODE), "su": _sb(128, "uint8"), "qup": _sb(128, CODE), "sup": _sb(128, "uint8"),
+    "qv": _sb(128, CODE), "sv": _sb(128, "uint8"), "uoff": _sb(16, "uint16"),
+    "ebig": _sb(528, "bfloat16"), "ones": _sb(128, "bfloat16"), "qe": _sb(512, CODE), "se": _sb(512, "uint8"),
+    "a16": _sb(24, "int32"), "b16": _sb(24, "int32"), "e0": _sb(16, "float32"), "e1": _sb(16, "float32"),
+    "cps": _sb(16, "float32"), "i16": _sb(24, "float32"), "iw": _sb(24, "float32"), "kc": _sb(16, "float32"),
+    "hk": _sb(C, "bfloat16"), "hk2": _sb(A, "bfloat16"), "iot": _sb(C, "bfloat16"), "i1k": _sb(C, "float32"),
+    "c1": _sb(C, "bfloat16"), "cdf": _sb(2 * C, H16), "flg": _sb(2 * C, "bfloat16"), "zer": _sb(4 * C, "bfloat16"),
+    "sc": _sb(C, "float32"), "sc2": _sb(C, "float32"), "d1": _sb(C, "float32"), "g2": _sb(C, "float32"), "d2": _sb(C, "float32"),
+    "a1": _sb(C, "float32"), "a2": _sb(C, "float32"),
+    "w1": _sb(2 * PW, "bfloat16"), "w2": _sb(PW, "bfloat16"), "wa": _sb(PW, "bfloat16"), "wb": _sb(PW, "bfloat16"),
+    "lab": _sb(PW, "bfloat16"), "hb": _sb(C, H16), "hh": _sb(C, H16), "hl": _sb(C, H16),
+    "offa": _sb(32, "uint16"), "offb": _sb(32, "uint16"),
+    "bq": _sb(24, "float32"), "qf": _sb(40, "float32"), "qq": _sb(48, "uint16"),
+    "ef": _sb(4 * C, "bfloat16"), "cum": _sb(4 * C, "bfloat16"), "val": _sb(C, "float32"), "pl": _sb(C, "bfloat16"),
+    "plo": _sb(32, "uint16"), "oo": _sb(32, "uint16"), "srt": _sb(C, "float32"), "h2": _sb(C, "float32"), "sg": _sb(16, "float32"),
+    "adj": _sb(16, "float32"), "vi": _sb(16, "int32"), "li": _sb(16, "int32"),
+    "fd": _sb(4 * 2 * C, "bfloat16"), "gd": _sb(4 * C, "bfloat16"), "fo": _sb(4 * C, "bfloat16"), "zx": _sb(4 * C, "bfloat16"),
+    "mw": _sb(12 * MWW, "bfloat16"), "gb": _sb(4 * A, "bfloat16"), "ys": _sb(C, "float32"),
+    "ps": ("psum", [128, 512 * 8], "float32"),
+}
+for _r in range(R + 1):
+    SCRATCH["qx%d" % _r] = _sb(C, CODE)
+    SCRATCH["sx%d" % _r] = _sb(C, "uint8")
+for _r in range(R):
+    SCRATCH["xn%d" % _r] = _sb(4 * C, "bfloat16")
+    SCRATCH["lq%d" % _r] = _sb(C, CODE)
+    SCRATCH["ls%d" % _r] = _sb(C, "uint8")
+    SCRATCH["lb%d" % _r] = _sb(32, "uint16")
+    SCRATCH["ll%d" % _r] = _sb(32, "uint16")
+    SCRATCH["ob%d" % _r] = _sb(32, "uint16")
+    SCRATCH["ol%d" % _r] = _sb(32, "uint16")
+    SCRATCH["pt%d" % _r] = _sb(4 * A, "bfloat16")
+    SCRATCH["qp%d" % _r] = _sb(A, CODE)
+    SCRATCH["sp%d" % _r] = _sb(A, "uint8")
+    SCRATCH["mt%d" % _r] = _sb(4 * A, "bfloat16")
+    SCRATCH["qm%d" % _r] = _sb(A, CODE)
+    SCRATCH["sm%d" % _r] = _sb(A, "uint8")
+
+SEMAPHORES = (["cV", "cS", "cP", "cG", "sent", "l_cd", "l_u", "l_xa", "l_xb", "l_v", "l_wc", "l_ws", "outS", "outY"]
+              + ["a%s%d" % (k, r) for k in "qblm" for r in range(R)])
+
+REBUILD = [("cv", 2, 0), ("g", 3, 1), ("g", 2, 1), ("cv", 1, 0), ("cs", 0, 0), ("g", 1, 1), ("a", 3, 1), ("v", 3, 2), ("a", 2, 1),
+           ("g", 0, 1), ("v", 3, 3), ("g", 2, 2), ("a", 1, 1), ("a", 0, 1), ("v", 1, 2), ("g", 0, 2), ("a", 2, 2), ("a", 0, 2),
+           ("g", 1, 3), ("v", 2, 3), ("g", 0, 3), ("a", 1, 3), ("a", 0, 3)]
+
+
+def _plan():
+    return {"ops": [], "w": {}, "r": {}}
+
+
+def _add(pl, eng, fn, reads, writes, kind="c", sem=None, total=0):
+    ops, n = pl["ops"], len(pl["ops"])
+    deps = set()
+    for k in reads:
+        if k in pl["w"]:
+            deps.add(pl["w"][k])
+        if k.startswith("bank"):
+            deps.update(j for j in pl["r"].get(k, []) if ops[j]["eng"] != eng)
+    for k in writes:
+        if k in pl["w"]:
+            deps.add(pl["w"][k])
+        deps.update(pl["r"].get(k, []))
+    for k in reads:
+        pl["r"].setdefault(k, []).append(n)
+    for k in writes:
+        pl["w"][k] = n
+        pl["r"][k] = []
+    ops.append({"eng": eng, "fn": fn, "deps": deps, "kind": kind, "sem": sem, "total": total})
+
+
+def _emit(pl, g, T):
+    ops = pl["ops"]
+    queue = {"V": g.vector, "S": g.scalar, "P": g.tensor, "G": g, "Y": g.sync}
+    known = {e: {} for e in queue}
+    for n, op in enumerate(ops):
+        op["line"] = op["eng"] if op["kind"] == "c" else "d%d" % n
+        op["waits"] = []
+        if op["kind"] == "in":
+            op["clock"] = {op["line"]: n}
+            continue
+        kn = known[op["eng"]]
+        for j in sorted(op["deps"], reverse=True):
+            d = ops[j]
+            if d["kind"] == "send" or kn.get(d["line"], -1) >= j:
+                continue
+            op["waits"].append(j)
+            d["signals"] = True
+            for line, m in d["clock"].items():
+                kn[line] = max(kn.get(line, -1), m)
+        op["clock"] = dict(kn)
+        op["clock"][op["line"]] = n
+    count = {e: 0 for e in queue}
+    for op in ops:
+        if op["kind"] == "c" and op.get("signals"):
+            count[op["eng"]] += 1
+            op["sem"], op["total"] = "c" + op["eng"], count[op["eng"]]
+    for op in ops:
+        if op["kind"] == "in":
+            continue
+        q = queue[op["eng"]]
+        for j in op["waits"]:
+            q.wait_ge(T.sem[ops[j]["sem"]], ops[j]["total"])
+        ins = op["fn"]()
+        if op["kind"] == "dma":
+            ins.then_inc(T.sem[op["sem"]], 16)
+        elif op["kind"] == "c" and op.get("signals"):
+            ins.then_inc(T.sem[op["sem"]], 1)
+
+
+def rank_program(g, core, T, topo):
+    rank = T.rank_of(core)
+    if rank is None:
+        return
+    n_ranks = len(T.cores)
+    pl = _plan()
+    V, S = g.vector, g.scalar
+    sent = [0]
+    H, HA = C // 2, A // 2
+    halves = (("a", 0, H), ("b", H, C))
+
+    def v(fn, reads, writes):
+        _add(pl, "V", fn, reads, writes)
+
+    def s(fn, reads, writes):
+        _add(pl, "S", fn, reads, writes)
+
+    def gp(fn, reads, writes):
+        _add(pl, "G", fn, reads, writes)
+
+    def load(eng, out, in_, sem, key, after=()):
+        q = S if eng == "S" else g.sync
+        _add(pl, eng, lambda: q.dma_start(out, in_), list(after), [key], kind="dma", sem=sem, total=16)
+
+    def bank(b, n):
+        return T.ps[:, 512 * b:512 * b + n]
+
+    def mm(b, wq, ws, xq, xs_, n, reads):
+        _add(pl, "P", lambda: g.tensor.matmul_mx(bank(b, n), wq, ws, xq, xs_, True, True), reads, ["bank%d" % b])
+
+    def send(dst, out, in_, sem, reads):
+        rid, pid, _ = topo.addr(dst)
+        sent[0] += len(topo.engines(core, dst))
+        _add(pl, "G", lambda: g.remote_dma(out, in_, T.sem[sem], T.sem.sent, pid, rid, topo.mask(core, dst)), reads, [], kind="send")
+
+    def arrives(src, sem, writes, keys):
+        _add(pl, "G", None, [], keys, kind="in", sem=sem, total=writes * len(topo.engines(src, core)))
+
+    def vts(out, in0, s1, s2, op0, op1, reads, writes):
+        if op1 is None:
+            v(lambda: V.tensor_scalar(out, in0, s1, None, op0), reads, writes)
+        else:
+            v(lambda: V.tensor_scalar(out, in0, s1, s2, op0, op1), reads, writes)
+
+    def vtt(out, in0, in1, op, reads, writes):
+        v(lambda: V.tensor_tensor(out, in0, in1, op), reads, writes)
+
+    def vcp(out, in_, reads, writes):
+        v(lambda: V.tensor_copy(out, in_), reads, writes)
+
+    def vset(ap, c, writes):
+        v(lambda: V.memset(ap, c), [], writes)
+
+    def scan(out, d0, d1, first, op0, op1, reads, writes):
+        v(lambda: V.tensor_tensor_scan(out, d0, d1, first, op0, op1), reads, writes)
+
+    def act(out, in_, reads, writes, func=ACT.Copy, **kw):
+        s(lambda: S.activation(out, in_, func, **kw), reads, writes)
+
+    def times(eng, out, in_, c, reads, writes):
+        if eng == "S":
+            act(out, in_, reads, writes, scale=c)
+        else:
+            vts(out, in_, c, None, ALU.mult, None, reads, writes)
+
+    def iota(out, pattern, base, cm, key, small=True):
+        if small:
+            gp(lambda: g.iota(out, pattern, base, cm, allow_small_or_imprecise_dtypes=True), [], [key])
+        else:
+            gp(lambda: g.iota(out, pattern, base, cm), [], [key])
+
+    def wrap(out, data, reads, key, keep, kkey="hk"):
+        scan(out, keep, data, 0.0, ALU.add, ALU.max, reads + [kkey], key if isinstance(key, list) else [key])
+
+    def quant(q, sc, in_, reads, writes):
+        v(lambda: V.quantize_mx(q, sc, in_), reads, writes)
+
+    def col(j):
+        return T.cps[:, j:j + 1]
+
+    load("S", T.us[:], T.u[:], "l_u", "us")
+    load("Y", T.cdi[:], T.cd[:], "l_cd", "cdi")
+    load("Y", T.xs[:, 0:4 * H], T.x[:, 0:4 * H], "l_xa", "xs.a")
+    load("Y", T.xs[:, 4 * H:4 * C], T.x[:, 4 * H:4 * C], "l_xb", "xs.b")
+    load("Y", T.wq[:].bitcast(dt.uint8), T.wc[:], "l_wc", "wq", after=["xs.a", "xs.b"])
+    load("Y", T.wsc[:], T.ws[:], "l_ws", "wsc")
+    load("Y", T.vs[:], T.v[:], "l_v", "vs")
+
+    iota(T.i16[:, 0:20], [[16, 20]], 0, 0, "i16")
+    iota(T.a16[:, 0:16], [[1, 16]], 128, -1, "a16", small=False)
+    iota(T.a16[:, 16:17], [[1, 1]], 0, 1, "a16p", small=False)
+    iota(T.ones[:], [[0, 128]], 1, 0, "ones")
+    vset(T.ebig[:], 0.0, ["ebig"])
+    gp(lambda: g.affine_select(T.ebig[:, 3:515:4], T.ones[:], [[-1, 128]], ALU.is_equal, 0.0, 0, 1), ["ones"], ["ebig"])
+    iota(T.iot[:], [[1, C]], Z - SH, 0, "iot")
+    iota(T.w1[:, 0:2 * Z], [[1, Z], [0, 2]], -SH - 1, 0, "w1z")
+    iota(T.w2[:, 0:Z], [[0, 4], [-2, 2], [1, 2]], 2 - SH, 0, "w2z")
+    iota(T.wa[:, 0:Z], [[1, Z]], -SH, 0, "waz")
+    iota(T.wb[:, 0:Z], [[1, Z]], -SH, 0, "wbz")
+    iota(T.lab[:, 0:Z], [[0, 4], [C, 4]], 0, 0, "labz")
+    iota(T.i1k[:], [[1024, C]], 0, 0, "i1k")
+
+    vset(T.flg[:], 0.0, ["flg.a", "flg.b"])
+    vcp(T.uoff[:, 0:8], T.i16[:, 0:8], ["i16"], ["uoff"])
+    vts(T.b16[:, 0:17], T.a16[:, 0:17], 15, None, ALU.bitwise_and, None, ["a16", "a16p"], ["b16"])
+    vset(T.mw[:, A:12 * MWW:MWW], 0.0, ["mwz"])
+    vts(T.e0[:], T.b16[:, 0:16], 0.0, -4 * KEEP, ALU.is_equal, ALU.mult, ["b16"], ["e0"])
+    vts(T.e1[:], T.b16[:, 0:16], 1.0, KEEP, ALU.is_equal, ALU.mult, ["b16"], ["e1"])
+    vcp(col(8), T.b16[:, 16:17], ["b16"], ["cp8"])
+    vtt(T.hk[:, 0:16], T.e0[:], T.e1[:], ALU.add, ["e0", "e1"], ["hk"])
+    vset(T.zer[:], 0.0, ["zer"])
+    for j, (m, c0) in enumerate([(1.0, SH + 0.5), (1.0, SH), (1.0, SH - Z), (2.0, SH - Z - C), (1.0, H),
+                                 (2048.0, H + (A + 1024 * C) // 2), (1.0, 0), (2048.0, H)]):
+        act(col(j), T.e1[:, 0:1], ["e1"], ["cp%d" % j], func=ACT.Identity, bias=float(c0 - m * KEEP), scale=m)
+    cp_pair, cp_ptr, cp_base, cp_bq, cp_place, cp_adj, cp_none, cp_own = [col(j) for j in range(8)]
+    for a, b in ((16, 32), (32, 64), (64, 128), (128, 256), (256, 320)):
+        act(T.hk[:, a:b], T.hk[:, 0:b - a], ["hk"], ["hk"])
+    for b in range(4):
+        quant(T.qe[:, 128 * b:128 * b + 128], T.se[:, 128 * b:128 * b + 128], T.ebig[:, 3 - b:515 - b], ["ebig"], ["qe%d" % b])
+    vcp(T.cdo[:, 0:40], T.cdi[:], ["cdi"], ["cdo"])
+    quant(T.qu[:], T.su[:], T.us[:], ["us"], ["qu"])
+    act(T.c1[:], T.iot[:].indirect(T.cdo[:, 0:20]), ["iot", "cdo"], ["c1"])
+    vcp(T.qup[:].bitcast(dt.uint32), T.qu[:].bitcast(dt.uint32).indirect(T.uoff[:, 0:8]), ["qu", "uoff"], ["qup"])
+    act(T.sup[:], T.su[:].indirect(T.uoff[:, 0:8]), ["qu", "uoff"], ["sup"])
+    vtt(T.cdf[:, 0:2 * C:2], T.iot[:].indirect(T.cdo[:, 20:40]), T.c1[:], ALU.subtract, ["iot", "cdo", "c1"], ["cdf0"])
+    vset(T.w1[:, 1:2], 3.0 - SH, ["w1z"])
+
+    def unpack(b, into, q, sc, n, reads):
+        mm(into, T.qe[:, 128 * b:128 * b + 128], T.se[:, 128 * b:128 * b + 128], q, sc, n, reads + ["qe%d" % b])
+
+    def layer(b, into, q, sc, n, reads):
+        mm(into, T.wq[:, 128 * b:128 * b + 128], T.wsc[:, 128 * b:128 * b + 128], q, sc, n, reads + ["wq", "wsc"])
+
+    xt, xkeys = T.xs, (["xs.a"], ["xs.b"])
+    for r in range(R + 1):
+        qx, sx = T["qx%d" % r], T["sx%d" % r]
+        ka, kb = "qx%d.a" % r, "qx%d.b" % r
+        side = (T.qup[:], T.sup[:], ["qup", "sup"]) if r < R else (T.qv[:], T.sv[:], ["qv"])
+        quant(qx[:, 0:H], sx[:, 0:H], xt[:, 0:4 * H], xkeys[0], [ka])
+        for bk in ((4, 6) if r < R else (4,)):
+            mm(bk, side[0], side[1], qx[:, 0:H], sx[:, 0:H], H, side[2] + [ka])
+        if r == 0:
+            vset(T.c1[:, 0:1], 3.0 - SH, ["c1"])
+        quant(qx[:, H:C], sx[:, H:C], xt[:, 4 * H:4 * C], xkeys[1], [kb])
+        mm(5, side[0], side[1], qx[:, H:C], sx[:, H:C], H, side[2] + [kb])
+        if r == R:
+            break
+        dst, src = T.cores[(rank + STEP[r]) % n_ranks], T.cores[(rank - STEP[r]) % n_ranks]
+        lq, ls, lb, ll, ob, ol = [T["%s%d" % (k, r)] for k in ("lq", "ls", "lb", "ll", "ob", "ol")]
+        pt, qp, sp, mt, qm, sm, xn = [T["%s%d" % (k, r)] for k in ("pt", "qp", "sp", "mt", "qm", "sm", "xn")]
+        send(dst, lq[:].bitcast(dt.uint8), qx[:].bitcast(dt.uint8), "aq%d" % r, [ka, kb])
+        send(dst, ls[:], sx[:], "aq%d" % r, [ka, kb])
+        arrives(src, "aq%d" % r, 2, ["lq"])
+        arrives(src, "ab%d" % r, 1, ["lb"])
+        arrives(src, "al%d" % r, 1, ["ll"])
+        arrives(src, "am%d" % r, 1, ["lm"])
+
+        vcp(T.sc[:, 0:H], bank(4, H), ["bank4"], ["sc.a"])
+        act(T.sc2[:, 0:H], bank(6, H), ["bank6"], ["sc2.a"])
+        act(T.sc[:, H:C], bank(5, H), ["bank5"], ["sc.b"])
+        act(T.sc2[:, H:C], bank(5, H), ["bank5"], ["sc2.b"])
+        if r == 0:
+            vcp(T.cdf[:, 1:2 * C:2], T.c1[:], ["c1"], ["cdf1"])
+        vtt(T.d1[:, 0:H], T.sc[:, 0:H].indirect(T.cdo[:, 0:10]), T.sc2[:, 0:H], ALU.subtract, ["sc.a", "sc2.a", "cdo"], ["d1.a"])
+        vtt(T.d2[:, 0:H], T.sc[:, 0:H].indirect(T.cdo[:, 20:30]), T.sc2[:, 0:H], ALU.subtract, ["sc.a", "sc2.a", "cdo"], ["d2.a"])
+        act(T.g2[:, H:C], T.sc[:].indirect(T.cdo[:, 30:40]), ["sc.a", "sc.b", "cdo"], ["g2"])
+        vtt(T.d1[:, H:C], T.sc[:].indirect(T.cdo[:, 10:20]), T.sc2[:, H:C], ALU.subtract, ["sc.a", "sc.b", "sc2.b", "cdo"], ["d1.b"])
+        vtt(T.d2[:, H:C], T.g2[:, H:C], bank(5, H), ALU.subtract, ["g2", "bank5"], ["d2.b"])
+        for h, a, b in halves:
+            act(T.a1[:, a:b], T.d1[:, a:b], ["d1." + h], ["a1." + h], func=ACT.Abs)
+            act(T.a2[:, a:b], T.d2[:, a:b], ["d2." + h], ["a2." + h], func=ACT.Abs)
+        for b in (0, 2, 3, 1):
+            unpack(b, 4 + b, qx[:], sx[:], C, [ka, kb])
+
+        def mine(b):
+            act(T.fo[:, C * b:C * b + C], bank(4 + b, C), ["bank%d" % (4 + b)], ["fo%d" % b])
+
+        for h, a, b in halves:
+            vtt(T.flg[:, 2 * a + 1:2 * b:2], T.a2[:, a:b], T.a1[:, a:b], ALU.is_lt, ["a1." + h, "a2." + h], ["flg." + h])
+        mine(0)
+        mine(1)
+        for h, a, b in halves:
+            scan(T.w1[:, 2 * (Z + a):2 * (Z + b)], T.flg[:, 2 * a:2 * b], T.cdf[:, 2 * a:2 * b], 0.0, ALU.mult, ALU.add,
+                 ["flg." + h, "cdf0", "cdf1"], ["w1." + h])
+        for h, a, b in halves:
+            wrap(T.hb[:, a:b], T.w1[:, 2 * (Z + a) + 1:2 * (Z + b):2], ["w1." + h], "hb." + h, T.hk[:, 0:H])
+        for h, a, b in halves:
+            vts(T.offa[:, a // 16:b // 16], T.hb[:, a + 15:b:16], cp_pair, 2.0, ALU.add, ALU.mult, ["hb." + h, "cp0"], ["offa." + h])
+
+        wins = [("w1", T.w1), ("w2", T.w2), ("wa", T.wa), ("wb", T.wb), ("wa", T.wa), ("wb", T.wb)]
+        offs = [("offa", T.offa), ("offb", T.offb)]
+        for d in range(5):
+            (k0, w0), (k1, w1_), (ko, of), (kn, on) = wins[d], wins[d + 1], offs[d % 2], offs[(d + 1) % 2]
+            low = (2 if d == 0 else 1) * (Z + H)
+            act(w1_[:, Z + H:PW], w0[:].indirect(of[:, 10:20]), [k0 + ".a", k0 + ".b", k0 + "z", ko + ".b"], [k1 + ".b"])
+            vcp(w1_[:, Z:Z + H], w0[:, 0:low].indirect(of[:, 0:10]), [k0 + ".a", k0 + "z", ko + ".a"], [k1 + ".a"])
+            if d == 0:
+                vts(ob[:, 0:20], T.hb[:, 15:C:16], cp_base, None, ALU.add, None, ["hb.a", "hb.b", "cp2"], ["ob%d" % r])
+                send(dst, lb[:, 0:20], ob[:, 0:20], "ab%d" % r, ["ob%d" % r])
+            for h, a, b in (halves if d == 0 else halves[::-1]):
+                wrap(T.hh[:, a:b], w1_[:, Z + a:Z + b], [k1 + "." + h], "hh." + h, T.hk[:, 0:H])
+            if d == 0:
+                vts(T.bq[:, 0:20], T.hb[:, 15:C:16], cp_bq, None, ALU.add, None, ["hb.a", "hb.b", "cp3"], ["bq"])
+            for h, a, b in halves[::-1]:
+                vts(on[:, a // 16:b // 16], T.hh[:, a + 15:b:16], cp_ptr, None, ALU.add, None, ["hh." + h, "cp1"], [kn + "." + h])
+
+        def theirs(b):
+            act(T.fd[:, 2 * C * b:2 * C * b + C], bank(b, C), ["bank%d" % b], ["fd%d.f" % b])
+
+        def piece(what, k):
+            a, b = ((0, LOW), (LOW, C))[k]
+            lab, rd = T.lab[:, Z + a:Z + b], ["lab%d" % j for j, (lo, hi) in enumerate(RUNS) if a <= lo < b]
+            if what == "s":
+                act(T.ef[:, a:b], lab, rd, ["ef0.%d" % k], func=ACT.Relu, bias=1.0, scale=-1.0)
+                act(T.ef[:, 3 * C + a:3 * C + b], lab, rd, ["ef3.%d" % k], func=ACT.Relu, bias=1.0 - 3 * C)
+            elif what == "w":
+                wrap(T.hl[:, a:b], lab, rd, "hl.%d" % k, T.hk[:, 0:b - a])
+            else:
+                vts(T.ef[:, what * C + a:what * C + b], lab, float(what * C), None, ALU.is_equal, None, rd, ["ef%d.%d" % (what, k)])
+
+        for b in range(4):
+            unpack(b, b, lq[:], ls[:], C, ["lq"])
+        act(T.wa[:, Z + LOW:PW], T.wb[:].indirect(T.offb[:, LOW // 16:20]), ["wb.a", "wb.b", "wbz", "offb.a", "offb.b"], ["wa.a", "wa.b"])
+        mine(2)
+        for j, (a, b) in enumerate(RUNS):
+            of, ko = (T.offb, ["offb.a"]) if a < LOW else (T.offa, ["offa.a", "offa.b"])
+            vcp(T.lab[:, Z + a:Z + b], T.lab[:, 0:Z + a].indirect(of[:, a // 16:b // 16]),
+                ["labz"] + ko + ["lab%d" % i for i in range(j)], ["lab%d" % j])
+            if r == 0 and j == 0:
+                vts(T.iw[:, 0:20], T.i16[:, 0:20], col(8), cp_none, ALU.add, ALU.add, ["i16", "cp8", "cp6"], ["iw"])
+            if r == 0 and j == 1:
+                vts(T.kc[:], T.i16[:, 0:16], col(8), -(H + 0.5), ALU.add, ALU.add, ["i16", "cp8"], ["kc"])
+            if j == 2:
+                wrap(T.hh[:, LOW:C], T.wa[:, Z + LOW:PW], ["wa.a", "wa.b"], ["hh.a", "hh.b"], T.hk[:, 0:C - LOW])
+            if j == 3:
+                vts(T.offa[:, LOW // 16:20], T.hh[:, LOW + 15:C:16], cp_ptr, None, ALU.add, None, ["hh.a", "hh.b", "cp1"], ["offa.a", "offa.b"])
+                piece(1, 0)
+                piece("s", 0)
+                if r == 0:
+                    act(T.hk2[:], T.hk[:, 0:A], ["hk"], ["hk2"], scale=2048.0)
+            if j == 4:
+                piece(2, 0)
+            if j == 5:
+                piece("w", 0)
+
+        piece("s", 1)
+        mine(3)
+        theirs(0)
+        hl = ["hl.0", "hl.1"]
+        piece("w", 1)
+        piece(1, 1)
+        vtt(T.qf[:, 0:20], T.hl[:, 15:C:16], T.iw[:, 0:20], ALU.add, hl + ["iw"], ["qf0"])
+        vtt(T.qf[:, 20:40], T.hl[:, 15:C:16], T.bq[:, 0:20], ALU.add, hl + ["bq"], ["qf1"])
+        piece(2, 1)
+        vcp(T.qq[:, 0:40], T.qf[:], ["qf0", "qf1"], ["qq"])
+        scan(T.cum[:], T.ef[:], T.zer[:], -(H + 1.0), ALU.add, ALU.add,
+             ["ef%d.%d" % (d, k) for d in range(4) for k in range(2)] + ["zer"], ["cum"])
+        act(T.pl[:], T.cum[:].indirect(T.qq[:, 0:20]), ["cum", "qq"], ["pl"])
+        vtt(T.val[:], T.cum[:].indirect(T.qq[:, 20:40]), T.i1k[:], ALU.add, ["cum", "qq", "i1k"], ["val"])
+        act(T.sg[:], T.kc[:], ["kc", "cum"], ["sg"], func=ACT.Sign, bias=T.cum[:, C - 1:C], scale=-1.0)
+        theirs(1)
+        act(T.adj[:], T.sg[:], ["sg", "cp5"], ["adj"], func=ACT.Identity, bias=cp_adj, scale=(A - 1024.0 * C) / 2)
+        for b in range(4):
+            if b < 2:
+                theirs(b + 2)
+            act(T.gd[:, C * b:C * b + C], T.fd[:, 2 * C * b:2 * C * b + C].indirect(lb[:, 0:20]), ["fd%d.f" % b, "lb"], ["gd%d" % b])
+        wrap(T.hh[:], T.pl[:], ["pl"], ["hh.a", "hh.b"], T.hk[:])
+        vts(T.plo[:, 0:20], T.hh[:, 15:C:16], cp_place, None, ALU.add, None, ["hh.a", "hh.b", "cp4"], ["plo"])
+        vcp(T.srt[:].indirect(T.plo[:, 0:20]), T.val[:], ["val", "plo"], ["srt"])
+        wrap(T.h2[:, 0:A], T.srt[:, 0:A], ["srt"], "h2", T.hk2[:], "hk2")
+        wrap(T.h2[:, A:C], T.srt[:, A:C], ["srt"], "h2t", T.hk2[:, 0:C - A], "hk2")
+        vtt(T.vi[:], T.h2[:, 15:A:16], T.adj[:], ALU.add, ["h2", "adj"], ["vi"])
+        vts(T.oo[:, 0:20], T.h2[:, 15:C:16], cp_own, 1.0 / 1024, ALU.add, ALU.mult, ["h2", "h2t", "cp7"], ["oo"])
+        vts(ol[:, 0:16], T.vi[:], 1.0 / 1024, None, ALU.mult, None, ["vi"], ["ol%d" % r])
+        send(dst, ll[:, 0:16], ol[:, 0:16], "al%d" % r, ["ol%d" % r])
+        vts(T.li[:], T.vi[:], 1023, None, ALU.bitwise_and, None, ["vi"], ["li"])
+
+        def ordered(eng, b):
+            times(eng, T.zx[:, C * b:C * b + C], T.fo[:, C * b:C * b + C].indirect(T.oo[:, 0:20]), 64.0, ["fo%d" % b, "oo"],
+                  ["zx%d.a" % b, "zx%d.b" % b])
+
+        for b in range(4):
+            if b == 2:
+                ordered("V", 0)
+            vtt(T.fd[:, 2 * C * b + C:2 * C * (b + 1)], bank(b, C), T.gd[:, C * b:C * b + C], ALU.subtract,
+                ["bank%d" % b, "gd%d" % b], ["fd%d.d" % b])
+            if b == 0:
+                vcp(ol[:, 16:32], T.li[:], ["li"], ["om%d" % r])
+                send(dst, ll[:, 16:32], ol[:, 16:32], "am%d" % r, ["om%d" % r])
+        ordered("S", 1)
+        if r == 0:
+            quant(T.qv[:], T.sv[:], T.vs[:], ["vs"], ["qv"])
+
+        for b in (2, 0, 3, 1):
+            f = act if b >= 2 else vcp
+            f(pt[:, b:4 * A:4], T.fd[:, 2 * C * b:2 * C * (b + 1)].indirect(ll[:, 0:16]), ["fd%d.f" % b, "fd%d.d" % b, "ll"], ["pt%d" % b])
+        ordered("S", 2)
+        for h, a, bk in (("a", 0, 4), ("b", HA, 5)):
+            quant(qp[:, a:a + HA], sp[:, a:a + HA], pt[:, 4 * a:4 * (a + HA)], ["pt0", "pt1", "pt2", "pt3"], ["qp." + h])
+            unpack(3, bk, qp[:, a:a + HA], sp[:, a:a + HA], HA, ["qp." + h])
+        for b in (2, 1, 0, 3):
+            unpack(b, b, qp[:], sp[:], A, ["qp.a", "qp.b"])
+
+        def plane(st, b):
+            return T.mw[:, MWW * (4 * st + b):MWW * (4 * st + b) + A]
+
+        def based(st, b):
+            return T.mw[:, MWW * (4 * st + b):MWW * (4 * st + b) + A + 1].indirect(ll[:, 16:32])
+
+        def into(st, b):
+            return (plane(st, b), "m%d.%d" % (st, b)) if st < 3 else (mt[:, b:4 * A:4], "mt%d" % b)
+
+        vcp(T.mw[:, 3 * MWW:3 * MWW + HA], bank(4, HA), ["bank4"], ["m0.3a"])
+        vcp(T.mw[:, 3 * MWW + HA:3 * MWW + A], bank(5, HA), ["bank5"], ["m0.3"])
+        for what, b, st in REBUILD:
+            out, ko = into(st, b)
+            gb = T.gb[:, A * b:A * b + A]
+            if what[0] == "c":
+                (act if what == "cs" else vcp)(out, bank(b, A), ["bank%d" % b], [ko])
+            elif what == "g":
+                act(gb, based(st - 1, b), ["m%d.%d" % (st - 1, b), "m0.3a", "mwz", "lm"], ["gb%d" % b])
+            elif what == "a":
+                vtt(out, bank(b, A), gb, ALU.add, ["bank%d" % b, "gb%d" % b], [ko])
+            else:
+                vtt(out, based(st - 1, b), plane(0, b), ALU.add, ["m%d.%d" % (st - 1, b), "m0.%d" % b, "m0.3a", "mwz", "lm"], [ko])
+        ordered("S", 3)
+
+        for h, a, bk in (("a", 0, 4), ("b", HA, 5)):
+            quant(qm[:, a:a + HA], sm[:, a:a + HA], mt[:, 4 * a:4 * (a + HA)], ["mt0", "mt1", "mt2", "mt3"], ["qm." + h])
+            layer(0, bk, qm[:, a:a + HA], sm[:, a:a + HA], HA, ["qm." + h])
+        for b in (1, 3, 2):
+            layer(b, b, qm[:], sm[:], A, ["qm.a", "qm.b"])
+        for h, a, bk in (("a", 0, 4), ("b", HA, 5)):
+            vtt(T.zx[:, a:a + HA], bank(bk, HA), T.zx[:, a:a + HA], ALU.add, ["bank%d" % bk, "zx0." + h], ["zx0." + h])
+
+        def fetch(eng, b, a, e):
+            times(eng, xn[:, 4 * a + b:4 * e:4], T.zx[:, C * b:C * b + C].indirect(T.plo[:, a // 16:e // 16]), 0.015625,
+                  ["zx%d.a" % b, "zx%d.b" % b, "plo"], ["xn%d.%d" % (b, a)])
+
+        fetch("S", 0, 0, C)
+        for b in (1, 3, 2):
+            vtt(T.zx[:, C * b:C * b + A], bank(b, A), T.zx[:, C * b:C * b + A], ALU.add, ["bank%d" % b, "zx%d.a" % b], ["zx%d.a" % b])
+            if b == 1:
+                fetch("S", 1, 0, C)
+        fetch("V", 3, 0, C)
+        fetch("S", 2, HA, C)
+        fetch("V", 2, 0, HA)
+        xt, xkeys = xn, (["xn0.0", "xn1.0", "xn2.0", "xn2.%d" % HA, "xn3.0"], ["xn0.0", "xn1.0", "xn2.%d" % HA, "xn3.0"])
+
+    outs = {"S": 0, "Y": 0}
+
+    def store(eng, out, in_, reads):
+        outs[eng] += 16
+        q = S if eng == "S" else g.sync
+        _add(pl, eng, lambda: q.dma_start(out, in_), reads, [], kind="dma", sem="out" + eng)
+
+    act(T.ys[:, 0:H], bank(4, H), ["bank4"], ["ys.a"])
+    vcp(T.ys[:, H:C], bank(5, H), ["bank5"], ["ys.b"])
+    store("Y", T.oc[:], qx[:].bitcast(dt.uint8), [ka, kb])
+    store("S", T.y[:], T.ys[:], ["ys.a", "ys.b"])
+    for k in range(4):
+        store("Y" if k < 2 else "S", T.osc[4 * k:4 * k + 4, :], sx[32 * k:32 * k + 4, :], [ka, kb])
+    _emit(pl, g, T)
+    S.wait_ge(T.sem.outS, outs["S"])
+    g.sync.wait_ge(T.sem.outY, outs["Y"])
+    g.wait_ge(T.sem.sent, sent[0])

@@ -11,6 +11,8 @@ KEEP = 1024.0
 MWW = 272
 LOW = 128
 RUNS = [(0, 32), (32, 64), (64, 96), (96, 128), (128, 192), (192, 256), (256, 320)]
+PARTS = [(0, 128, "V"), (128, 224, "S"), (224, 320, "S")]
+DOUBLING = [("g", 1), ("g", 0), ("g", 2), ("w", 1), ("w", 0), ("c", 1), ("w", 2), ("c", 0), ("c", 2)]
 
 
 def _sb(n, d):
@@ -25,17 +27,17 @@ SCRATCH = {
     "ebig": _sb(528, "bfloat16"), "ones": _sb(128, "bfloat16"), "qe": _sb(512, CODE), "se": _sb(512, "uint8"),
     "a16": _sb(24, "int32"), "b16": _sb(24, "int32"), "e0": _sb(16, "float32"), "e1": _sb(16, "float32"),
     "cps": _sb(16, "float32"), "i16": _sb(24, "float32"), "iw": _sb(24, "float32"), "kc": _sb(16, "float32"),
-    "hk": _sb(C, "bfloat16"), "hk2": _sb(A, "bfloat16"), "iot": _sb(C, "bfloat16"), "i1k": _sb(C, "float32"),
+    "hk": _sb(C, "bfloat16"), "iot": _sb(C, "bfloat16"),
     "c1": _sb(C, "bfloat16"), "cdf": _sb(2 * C, H16), "flg": _sb(2 * C, "bfloat16"), "zer": _sb(4 * C, "bfloat16"),
     "sc": _sb(C, "float32"), "sc2": _sb(C, "float32"), "d1": _sb(C, "float32"), "g2": _sb(C, "float32"), "d2": _sb(C, "float32"),
     "a1": _sb(C, "float32"), "a2": _sb(C, "float32"),
     "w1": _sb(2 * PW, "bfloat16"), "w2": _sb(PW, "bfloat16"), "wa": _sb(PW, "bfloat16"), "wb": _sb(PW, "bfloat16"),
-    "lab": _sb(PW, "bfloat16"), "hb": _sb(C, H16), "hh": _sb(C, H16), "hl": _sb(C, H16),
+    "lab": _sb(PW, "bfloat16"), "hb": _sb(C, H16), "hh": _sb(C, H16), "hl": _sb(C, H16), "h2": _sb(C, H16), "h3": _sb(A, H16),
     "offa": _sb(32, "uint16"), "offb": _sb(32, "uint16"),
     "bq": _sb(24, "float32"), "qf": _sb(40, "float32"), "qq": _sb(48, "uint16"),
-    "ef": _sb(4 * C, "bfloat16"), "cum": _sb(4 * C, "bfloat16"), "val": _sb(C, "float32"), "pl": _sb(C, "bfloat16"),
-    "plo": _sb(32, "uint16"), "oo": _sb(32, "uint16"), "srt": _sb(C, "float32"), "h2": _sb(C, "float32"), "sg": _sb(16, "float32"),
-    "adj": _sb(16, "float32"), "vi": _sb(16, "int32"), "li": _sb(16, "int32"),
+    "ef": _sb(4 * C, "bfloat16"), "cum": _sb(4 * C, "bfloat16"), "pb": _sb(C, "bfloat16"), "pbo": _sb(A, "bfloat16"),
+    "pl": _sb(C, "bfloat16"), "plo": _sb(32, "uint16"), "oo": _sb(32, "uint16"), "srt": _sb(C, "bfloat16"),
+    "sg": _sb(16, "float32"), "adj": _sb(32, "float32"), "vi": _sb(32, "float32"),
     "fd": _sb(4 * 2 * C, "bfloat16"), "gd": _sb(4 * C, "bfloat16"), "fo": _sb(4 * C, "bfloat16"), "zx": _sb(4 * C, "bfloat16"),
     "mw": _sb(12 * MWW, "bfloat16"), "gb": _sb(4 * A, "bfloat16"), "ys": _sb(C, "float32"),
     "ps": ("psum", [128, 512 * 8], "float32"),
@@ -61,9 +63,9 @@ for _r in range(R):
 SEMAPHORES = (["cV", "cS", "cP", "cG", "sent", "l_cd", "l_u", "l_xa", "l_xb", "l_v", "l_wc", "l_ws", "outS", "outY"]
               + ["a%s%d" % (k, r) for k in "qblm" for r in range(R)])
 
-REBUILD = [("cv", 2, 0), ("g", 3, 1), ("g", 2, 1), ("cv", 1, 0), ("cs", 0, 0), ("g", 1, 1), ("a", 3, 1), ("v", 3, 2), ("a", 2, 1),
-           ("g", 0, 1), ("v", 3, 3), ("g", 2, 2), ("a", 1, 1), ("a", 0, 1), ("v", 1, 2), ("g", 0, 2), ("a", 2, 2), ("a", 0, 2),
-           ("g", 1, 3), ("v", 2, 3), ("g", 0, 3), ("a", 1, 3), ("a", 0, 3)]
+REBUILD = [("cv", 2, 0), ("cv", 1, 0), ("g", 3, 1), ("cv", 0, 0), ("g", 2, 1), ("g", 1, 1), ("a", 3, 1), ("g", 0, 1), ("a", 2, 1),
+           ("g", 2, 2), ("v", 3, 2), ("g", 3, 3), ("a", 1, 1), ("a", 0, 1), ("v", 1, 2), ("a", 2, 2), ("g", 1, 3), ("v", 0, 2),
+           ("a", 3, 3), ("v", 0, 3), ("a", 1, 3), ("g", 2, 3), ("a", 2, 3)]
 
 
 def _plan():
@@ -153,8 +155,8 @@ def rank_program(g, core, T, topo):
         q = S if eng == "S" else g.sync
         _add(pl, eng, lambda: q.dma_start(out, in_), list(after), [key], kind="dma", sem=sem, total=16)
 
-    def bank(b, n):
-        return T.ps[:, 512 * b:512 * b + n]
+    def bank(b, n, a=0):
+        return T.ps[:, 512 * b + a:512 * b + n]
 
     def mm(b, wq, ws, xq, xs_, n, reads):
         _add(pl, "P", lambda: g.tensor.matmul_mx(bank(b, n), wq, ws, xq, xs_, True, True), reads, ["bank%d" % b])
@@ -200,8 +202,8 @@ def rank_program(g, core, T, topo):
         else:
             gp(lambda: g.iota(out, pattern, base, cm), [], [key])
 
-    def wrap(out, data, reads, key, keep, kkey="hk"):
-        scan(out, keep, data, 0.0, ALU.add, ALU.max, reads + [kkey], key if isinstance(key, list) else [key])
+    def wrap(out, data, reads, key, n):
+        scan(out, T.hk[:, 0:n], data, 0.0, ALU.add, ALU.max, reads + ["hk"], key if isinstance(key, list) else [key])
 
     def quant(q, sc, in_, reads, writes):
         v(lambda: V.quantize_mx(q, sc, in_), reads, writes)
@@ -220,41 +222,41 @@ def rank_program(g, core, T, topo):
     iota(T.i16[:, 0:20], [[16, 20]], 0, 0, "i16")
     iota(T.a16[:, 0:16], [[1, 16]], 128, -1, "a16", small=False)
     iota(T.a16[:, 16:17], [[1, 1]], 0, 1, "a16p", small=False)
+    iota(T.iot[:], [[1, C]], Z - SH, 0, "iot")
     iota(T.ones[:], [[0, 128]], 1, 0, "ones")
     vset(T.ebig[:], 0.0, ["ebig"])
     gp(lambda: g.affine_select(T.ebig[:, 3:515:4], T.ones[:], [[-1, 128]], ALU.is_equal, 0.0, 0, 1), ["ones"], ["ebig"])
-    iota(T.iot[:], [[1, C]], Z - SH, 0, "iot")
     iota(T.w1[:, 0:2 * Z], [[1, Z], [0, 2]], -SH - 1, 0, "w1z")
     iota(T.w2[:, 0:Z], [[0, 4], [-2, 2], [1, 2]], 2 - SH, 0, "w2z")
     iota(T.wa[:, 0:Z], [[1, Z]], -SH, 0, "waz")
     iota(T.wb[:, 0:Z], [[1, Z]], -SH, 0, "wbz")
     iota(T.lab[:, 0:Z], [[0, 4], [C, 4]], 0, 0, "labz")
-    iota(T.i1k[:], [[1024, C]], 0, 0, "i1k")
 
     vset(T.flg[:], 0.0, ["flg.a", "flg.b"])
     vcp(T.uoff[:, 0:8], T.i16[:, 0:8], ["i16"], ["uoff"])
     vts(T.b16[:, 0:17], T.a16[:, 0:17], 15, None, ALU.bitwise_and, None, ["a16", "a16p"], ["b16"])
     vset(T.mw[:, A:12 * MWW:MWW], 0.0, ["mwz"])
+    vset(T.zer[:], 0.0, ["zer"])
     vts(T.e0[:], T.b16[:, 0:16], 0.0, -4 * KEEP, ALU.is_equal, ALU.mult, ["b16"], ["e0"])
     vts(T.e1[:], T.b16[:, 0:16], 1.0, KEEP, ALU.is_equal, ALU.mult, ["b16"], ["e1"])
     vcp(col(8), T.b16[:, 16:17], ["b16"], ["cp8"])
-    vtt(T.hk[:, 0:16], T.e0[:], T.e1[:], ALU.add, ["e0", "e1"], ["hk"])
-    vset(T.zer[:], 0.0, ["zer"])
-    for j, (m, c0) in enumerate([(1.0, SH + 0.5), (1.0, SH), (1.0, SH - Z), (2.0, SH - Z - C), (1.0, H),
-                                 (2048.0, H + (A + 1024 * C) // 2), (1.0, 0), (2048.0, H)]):
-        act(col(j), T.e1[:, 0:1], ["e1"], ["cp%d" % j], func=ACT.Identity, bias=float(c0 - m * KEEP), scale=m)
-    cp_pair, cp_ptr, cp_base, cp_bq, cp_place, cp_adj, cp_none, cp_own = [col(j) for j in range(8)]
-    for a, b in ((16, 32), (32, 64), (64, 128), (128, 256), (256, 320)):
-        act(T.hk[:, a:b], T.hk[:, 0:b - a], ["hk"], ["hk"])
-    for b in range(4):
-        quant(T.qe[:, 128 * b:128 * b + 128], T.se[:, 128 * b:128 * b + 128], T.ebig[:, 3 - b:515 - b], ["ebig"], ["qe%d" % b])
     vcp(T.cdo[:, 0:40], T.cdi[:], ["cdi"], ["cdo"])
-    quant(T.qu[:], T.su[:], T.us[:], ["us"], ["qu"])
+    vtt(T.hk[:, 0:16], T.e0[:], T.e1[:], ALU.add, ["e0", "e1"], ["hk"])
     act(T.c1[:], T.iot[:].indirect(T.cdo[:, 0:20]), ["iot", "cdo"], ["c1"])
+    quant(T.qu[:], T.su[:], T.us[:], ["us"], ["qu"])
+    for b in range(2):
+        quant(T.qe[:, 128 * b:128 * b + 128], T.se[:, 128 * b:128 * b + 128], T.ebig[:, 3 - b:515 - b], ["ebig"], ["qe%d" % b])
     vcp(T.qup[:].bitcast(dt.uint32), T.qu[:].bitcast(dt.uint32).indirect(T.uoff[:, 0:8]), ["qu", "uoff"], ["qup"])
     act(T.sup[:], T.su[:].indirect(T.uoff[:, 0:8]), ["qu", "uoff"], ["sup"])
     vtt(T.cdf[:, 0:2 * C:2], T.iot[:].indirect(T.cdo[:, 20:40]), T.c1[:], ALU.subtract, ["iot", "cdo", "c1"], ["cdf0"])
     vset(T.w1[:, 1:2], 3.0 - SH, ["w1z"])
+    steps = ((16, 32), (32, 64), (64, 128), (128, 256), (256, 320))
+    for j, (m, c0) in enumerate([(1.0, SH + 0.5), (1.0, SH), (1.0, SH - Z), (2.0, SH - Z - C), (1.0, H),
+                                 (1.0, SH - Z + C // 2), (1.0, 0), (1.0, H + A // 2)]):
+        if j < len(steps):
+            act(T.hk[:, steps[j][0]:steps[j][1]], T.hk[:, 0:steps[j][1] - steps[j][0]], ["hk"], ["hk"])
+        act(col(j), T.e1[:, 0:1], ["e1"], ["cp%d" % j], func=ACT.Identity, bias=float(c0 - m * KEEP), scale=m)
+    cp_pair, cp_ptr, cp_base, cp_bq, cp_place, cp_take, cp_none, cp_from = [col(j) for j in range(8)]
 
     def unpack(b, into, q, sc, n, reads):
         mm(into, T.qe[:, 128 * b:128 * b + 128], T.se[:, 128 * b:128 * b + 128], q, sc, n, reads + ["qe%d" % b])
@@ -286,12 +288,15 @@ def rank_program(g, core, T, topo):
         arrives(src, "al%d" % r, 1, ["ll"])
         arrives(src, "am%d" % r, 1, ["lm"])
 
+        if r == 0:
+            vcp(T.cdf[:, 1:2 * C:2], T.c1[:], ["c1"], ["cdf1"])
+            quant(T.qe[:, 256:384], T.se[:, 256:384], T.ebig[:, 1:513], ["ebig"], ["qe2"])
         vcp(T.sc[:, 0:H], bank(4, H), ["bank4"], ["sc.a"])
         act(T.sc2[:, 0:H], bank(6, H), ["bank6"], ["sc2.a"])
         act(T.sc[:, H:C], bank(5, H), ["bank5"], ["sc.b"])
         act(T.sc2[:, H:C], bank(5, H), ["bank5"], ["sc2.b"])
         if r == 0:
-            vcp(T.cdf[:, 1:2 * C:2], T.c1[:], ["c1"], ["cdf1"])
+            quant(T.qe[:, 384:512], T.se[:, 384:512], T.ebig[:, 0:512], ["ebig"], ["qe3"])
         vtt(T.d1[:, 0:H], T.sc[:, 0:H].indirect(T.cdo[:, 0:10]), T.sc2[:, 0:H], ALU.subtract, ["sc.a", "sc2.a", "cdo"], ["d1.a"])
         vtt(T.d2[:, 0:H], T.sc[:, 0:H].indirect(T.cdo[:, 20:30]), T.sc2[:, 0:H], ALU.subtract, ["sc.a", "sc2.a", "cdo"], ["d2.a"])
         act(T.g2[:, H:C], T.sc[:].indirect(T.cdo[:, 30:40]), ["sc.a", "sc.b", "cdo"], ["g2"])
@@ -308,53 +313,66 @@ def rank_program(g, core, T, topo):
 
         for h, a, b in halves:
             vtt(T.flg[:, 2 * a + 1:2 * b:2], T.a2[:, a:b], T.a1[:, a:b], ALU.is_lt, ["a1." + h, "a2." + h], ["flg." + h])
-        mine(0)
-        mine(1)
+        for b in range(3):
+            mine(b)
         for h, a, b in halves:
             scan(T.w1[:, 2 * (Z + a):2 * (Z + b)], T.flg[:, 2 * a:2 * b], T.cdf[:, 2 * a:2 * b], 0.0, ALU.mult, ALU.add,
-                 ["flg." + h, "cdf0", "cdf1"], ["w1." + h])
+                 ["flg." + h, "cdf0", "cdf1"], ["w1.0", "w1.1"] if h == "a" else ["w1.1b", "w1.2"])
         for h, a, b in halves:
-            wrap(T.hb[:, a:b], T.w1[:, 2 * (Z + a) + 1:2 * (Z + b):2], ["w1." + h], "hb." + h, T.hk[:, 0:H])
+            wrap(T.hb[:, a:b], T.w1[:, 2 * (Z + a) + 1:2 * (Z + b):2], ["w1.0" if h == "a" else "w1.2"], "hb." + h, H)
         for h, a, b in halves:
-            vts(T.offa[:, a // 16:b // 16], T.hb[:, a + 15:b:16], cp_pair, 2.0, ALU.add, ALU.mult, ["hb." + h, "cp0"], ["offa." + h])
+            vts(T.offa[:, a // 16:b // 16], T.hb[:, a + 15:b:16], cp_pair, 2.0, ALU.add, ALU.mult, ["hb." + h, "cp0"],
+                ["offa.0", "offa.1"] if h == "a" else ["offa.1b", "offa.2"])
 
         wins = [("w1", T.w1), ("w2", T.w2), ("wa", T.wa), ("wb", T.wb), ("wa", T.wa), ("wb", T.wb)]
         offs = [("offa", T.offa), ("offb", T.offb)]
         for d in range(5):
             (k0, w0), (k1, w1_), (ko, of), (kn, on) = wins[d], wins[d + 1], offs[d % 2], offs[(d + 1) % 2]
-            low = (2 if d == 0 else 1) * (Z + H)
-            act(w1_[:, Z + H:PW], w0[:].indirect(of[:, 10:20]), [k0 + ".a", k0 + ".b", k0 + "z", ko + ".b"], [k1 + ".b"])
-            vcp(w1_[:, Z:Z + H], w0[:, 0:low].indirect(of[:, 0:10]), [k0 + ".a", k0 + "z", ko + ".a"], [k1 + ".a"])
-            if d == 0:
-                vts(ob[:, 0:20], T.hb[:, 15:C:16], cp_base, None, ALU.add, None, ["hb.a", "hb.b", "cp2"], ["ob%d" % r])
-                send(dst, lb[:, 0:20], ob[:, 0:20], "ab%d" % r, ["ob%d" % r])
-            for h, a, b in (halves if d == 0 else halves[::-1]):
-                wrap(T.hh[:, a:b], w1_[:, Z + a:Z + b], [k1 + "." + h], "hh." + h, T.hk[:, 0:H])
-            if d == 0:
-                vts(T.bq[:, 0:20], T.hb[:, 15:C:16], cp_bq, None, ALU.add, None, ["hb.a", "hb.b", "cp3"], ["bq"])
-            for h, a, b in halves[::-1]:
-                vts(on[:, a // 16:b // 16], T.hh[:, a + 15:b:16], cp_ptr, None, ALU.add, None, ["hh." + h, "cp1"], [kn + "." + h])
-
-        def theirs(b):
-            act(T.fd[:, 2 * C * b:2 * C * b + C], bank(b, C), ["bank%d" % b], ["fd%d.f" % b])
+            for what, p in DOUBLING:
+                a, b, e = PARTS[p]
+                if what == "g":
+                    (act if e == "S" else vcp)(w1_[:, Z + a:Z + b], w0[:, 0:(2 if d == 0 else 1) * (Z + b)].indirect(of[:, a // 16:b // 16]),
+                                               ["%s.%d" % (k0, q) for q in range(p + 1)] + [k0 + "z", "%s.%d" % (ko, p)]
+                                               + (["w1.1b", "offa.1b"] if d == 0 and p > 0 else []), ["%s.%d" % (k1, p)])
+                    if d == 0 and p == 0:
+                        vts(ob[:, 0:20], T.hb[:, 15:C:16], cp_base, None, ALU.add, None, ["hb.a", "hb.b", "cp2"], ["ob%d" % r])
+                        send(dst, lb[:, 0:20], ob[:, 0:20], "ab%d" % r, ["ob%d" % r])
+                        vts(T.bq[:, 0:20], T.hb[:, 15:C:16], cp_bq, None, ALU.add, None, ["hb.a", "hb.b", "cp3"], ["bq"])
+                elif what == "w":
+                    wrap(T.hh[:, a:b], w1_[:, Z + a:Z + b], ["%s.%d" % (k1, p)], "hh.%d" % p, b - a)
+                else:
+                    vts(on[:, a // 16:b // 16], T.hh[:, a + 15:b:16], cp_ptr, None, ALU.add, None, ["hh.%d" % p, "cp1"], ["%s.%d" % (kn, p)])
 
         def piece(what, k):
-            a, b = ((0, LOW), (LOW, C))[k]
+            a, b = ((0, LOW), (LOW, A), (A, C))[k]
             lab, rd = T.lab[:, Z + a:Z + b], ["lab%d" % j for j, (lo, hi) in enumerate(RUNS) if a <= lo < b]
             if what == "s":
                 act(T.ef[:, a:b], lab, rd, ["ef0.%d" % k], func=ACT.Relu, bias=1.0, scale=-1.0)
                 act(T.ef[:, 3 * C + a:3 * C + b], lab, rd, ["ef3.%d" % k], func=ACT.Relu, bias=1.0 - 3 * C)
             elif what == "w":
-                wrap(T.hl[:, a:b], lab, rd, "hl.%d" % k, T.hk[:, 0:b - a])
+                wrap(T.hl[:, a:b], lab, rd, "hl.%d" % k, b - a)
             else:
                 vts(T.ef[:, what * C + a:what * C + b], lab, float(what * C), None, ALU.is_equal, None, rd, ["ef%d.%d" % (what, k)])
 
+        def theirs(b):
+            act(T.fd[:, 2 * C * b:2 * C * b + C], bank(b, C), ["bank%d" % b], ["fd%d.f" % b])
+
+        def bases(b):
+            act(T.gd[:, C * b:C * b + C], T.fd[:, 2 * C * b:2 * C * b + C].indirect(lb[:, 0:20]), ["fd%d.f" % b, "lb"], ["gd%d" % b])
+
+        def minus(b, a=0, e=C):
+            vtt(T.fd[:, 2 * C * b + C + a:2 * C * b + C + e], bank(b, e, a), T.gd[:, C * b + a:C * b + e], ALU.subtract,
+                ["bank%d" % b, "gd%d" % b], ["fd%d.d%d" % (b, a)])
+
         for b in range(4):
             unpack(b, b, lq[:], ls[:], C, ["lq"])
-        act(T.wa[:, Z + LOW:PW], T.wb[:].indirect(T.offb[:, LOW // 16:20]), ["wb.a", "wb.b", "wbz", "offb.a", "offb.b"], ["wa.a", "wa.b"])
-        mine(2)
+        act(T.wa[:, Z + LOW:PW], T.wb[:].indirect(T.offb[:, LOW // 16:20]), ["wb.0", "wb.1", "wb.2", "wbz", "offb.1", "offb.2"], ["wa.1", "wa.2"])
+        if r > 0:
+            theirs(0)
+        else:
+            mine(3)
         for j, (a, b) in enumerate(RUNS):
-            of, ko = (T.offb, ["offb.a"]) if a < LOW else (T.offa, ["offa.a", "offa.b"])
+            of, ko = (T.offb, ["offb.0"]) if a < LOW else (T.offa, ["offa.1", "offa.2"])
             vcp(T.lab[:, Z + a:Z + b], T.lab[:, 0:Z + a].indirect(of[:, a // 16:b // 16]),
                 ["labz"] + ko + ["lab%d" % i for i in range(j)], ["lab%d" % j])
             if r == 0 and j == 0:
@@ -362,69 +380,84 @@ def rank_program(g, core, T, topo):
             if r == 0 and j == 1:
                 vts(T.kc[:], T.i16[:, 0:16], col(8), -(H + 0.5), ALU.add, ALU.add, ["i16", "cp8"], ["kc"])
             if j == 2:
-                wrap(T.hh[:, LOW:C], T.wa[:, Z + LOW:PW], ["wa.a", "wa.b"], ["hh.a", "hh.b"], T.hk[:, 0:C - LOW])
+                wrap(T.hh[:, LOW:C], T.wa[:, Z + LOW:PW], ["wa.1", "wa.2"], ["hh.1", "hh.2"], C - LOW)
             if j == 3:
-                vts(T.offa[:, LOW // 16:20], T.hh[:, LOW + 15:C:16], cp_ptr, None, ALU.add, None, ["hh.a", "hh.b", "cp1"], ["offa.a", "offa.b"])
-                piece(1, 0)
+                vts(T.offa[:, LOW // 16:20], T.hh[:, LOW + 15:C:16], cp_ptr, None, ALU.add, None, ["hh.1", "hh.2", "cp1"],
+                    ["offa.1", "offa.1b", "offa.2"])
                 piece("s", 0)
-                if r == 0:
-                    act(T.hk2[:], T.hk[:, 0:A], ["hk"], ["hk2"], scale=2048.0)
+                theirs(1 if r > 0 else 0)
             if j == 4:
+                piece(1, 0)
                 piece(2, 0)
             if j == 5:
                 piece("w", 0)
+                piece("s", 1)
+            if j == 6:
+                piece("w", 1)
+                piece(1, 1)
+                piece(2, 1)
 
-        piece("s", 1)
-        mine(3)
-        theirs(0)
-        hl = ["hl.0", "hl.1"]
-        piece("w", 1)
-        piece(1, 1)
+        piece("s", 2)
+        bases(0)
+        if r == 0:
+            theirs(1)
+        hl = ["hl.0", "hl.1", "hl.2"]
+        piece("w", 2)
+        piece(1, 2)
+        piece(2, 2)
         vtt(T.qf[:, 0:20], T.hl[:, 15:C:16], T.iw[:, 0:20], ALU.add, hl + ["iw"], ["qf0"])
         vtt(T.qf[:, 20:40], T.hl[:, 15:C:16], T.bq[:, 0:20], ALU.add, hl + ["bq"], ["qf1"])
-        piece(2, 1)
-        vcp(T.qq[:, 0:40], T.qf[:], ["qf0", "qf1"], ["qq"])
         scan(T.cum[:], T.ef[:], T.zer[:], -(H + 1.0), ALU.add, ALU.add,
-             ["ef%d.%d" % (d, k) for d in range(4) for k in range(2)] + ["zer"], ["cum"])
-        act(T.pl[:], T.cum[:].indirect(T.qq[:, 0:20]), ["cum", "qq"], ["pl"])
-        vtt(T.val[:], T.cum[:].indirect(T.qq[:, 20:40]), T.i1k[:], ALU.add, ["cum", "qq", "i1k"], ["val"])
+             ["ef%d.%d" % (d, k) for d in range(4) for k in range(3)] + ["zer"], ["cum"])
+        vcp(T.qq[:, 0:40], T.qf[:], ["qf0", "qf1"], ["qq"])
+        act(T.pl[:, H:C], T.cum[:].indirect(T.qq[:, 10:20]), ["cum", "qq"], ["pl.b"])
+        vcp(T.pl[:, 0:H], T.cum[:].indirect(T.qq[:, 0:10]), ["cum", "qq"], ["pl.a"])
         act(T.sg[:], T.kc[:], ["kc", "cum"], ["sg"], func=ACT.Sign, bias=T.cum[:, C - 1:C], scale=-1.0)
-        theirs(1)
-        act(T.adj[:], T.sg[:], ["sg", "cp5"], ["adj"], func=ACT.Identity, bias=cp_adj, scale=(A - 1024.0 * C) / 2)
-        for b in range(4):
-            if b < 2:
-                theirs(b + 2)
-            act(T.gd[:, C * b:C * b + C], T.fd[:, 2 * C * b:2 * C * b + C].indirect(lb[:, 0:20]), ["fd%d.f" % b, "lb"], ["gd%d" % b])
-        wrap(T.hh[:], T.pl[:], ["pl"], ["hh.a", "hh.b"], T.hk[:])
-        vts(T.plo[:, 0:20], T.hh[:, 15:C:16], cp_place, None, ALU.add, None, ["hh.a", "hh.b", "cp4"], ["plo"])
-        vcp(T.srt[:].indirect(T.plo[:, 0:20]), T.val[:], ["val", "plo"], ["srt"])
-        wrap(T.h2[:, 0:A], T.srt[:, 0:A], ["srt"], "h2", T.hk2[:], "hk2")
-        wrap(T.h2[:, A:C], T.srt[:, A:C], ["srt"], "h2t", T.hk2[:, 0:C - A], "hk2")
-        vtt(T.vi[:], T.h2[:, 15:A:16], T.adj[:], ALU.add, ["h2", "adj"], ["vi"])
-        vts(T.oo[:, 0:20], T.h2[:, 15:C:16], cp_own, 1.0 / 1024, ALU.add, ALU.mult, ["h2", "h2t", "cp7"], ["oo"])
-        vts(ol[:, 0:16], T.vi[:], 1.0 / 1024, None, ALU.mult, None, ["vi"], ["ol%d" % r])
+        bases(1)
+        act(T.adj[:, 0:16], T.sg[:], ["sg", "cp5"], ["adj0"], func=ACT.Identity, bias=cp_take, scale=-C / 2)
+        act(T.adj[:, 16:32], T.sg[:], ["sg", "cp7"], ["adj1"], func=ACT.Identity, bias=cp_from, scale=A / 2)
+        theirs(2)
+        theirs(3)
+        act(T.pb[:], T.cum[:].indirect(T.qq[:, 20:40]), ["cum", "qq"], ["pb"])
+        bases(2)
+        bases(3)
+        minus(0, 0, H)
+        for h, a, b in halves:
+            wrap(T.hh[:, a:b], T.pl[:, a:b], ["pl." + h], ["hh.0", "hh.1"] if h == "a" else ["hh.2"], H)
+        minus(0, H, C)
+        vts(T.plo[:, 0:20], T.hh[:, 15:C:16], cp_place, None, ALU.add, None, ["hh.0", "hh.1", "hh.2", "cp4"], ["plo"])
+        vcp(T.srt[:].indirect(T.plo[:, 0:20]), T.iot[:], ["iot", "plo"], ["srt"])
+        minus(1, 0, H)
+        wrap(T.h2[:, 0:A], T.srt[:, 0:A], ["srt"], "h2", A)
+        wrap(T.h2[:, A:C], T.srt[:, A:C], ["srt"], "h2t", C - A)
+        minus(1, H, C)
+        vtt(T.vi[:, 0:16], T.h2[:, 15:A:16], T.adj[:, 0:16], ALU.add, ["h2", "adj0"], ["vi0"])
+        vts(T.oo[:, 0:20], T.h2[:, 15:C:16], cp_base, None, ALU.add, None, ["h2", "h2t", "cp2"], ["oo"])
+        vcp(ol[:, 0:16], T.vi[:, 0:16], ["vi0"], ["ol%d" % r])
         send(dst, ll[:, 0:16], ol[:, 0:16], "al%d" % r, ["ol%d" % r])
-        vts(T.li[:], T.vi[:], 1023, None, ALU.bitwise_and, None, ["vi"], ["li"])
 
         def ordered(eng, b):
             times(eng, T.zx[:, C * b:C * b + C], T.fo[:, C * b:C * b + C].indirect(T.oo[:, 0:20]), 64.0, ["fo%d" % b, "oo"],
                   ["zx%d.a" % b, "zx%d.b" % b])
 
-        for b in range(4):
-            if b == 2:
-                ordered("V", 0)
-            vtt(T.fd[:, 2 * C * b + C:2 * C * (b + 1)], bank(b, C), T.gd[:, C * b:C * b + C], ALU.subtract,
-                ["bank%d" % b, "gd%d" % b], ["fd%d.d" % b])
-            if b == 0:
-                vcp(ol[:, 16:32], T.li[:], ["li"], ["om%d" % r])
-                send(dst, ll[:, 16:32], ol[:, 16:32], "am%d" % r, ["om%d" % r])
         ordered("S", 1)
+        if r > 0:
+            mine(3)
+        vcp(T.pbo[:], T.pb[:].indirect(T.oo[:, 0:16]), ["pb", "oo"], ["pbo"])
+        minus(2)
+        wrap(T.h3[:], T.pbo[:], ["pbo"], "h3", A)
+        minus(3)
+        vtt(T.vi[:, 16:32], T.h3[:, 15:A:16], T.adj[:, 16:32], ALU.add, ["h3", "adj1"], ["vi1"])
+        ordered("V", 0)
         if r == 0:
             quant(T.qv[:], T.sv[:], T.vs[:], ["vs"], ["qv"])
+        vcp(ol[:, 16:32], T.vi[:, 16:32], ["vi1"], ["om%d" % r])
+        send(dst, ll[:, 16:32], ol[:, 16:32], "am%d" % r, ["om%d" % r])
 
         for b in (2, 0, 3, 1):
             f = act if b >= 2 else vcp
-            f(pt[:, b:4 * A:4], T.fd[:, 2 * C * b:2 * C * (b + 1)].indirect(ll[:, 0:16]), ["fd%d.f" % b, "fd%d.d" % b, "ll"], ["pt%d" % b])
+            f(pt[:, b:4 * A:4], T.fd[:, 2 * C * b:2 * C * (b + 1)].indirect(ll[:, 0:16]),
+              ["fd%d.f" % b, "fd%d.d0" % b, "fd%d.d%d" % (b, H), "ll"], ["pt%d" % b])
         ordered("S", 2)
         for h, a, bk in (("a", 0, 4), ("b", HA, 5)):
             quant(qp[:, a:a + HA], sp[:, a:a + HA], pt[:, 4 * a:4 * (a + HA)], ["pt0", "pt1", "pt2", "pt3"], ["qp." + h])
@@ -446,8 +479,8 @@ def rank_program(g, core, T, topo):
         for what, b, st in REBUILD:
             out, ko = into(st, b)
             gb = T.gb[:, A * b:A * b + A]
-            if what[0] == "c":
-                (act if what == "cs" else vcp)(out, bank(b, A), ["bank%d" % b], [ko])
+            if what == "cv":
+                vcp(out, bank(b, A), ["bank%d" % b], [ko])
             elif what == "g":
                 act(gb, based(st - 1, b), ["m%d.%d" % (st - 1, b), "m0.3a", "mwz", "lm"], ["gb%d" % b])
             elif what == "a":
@@ -474,9 +507,9 @@ def rank_program(g, core, T, topo):
             if b == 1:
                 fetch("S", 1, 0, C)
         fetch("V", 3, 0, C)
-        fetch("S", 2, HA, C)
-        fetch("V", 2, 0, HA)
-        xt, xkeys = xn, (["xn0.0", "xn1.0", "xn2.0", "xn2.%d" % HA, "xn3.0"], ["xn0.0", "xn1.0", "xn2.%d" % HA, "xn3.0"])
+        fetch("S", 2, H, C)
+        fetch("V", 2, 0, H)
+        xt, xkeys = xn, (["xn0.0", "xn1.0", "xn2.0", "xn3.0"], ["xn0.0", "xn1.0", "xn2.%d" % H, "xn3.0"])
 
     outs = {"S": 0, "Y": 0}
 

@@ -7,12 +7,25 @@ H16 = "float16"
 Z = 16
 PW = Z + C
 SH = PW // 2
-KEEP = 1024.0
-MWW = 272
-LOW = 128
-RUNS = [(0, 32), (32, 64), (64, 96), (96, 128), (128, 192), (192, 256), (256, 320)]
-PARTS = [(0, 128, "V"), (128, 224, "S"), (224, 320, "S")]
-DOUBLING = [("g", 1), ("g", 0), ("g", 2), ("w", 1), ("w", 0), ("c", 1), ("w", 2), ("c", 0), ("c", 2)]
+KEEP = 1280.0
+LAB = 5 * C
+BANK = 512
+
+CFG = {
+    "low": 128,
+    "parts": [(0, 160, "V"), (160, 320, "S")],
+    "pieces": [(0, 256), (256, 320)],
+    "cand": "VVVS",
+    "steps": {2: "VSSS", 3: "VSSS"},
+    "state": "VVVS",
+    "xparts": [(0, 160), (160, 320)],
+    "mparts": [(0, 128), (128, 256)],
+    "b0": [0, 1, 2, 3], "lparts": [((0, 128), [0, 1, 2, 3]), ((128, 256), [0, 1, 4, 5])], "lorder": [2, 0, 3, 1],
+    "fill": 160,
+    "wake": 170.0, "f": 1.15, "g": 1.56, "sc": 3.8, "link": 2000.0, "bw": 80.0, "rows": 480.0, "first": 1000.0, "load": 1500.0, "lrows": 240.0, "passes": 5,
+    "ahead": 60.0, "over": 400.0, "give": 300.0, "mix": 1.0, "eft": "VS", "egt": "VS", "em": "VS", "erun": "VS",
+}
+ORDER = []
 
 
 def _sb(n, d):
@@ -26,105 +39,187 @@ SCRATCH = {
     "qv": _sb(128, CODE), "sv": _sb(128, "uint8"), "uoff": _sb(16, "uint16"),
     "ebig": _sb(528, "bfloat16"), "ones": _sb(128, "bfloat16"), "qe": _sb(512, CODE), "se": _sb(512, "uint8"),
     "a16": _sb(24, "int32"), "b16": _sb(24, "int32"), "e0": _sb(16, "float32"), "e1": _sb(16, "float32"),
-    "cps": _sb(16, "float32"), "i16": _sb(24, "float32"), "iw": _sb(24, "float32"), "kc": _sb(16, "float32"),
-    "hk": _sb(C, "bfloat16"), "iot": _sb(C, "bfloat16"),
+    "cps": _sb(16, "float32"), "i16": _sb(8, "float32"),
+    "hk": _sb(C, "bfloat16"), "iot": _sb(C, "bfloat16"), "col32": _sb(C, "float32"), "col16": _sb(C, H16),
     "c1": _sb(C, "bfloat16"), "cdf": _sb(2 * C, H16), "flg": _sb(2 * C, "bfloat16"), "zer": _sb(4 * C, "bfloat16"),
-    "sc": _sb(C, "float32"), "sc2": _sb(C, "float32"), "d1": _sb(C, "float32"), "g2": _sb(C, "float32"), "d2": _sb(C, "float32"),
-    "a1": _sb(C, "float32"), "a2": _sb(C, "float32"),
+    "sc": _sb(C, "float32"), "sc2": _sb(C, "float32"), "gc": _sb(2 * C, "float32"), "dd": _sb(2 * C, "float32"), "aa": _sb(2 * C, "float32"),
     "w1": _sb(2 * PW, "bfloat16"), "w2": _sb(PW, "bfloat16"), "wa": _sb(PW, "bfloat16"), "wb": _sb(PW, "bfloat16"),
-    "lab": _sb(PW, "bfloat16"), "hb": _sb(C, H16), "hh": _sb(C, H16), "hl": _sb(C, H16), "h2": _sb(C, H16), "h3": _sb(A, H16),
-    "offa": _sb(32, "uint16"), "offb": _sb(32, "uint16"),
-    "bq": _sb(24, "float32"), "qf": _sb(40, "float32"), "qq": _sb(48, "uint16"),
-    "ef": _sb(4 * C, "bfloat16"), "cum": _sb(4 * C, "bfloat16"), "pb": _sb(C, "bfloat16"), "pbo": _sb(A, "bfloat16"),
-    "pl": _sb(C, "bfloat16"), "plo": _sb(32, "uint16"), "oo": _sb(32, "uint16"), "srt": _sb(C, "bfloat16"),
-    "sg": _sb(16, "float32"), "adj": _sb(32, "float32"), "vi": _sb(32, "float32"),
-    "fd": _sb(4 * 2 * C, "bfloat16"), "gd": _sb(4 * C, "bfloat16"), "fo": _sb(4 * C, "bfloat16"), "zx": _sb(4 * C, "bfloat16"),
-    "mw": _sb(12 * MWW, "bfloat16"), "gb": _sb(4 * A, "bfloat16"), "ys": _sb(C, "float32"),
-    "ps": ("psum", [128, 512 * 8], "float32"),
+    "wc2": _sb(PW, "bfloat16"), "wd": _sb(PW, "bfloat16"), "we": _sb(PW, "bfloat16"),
+    "lab": _sb(PW, "bfloat16"), "hb": _sb(C, H16), "hh": _sb(6 * C, H16), "li": _sb(C, H16), "hl": _sb(C, H16), "hp": _sb(C, H16),
+    "h2": _sb(A, H16), "off": _sb(7 * 32, "uint16"), "qq": _sb(32, "uint16"),
+    "ef": _sb(4 * C, "bfloat16"), "cum": _sb(4 * C, "bfloat16"), "pl": _sb(C, "bfloat16"), "plo": _sb(32, "uint16"),
+    "srt": _sb(C, "float32"), "lb4": _sb(80, "uint16"),
+    "fo": _sb(4 * C, "bfloat16"), "md": _sb(4 * C, "bfloat16"), "mv": _sb(16 * C, "bfloat16"), "gb": _sb(8 * C, "bfloat16"),
+    "pr": _sb(4 * C, "float32"), "gx": _sb(4 * C, "float32"), "ys": _sb(C, "float32"),
+    "ft": _sb(4 * C, "bfloat16"), "gt": _sb(4 * C, "bfloat16"), "pt": _sb(4 * C, "bfloat16"), "mt": _sb(4 * A, "bfloat16"),
+    "xn": _sb(4 * C, "bfloat16"),
+    "ps": ("psum", [128, BANK * 8], "float32"),
 }
 for _r in range(R + 1):
     SCRATCH["qx%d" % _r] = _sb(C, CODE)
     SCRATCH["sx%d" % _r] = _sb(C, "uint8")
 for _r in range(R):
-    SCRATCH["xn%d" % _r] = _sb(4 * C, "bfloat16")
     SCRATCH["lq%d" % _r] = _sb(C, CODE)
     SCRATCH["ls%d" % _r] = _sb(C, "uint8")
     SCRATCH["lb%d" % _r] = _sb(32, "uint16")
-    SCRATCH["ll%d" % _r] = _sb(32, "uint16")
+    SCRATCH["ll%d" % _r] = _sb(16, "uint16")
     SCRATCH["ob%d" % _r] = _sb(32, "uint16")
-    SCRATCH["ol%d" % _r] = _sb(32, "uint16")
-    SCRATCH["pt%d" % _r] = _sb(4 * A, "bfloat16")
-    SCRATCH["qp%d" % _r] = _sb(A, CODE)
-    SCRATCH["sp%d" % _r] = _sb(A, "uint8")
-    SCRATCH["mt%d" % _r] = _sb(4 * A, "bfloat16")
+    SCRATCH["ol%d" % _r] = _sb(16, "uint16")
+    SCRATCH["qp%d" % _r] = _sb(3 * C, CODE)
+    SCRATCH["sp%d" % _r] = _sb(3 * C, "uint8")
     SCRATCH["qm%d" % _r] = _sb(A, CODE)
     SCRATCH["sm%d" % _r] = _sb(A, "uint8")
 
 SEMAPHORES = (["cV", "cS", "cP", "cG", "sent", "l_cd", "l_u", "l_xa", "l_xb", "l_v", "l_wc", "l_ws", "outS", "outY"]
-              + ["a%s%d" % (k, r) for k in "qblm" for r in range(R)])
+              + ["a%s%d" % (k, r) for k in "qrbl" for r in range(R)])
 
-REBUILD = [("cv", 2, 0), ("cv", 1, 0), ("g", 3, 1), ("cv", 0, 0), ("g", 2, 1), ("g", 1, 1), ("a", 3, 1), ("g", 0, 1), ("a", 2, 1),
-           ("g", 2, 2), ("v", 3, 2), ("g", 3, 3), ("a", 1, 1), ("a", 0, 1), ("v", 1, 2), ("a", 2, 2), ("g", 1, 3), ("v", 0, 2),
-           ("a", 3, 3), ("v", 0, 3), ("a", 1, 3), ("g", 2, 3), ("a", 2, 3)]
+BYTES = {"float32": 4, "int32": 4, CODE: 4, "bfloat16": 2, H16: 2, "uint16": 2, "uint8": 1}
 
 
-def _plan():
-    return {"ops": [], "w": {}, "r": {}}
-
-
-def _add(pl, eng, fn, reads, writes, kind="c", sem=None, total=0):
+def _add(pl, costs, fn, reads, writes, kind="c", sem=None, total=0, lag=0.0, after=(), behind=()):
     ops, n = pl["ops"], len(pl["ops"])
-    deps = set()
-    for k in reads:
-        if k in pl["w"]:
-            deps.add(pl["w"][k])
-        if k.startswith("bank"):
-            deps.update(j for j in pl["r"].get(k, []) if ops[j]["eng"] != eng)
-    for k in writes:
-        if k in pl["w"]:
-            deps.add(pl["w"][k])
-        deps.update(pl["r"].get(k, []))
-    for k in reads:
-        pl["r"].setdefault(k, []).append(n)
-    for k in writes:
-        pl["w"][k] = n
-        pl["r"][k] = []
-    ops.append({"eng": eng, "fn": fn, "deps": deps, "kind": kind, "sem": sem, "total": total})
+    deps, shared = set(after), set()
+    for name, cols in reads:
+        for j, c, wrote in pl["seen"].get(name, []):
+            if c & cols:
+                if wrote:
+                    deps.add(j)
+                elif name == "ps":
+                    shared.add(j)
+    for name, cols in writes:
+        kept = []
+        for j, c, wrote in pl["seen"].get(name, []):
+            if c & cols:
+                deps.add(j)
+            if c & ~cols:
+                kept.append((j, c & ~cols, wrote))
+        pl["seen"][name] = kept
+    for name, cols in reads:
+        pl["seen"].setdefault(name, []).append((n, cols, False))
+    for name, cols in writes:
+        pl["seen"].setdefault(name, []).append((n, cols, True))
+    ops.append({"costs": costs, "fn": fn, "deps": deps, "shared": shared - deps, "kind": kind, "sem": sem, "total": total, "lag": lag,
+                "behind": list(behind)})
+    return n
+
+
+def _list(ops, pred, succ, worth, first):
+    n = len(ops)
+    left = [len(p) for p in pred]
+    since = list(first)
+    ready = {k: since[k] for k in range(n) if not left[k]}
+    free = {e: 0.0 for e in ("V", "S", "P", "G", "Y", "in", "L")}
+    order, eng, end = [], {}, [0.0] * n
+
+    def choose(e, mine):
+        t = max(free[e], min(ready[k] for k in mine))
+        for i, k in enumerate(mine):
+            s = max(t, ready[k])
+            if ready[k] <= t + CFG["ahead"] and all(s + ops[k]["costs"][e] <= ready[j] + CFG["over"] for j in mine[:i]):
+                return s, k
+        k = min(mine, key=lambda k: (ready[k] if ready[k] > t else 1e18, -worth[k]))
+        return max(t, ready[k]), k
+
+    while ready:
+        best = None
+        ranked = sorted(ready, key=lambda k: (-worth[k], k))
+        for e in free:
+            mine = [k for k in ranked if e in ops[k]["costs"]]
+            if e == "V":
+                ts, theirs = free["S"], set()
+                for k in ranked:
+                    if "S" in ops[k]["costs"] and max(ts, ready[k]) <= max(free["V"], ready[k]) + CFG["give"]:
+                        theirs.add(k)
+                        ts = max(ts, ready[k]) + ops[k]["costs"]["S"]
+                mine = [k for k in mine if k not in theirs]
+            if not mine:
+                continue
+            t, k = choose(e, mine)
+            if best is None or t < best[0]:
+                best = (t, e, k)
+        t, e, k = best
+        end[k] = t + ops[k]["costs"][e]
+        if e != "in":
+            free[e] = end[k]
+        eng[k] = e
+        order.append(k)
+        del ready[k]
+        for j, delay in succ[k]:
+            since[j] = max(since[j], end[k] + delay)
+            left[j] -= 1
+            if not left[j]:
+                ready[j] = since[j]
+    return order, eng, end
+
+
+def _edges(ops):
+    pred = [[(j, ops[j]["lag"] + CFG["wake"]) for j in sorted(op["deps"] | op["shared"])] + [(j, 0.0) for j in op["behind"]] for op in ops]
+    succ = [[] for _ in ops]
+    for k in range(len(ops)):
+        for j, delay in pred[k]:
+            succ[j].append((k, delay))
+    return pred, succ
+
+
+def _order(ops):
+    n = len(ops)
+    pred, succ = _edges(ops)
+    worth = [0.0] * n
+    for k in range(n - 1, -1, -1):
+        worth[k] = min(ops[k]["costs"].values()) + max([delay + worth[j] for j, delay in succ[k]] + [ops[k]["lag"]])
+    best = None
+    for _ in range(CFG["passes"]):
+        order, eng, end = _list(ops, pred, succ, worth, [0.0] * n)
+        span = max(end[k] + ops[k]["lag"] for k in range(n))
+        if best is None or span < best[0]:
+            best = (span, order, eng)
+        back = _list(ops, succ, pred, end, [op["lag"] for op in ops])[2]
+        worth = [CFG["mix"] * back[k] + (1 - CFG["mix"]) * worth[k] for k in range(n)]
+    return best
 
 
 def _emit(pl, g, T):
     ops = pl["ops"]
+    if not ORDER:
+        ORDER.append(_order(ops))
+    _, order, eng = ORDER[0]
+    at = {n: k for k, n in enumerate(order)}
     queue = {"V": g.vector, "S": g.scalar, "P": g.tensor, "G": g, "Y": g.sync}
     known = {e: {} for e in queue}
-    for n, op in enumerate(ops):
+    for n in order:
+        op = ops[n]
+        op["eng"] = eng[n]
         op["line"] = op["eng"] if op["kind"] == "c" else "d%d" % n
         op["waits"] = []
         if op["kind"] == "in":
-            op["clock"] = {op["line"]: n}
+            op["clock"] = {op["line"]: at[n]}
             continue
         kn = known[op["eng"]]
-        for j in sorted(op["deps"], reverse=True):
+        need = set(op["deps"]) | set(j for j in op["shared"] if eng[j] != eng[n])
+        for j in sorted(need, key=lambda j: -at[j]):
             d = ops[j]
-            if d["kind"] == "send" or kn.get(d["line"], -1) >= j:
+            if d["kind"] == "send" or kn.get(d["line"], -1) >= at[j]:
                 continue
             op["waits"].append(j)
             d["signals"] = True
             for line, m in d["clock"].items():
                 kn[line] = max(kn.get(line, -1), m)
         op["clock"] = dict(kn)
-        op["clock"][op["line"]] = n
+        op["clock"][op["line"]] = at[n]
     count = {e: 0 for e in queue}
-    for op in ops:
+    for n in order:
+        op = ops[n]
         if op["kind"] == "c" and op.get("signals"):
             count[op["eng"]] += 1
             op["sem"], op["total"] = "c" + op["eng"], count[op["eng"]]
-    for op in ops:
+    for n in order:
+        op = ops[n]
         if op["kind"] == "in":
             continue
         q = queue[op["eng"]]
         for j in op["waits"]:
             q.wait_ge(T.sem[ops[j]["sem"]], ops[j]["total"])
-        ins = op["fn"]()
+        ins = op["fn"](op["eng"])
         if op["kind"] == "dma":
             ins.then_inc(T.sem[op["sem"]], 16)
         elif op["kind"] == "c" and op.get("signals"):
@@ -136,394 +231,343 @@ def rank_program(g, core, T, topo):
     if rank is None:
         return
     n_ranks = len(T.cores)
-    pl = _plan()
+    pl = {"ops": [], "seen": {}}
     V, S = g.vector, g.scalar
-    sent = [0]
-    H, HA = C // 2, A // 2
-    halves = (("a", 0, H), ("b", H, C))
+    sent, last, loads, queued = [0], [], [], [0.0]
+    H = C // 2
+    halves = ((0, H), (H, C))
+    cyc = 0.83 * CFG["f"]
 
-    def v(fn, reads, writes):
-        _add(pl, "V", fn, reads, writes)
+    def at(name, a=0, b=None, st=1):
+        where, shape, kind = SCRATCH[name]
+        b = shape[1] if b is None else b
+        n = len(range(a, b, st))
+        if where == "psum":
+            cols = 1 << (a // BANK)
+        elif st == 1:
+            cols = ((1 << n) - 1) << a
+        else:
+            cols = sum(1 << c for c in range(a, b, st))
+        return {"ap": T[name][:, a:b:st] if st > 1 else T[name][:, a:b], "keys": [(name, cols)], "n": n, "bytes": BYTES[kind],
+                "psum": where == "psum", "list": False}
 
-    def s(fn, reads, writes):
-        _add(pl, "S", fn, reads, writes)
-
-    def gp(fn, reads, writes):
-        _add(pl, "G", fn, reads, writes)
-
-    def load(eng, out, in_, sem, key, after=()):
-        q = S if eng == "S" else g.sync
-        _add(pl, eng, lambda: q.dma_start(out, in_), list(after), [key], kind="dma", sem=sem, total=16)
+    def by(win, off, words=False):
+        ap = win["ap"].bitcast(dt.uint32) if words else win["ap"]
+        return dict(win, ap=ap.indirect(off["ap"]), keys=win["keys"] + off["keys"], n=16 * off["n"], list=True)
 
     def bank(b, n, a=0):
-        return T.ps[:, 512 * b + a:512 * b + n]
+        return at("ps", BANK * b + a, BANK * b + n)
 
-    def mm(b, wq, ws, xq, xs_, n, reads):
-        _add(pl, "P", lambda: g.tensor.matmul_mx(bank(b, n), wq, ws, xq, xs_, True, True), reads, ["bank%d" % b])
+    def keys(*xs):
+        return [k for x in xs if isinstance(x, dict) for k in x["keys"]]
 
-    def send(dst, out, in_, sem, reads):
+    def ap(x):
+        return x["ap"] if isinstance(x, dict) else x
+
+    def cost(e, out, ins, k=None):
+        full = [x for x in ins if isinstance(x, dict) and x["n"] == out["n"]]
+        if out["list"]:
+            return 50 * CFG["f"] + CFG["sc"] * cyc * out["n"]
+        if any(x["list"] for x in full):
+            return (50 if e == "V" else 65) * CFG["f"] + CFG["g"] * cyc * out["n"]
+        if k is None:
+            k = 0.5 if e == "V" and all(x["bytes"] == 2 for x in full + [out]) else 1.0
+        return cyc * max(64, k * out["n"])
+
+    def call(engs, fn, out, ins, k=None):
+        return _add(pl, {e: cost(e, out, ins, k) for e in engs}, fn, keys(*ins), keys(out))
+
+    def copy(engs, out, in_, scale=None):
+        def fn(e):
+            if e == "S":
+                return S.activation(out["ap"], in_["ap"], ACT.Copy) if scale is None else S.activation(out["ap"], in_["ap"], ACT.Copy, scale=scale)
+            return V.tensor_copy(out["ap"], in_["ap"]) if scale is None else V.tensor_scalar(out["ap"], in_["ap"], scale, None, ALU.mult)
+        call(engs, fn, out, [in_])
+
+    def vts(out, in0, s1, s2, op0, op1=None):
+        if op1 is None:
+            call("V", lambda e: V.tensor_scalar(out["ap"], in0["ap"], ap(s1), None, op0), out, [in0, s1])
+        else:
+            call("V", lambda e: V.tensor_scalar(out["ap"], in0["ap"], ap(s1), ap(s2), op0, op1), out, [in0, s1, s2])
+
+    def vtt(out, in0, in1, op):
+        call("V", lambda e: V.tensor_tensor(out["ap"], in0["ap"], in1["ap"], op), out, [in0, in1], 1.0 if in0["psum"] or in1["psum"] else 2.0)
+
+    def vset(out, c):
+        call("V", lambda e: V.memset(out["ap"], c), out, [])
+
+    def scan(out, d0, d1, first, op0, op1):
+        call("V", lambda e: V.tensor_tensor_scan(out["ap"], d0["ap"], d1["ap"], first, op0, op1), out, [d0, d1])
+
+    def act(out, in_, func, bias=0.0, scale=1.0):
+        call("S", lambda e: S.activation(out["ap"], in_["ap"], func, bias=ap(bias), scale=scale), out, [in_, bias])
+
+    def iota(out, pattern, base, cm, small=True):
+        if small:
+            fn = lambda e: g.iota(out["ap"], pattern, base, cm, allow_small_or_imprecise_dtypes=True)
+        else:
+            fn = lambda e: g.iota(out["ap"], pattern, base, cm)
+        _add(pl, {"G": 130 * CFG["f"] + 2 * cyc * out["n"]}, fn, [], keys(out))
+
+    def wrap(out, data):
+        scan(out, at("hk", 0, data["n"]), data, 0.0, ALU.add, ALU.max)
+
+    def held(name, a, b):
+        return at(name, a + 15, b, 16)
+
+    def quant(q, sc, a, b, tile, ta):
+        in_ = at(tile, 4 * ta, 4 * (ta + b - a))
+        _add(pl, {"V": CFG["f"] * (12 + 0.22 * in_["n"])}, lambda e: V.quantize_mx(at(q, a, b)["ap"], at(sc, a, b)["ap"], in_["ap"]),
+             keys(in_), keys(at(q, a, b), at(sc, a, b)))
+
+    def mm(b, w, x, start=True, stop=True):
+        sides = [at(w[0], w[2], w[3]), at(w[1], w[2], w[3]), at(x[0], x[2], x[3]), at(x[1], x[2], x[3])]
+        out = bank(b, x[3] - x[2])
+        _add(pl, {"P": 0.65 * (x[3] - x[2] + 16)},
+             lambda e: g.tensor.matmul_mx(out["ap"], sides[0]["ap"], sides[1]["ap"], sides[2]["ap"], sides[3]["ap"], start, stop),
+             keys(*sides), keys(out))
+
+    def unpack(b, into, x, start=True, stop=True):
+        mm(into, ("qe", "se", 128 * b, 128 * b + 128), x, start, stop)
+
+    def load(eng, out, in_, sem, after=(), codes=False):
+        q = S if eng == "S" else g.sync
+        o = out["ap"].bitcast(dt.uint8) if codes else out["ap"]
+        queued[0] += CFG["lrows"] + 0.4 * out["n"] * out["bytes"]
+        n = _add(pl, {eng: 60.0}, lambda e: q.dma_start(o, in_), [], keys(out), kind="dma", sem=sem, total=16,
+                 lag=CFG["load"] + queued[0], after=after, behind=loads[-1:])
+        loads.append(n)
+        return n
+
+    def send(dst, out, in_, sem, codes=False):
         rid, pid, _ = topo.addr(dst)
         sent[0] += len(topo.engines(core, dst))
-        _add(pl, "G", lambda: g.remote_dma(out, in_, T.sem[sem], T.sem.sent, pid, rid, topo.mask(core, dst)), reads, [], kind="send")
+        o, i = (out["ap"].bitcast(dt.uint8), in_["ap"].bitcast(dt.uint8)) if codes else (out["ap"], in_["ap"])
+        n = _add(pl, {"G": 100.0}, lambda e: g.remote_dma(o, i, T.sem[sem], T.sem.sent, pid, rid, topo.mask(core, dst)), keys(in_), [],
+                 kind="send", lag=CFG["link"] + (0.0 if last else CFG["first"]), behind=last[-1:])
+        last.append(n)
+        return _add(pl, {"L": CFG["rows"] + 128 * in_["n"] * in_["bytes"] / CFG["bw"]}, None, [], [], kind="in", after=[n])
 
-    def arrives(src, sem, writes, keys):
-        _add(pl, "G", None, [], keys, kind="in", sem=sem, total=writes * len(topo.engines(src, core)))
-
-    def vts(out, in0, s1, s2, op0, op1, reads, writes):
-        if op1 is None:
-            v(lambda: V.tensor_scalar(out, in0, s1, None, op0), reads, writes)
-        else:
-            v(lambda: V.tensor_scalar(out, in0, s1, s2, op0, op1), reads, writes)
-
-    def vtt(out, in0, in1, op, reads, writes):
-        v(lambda: V.tensor_tensor(out, in0, in1, op), reads, writes)
-
-    def vcp(out, in_, reads, writes):
-        v(lambda: V.tensor_copy(out, in_), reads, writes)
-
-    def vset(ap, c, writes):
-        v(lambda: V.memset(ap, c), [], writes)
-
-    def scan(out, d0, d1, first, op0, op1, reads, writes):
-        v(lambda: V.tensor_tensor_scan(out, d0, d1, first, op0, op1), reads, writes)
-
-    def act(out, in_, reads, writes, func=ACT.Copy, **kw):
-        s(lambda: S.activation(out, in_, func, **kw), reads, writes)
-
-    def times(eng, out, in_, c, reads, writes):
-        if eng == "S":
-            act(out, in_, reads, writes, scale=c)
-        else:
-            vts(out, in_, c, None, ALU.mult, None, reads, writes)
-
-    def iota(out, pattern, base, cm, key, small=True):
-        if small:
-            gp(lambda: g.iota(out, pattern, base, cm, allow_small_or_imprecise_dtypes=True), [], [key])
-        else:
-            gp(lambda: g.iota(out, pattern, base, cm), [], [key])
-
-    def wrap(out, data, reads, key, n):
-        scan(out, T.hk[:, 0:n], data, 0.0, ALU.add, ALU.max, reads + ["hk"], key if isinstance(key, list) else [key])
-
-    def quant(q, sc, in_, reads, writes):
-        v(lambda: V.quantize_mx(q, sc, in_), reads, writes)
+    def arrives(src, sem, sends, outs):
+        _add(pl, {"in": 0.0}, None, [], keys(*outs), kind="in", sem=sem, total=len(sends) * len(topo.engines(src, core)),
+             lag=-CFG["wake"], after=sends)
 
     def col(j):
-        return T.cps[:, j:j + 1]
+        return at("cps", j, j + 1)
 
-    load("S", T.us[:], T.u[:], "l_u", "us")
-    load("Y", T.cdi[:], T.cd[:], "l_cd", "cdi")
-    load("Y", T.xs[:, 0:4 * H], T.x[:, 0:4 * H], "l_xa", "xs.a")
-    load("Y", T.xs[:, 4 * H:4 * C], T.x[:, 4 * H:4 * C], "l_xb", "xs.b")
-    load("Y", T.wq[:].bitcast(dt.uint8), T.wc[:], "l_wc", "wq", after=["xs.a", "xs.b"])
-    load("Y", T.wsc[:], T.ws[:], "l_ws", "wsc")
-    load("Y", T.vs[:], T.v[:], "l_v", "vs")
+    load("S", at("us"), T.u[:], "l_u")
+    load("Y", at("cdi"), T.cd[:], "l_cd")
+    xa = load("Y", at("xs", 0, 4 * H), T.x[:, 0:4 * H], "l_xa")
+    xb = load("Y", at("xs", 4 * H, 4 * C), T.x[:, 4 * H:4 * C], "l_xb")
 
-    iota(T.i16[:, 0:20], [[16, 20]], 0, 0, "i16")
-    iota(T.a16[:, 0:16], [[1, 16]], 128, -1, "a16", small=False)
-    iota(T.a16[:, 16:17], [[1, 1]], 0, 1, "a16p", small=False)
-    iota(T.iot[:], [[1, C]], Z - SH, 0, "iot")
-    iota(T.ones[:], [[0, 128]], 1, 0, "ones")
-    vset(T.ebig[:], 0.0, ["ebig"])
-    gp(lambda: g.affine_select(T.ebig[:, 3:515:4], T.ones[:], [[-1, 128]], ALU.is_equal, 0.0, 0, 1), ["ones"], ["ebig"])
-    iota(T.w1[:, 0:2 * Z], [[1, Z], [0, 2]], -SH - 1, 0, "w1z")
-    iota(T.w2[:, 0:Z], [[0, 4], [-2, 2], [1, 2]], 2 - SH, 0, "w2z")
-    iota(T.wa[:, 0:Z], [[1, Z]], -SH, 0, "waz")
-    iota(T.wb[:, 0:Z], [[1, Z]], -SH, 0, "wbz")
-    iota(T.lab[:, 0:Z], [[0, 4], [C, 4]], 0, 0, "labz")
+    iota(at("i16"), [[16, 8]], 0, 0)
+    iota(at("a16", 0, 16), [[1, 16]], 128, -1, small=False)
+    iota(at("iot"), [[1, C]], Z - SH, 0)
+    vset(at("ones"), 1.0)
+    vset(at("ebig"), 0.0)
+    diag = at("ebig", 3, 515, 4)
+    _add(pl, {"G": 170 * CFG["f"] + 256 * cyc},
+         lambda e: g.affine_select(diag["ap"], T.ones[:], [[-1, 128]], ALU.is_equal, 0.0, 0, 1), keys(at("ones")), keys(diag))
+    iota(at("w1", 0, 2 * Z), [[1, Z], [0, 2]], -SH - 1, 0)
+    iota(at("w2", 0, Z), [[0, 4], [-2, 2], [1, 2]], 2 - SH, 0)
+    for w in ("wa", "wb", "wc2", "wd"):
+        vts(at(w, 0, Z), at("iot", 0, Z), -float(Z), None, ALU.add)
+    iota(at("lab", 0, Z), [[0, 4], [C, 4]], -LAB, 0)
+    vts(at("col16"), at("iot"), float(3 * C + SH - Z), None, ALU.add)
+    vset(at("flg"), 0.0)
+    copy("V", at("uoff", 0, 8), at("i16"))
+    vts(at("b16", 0, 16), at("a16", 0, 16), 15, None, ALU.bitwise_and)
+    vset(at("zer"), 0.0)
+    for b in range(4):
+        vset(at("pr", C * b + A, C * b + C), 0.0)
+    vts(at("e0"), at("b16", 0, 16), 0.0, -4 * KEEP, ALU.is_equal, ALU.mult)
+    vts(at("e1"), at("b16", 0, 16), 1.0, KEEP, ALU.is_equal, ALU.mult)
+    copy("V", at("cdo", 0, 40), at("cdi"))
+    vtt(at("hk", 0, 16), at("e0"), at("e1"), ALU.add)
+    for a, b in ((16, 32), (32, 64), (64, 128), (128, 256)):
+        copy("VS", at("hk", a, b), at("hk", 0, b - a))
+    copy("VS", at("c1"), by(at("iot"), at("cdo", 0, 20)))
+    quant("qu", "su", 0, 128, "us", 0)
+    for b in range(4):
+        diag_b = at("ebig", 3 - b, 515 - b)
+        _add(pl, {"V": CFG["f"] * (12 + 0.22 * 512)},
+             lambda e, b=b, t=diag_b: V.quantize_mx(T.qe[:, 128 * b:128 * b + 128], T.se[:, 128 * b:128 * b + 128], t["ap"]),
+             keys(diag_b), keys(at("qe", 128 * b, 128 * b + 128), at("se", 128 * b, 128 * b + 128)))
+    picked = by(at("qu"), at("uoff", 0, 8), words=True)
+    call("V", lambda e: V.tensor_copy(T.qup[:].bitcast(dt.uint32), picked["ap"]), at("qup"), [picked])
+    copy("VS", at("sup"), by(at("su"), at("uoff", 0, 8)))
+    vtt(at("cdf", 0, 2 * C, 2), by(at("iot"), at("cdo", 20, 40)), at("c1"), ALU.subtract)
+    vset(at("w1", 1, 2), 3.0 - SH)
+    copy("V", at("cdf", 3, 2 * C, 2), at("c1", 1, C))
+    vset(at("cdf", 1, 2), 3.0 - SH)
+    for j, c0 in enumerate([SH + 0.5, SH, SH - Z, H, 2 * C]):
+        act(col(j), at("e1", 0, 1), ACT.Identity, bias=float(c0 - KEEP))
+    cp_pair, cp_ptr, cp_base, cp_place, cp_slot = [col(j) for j in range(5)]
 
-    vset(T.flg[:], 0.0, ["flg.a", "flg.b"])
-    vcp(T.uoff[:, 0:8], T.i16[:, 0:8], ["i16"], ["uoff"])
-    vts(T.b16[:, 0:17], T.a16[:, 0:17], 15, None, ALU.bitwise_and, None, ["a16", "a16p"], ["b16"])
-    vset(T.mw[:, A:12 * MWW:MWW], 0.0, ["mwz"])
-    vset(T.zer[:], 0.0, ["zer"])
-    vts(T.e0[:], T.b16[:, 0:16], 0.0, -4 * KEEP, ALU.is_equal, ALU.mult, ["b16"], ["e0"])
-    vts(T.e1[:], T.b16[:, 0:16], 1.0, KEEP, ALU.is_equal, ALU.mult, ["b16"], ["e1"])
-    vcp(col(8), T.b16[:, 16:17], ["b16"], ["cp8"])
-    vcp(T.cdo[:, 0:40], T.cdi[:], ["cdi"], ["cdo"])
-    vtt(T.hk[:, 0:16], T.e0[:], T.e1[:], ALU.add, ["e0", "e1"], ["hk"])
-    act(T.c1[:], T.iot[:].indirect(T.cdo[:, 0:20]), ["iot", "cdo"], ["c1"])
-    quant(T.qu[:], T.su[:], T.us[:], ["us"], ["qu"])
-    for b in range(2):
-        quant(T.qe[:, 128 * b:128 * b + 128], T.se[:, 128 * b:128 * b + 128], T.ebig[:, 3 - b:515 - b], ["ebig"], ["qe%d" % b])
-    vcp(T.qup[:].bitcast(dt.uint32), T.qu[:].bitcast(dt.uint32).indirect(T.uoff[:, 0:8]), ["qu", "uoff"], ["qup"])
-    act(T.sup[:], T.su[:].indirect(T.uoff[:, 0:8]), ["qu", "uoff"], ["sup"])
-    vtt(T.cdf[:, 0:2 * C:2], T.iot[:].indirect(T.cdo[:, 20:40]), T.c1[:], ALU.subtract, ["iot", "cdo", "c1"], ["cdf0"])
-    vset(T.w1[:, 1:2], 3.0 - SH, ["w1z"])
-    steps = ((16, 32), (32, 64), (64, 128), (128, 256), (256, 320))
-    for j, (m, c0) in enumerate([(1.0, SH + 0.5), (1.0, SH), (1.0, SH - Z), (2.0, SH - Z - C), (1.0, H),
-                                 (1.0, SH - Z + C // 2), (1.0, 0), (1.0, H + A // 2)]):
-        if j < len(steps):
-            act(T.hk[:, steps[j][0]:steps[j][1]], T.hk[:, 0:steps[j][1] - steps[j][0]], ["hk"], ["hk"])
-        act(col(j), T.e1[:, 0:1], ["e1"], ["cp%d" % j], func=ACT.Identity, bias=float(c0 - m * KEEP), scale=m)
-    cp_pair, cp_ptr, cp_base, cp_bq, cp_place, cp_take, cp_none, cp_from = [col(j) for j in range(8)]
+    low = CFG["low"]
+    runs = [(a, a + 32) for a in range(0, low, 32)] + [(a, a + 64) for a in range(low, C, 64)]
+    fills = [(a, min(C, a + CFG["fill"])) for a in range(0, C, CFG["fill"])]
 
-    def unpack(b, into, q, sc, n, reads):
-        mm(into, T.qe[:, 128 * b:128 * b + 128], T.se[:, 128 * b:128 * b + 128], q, sc, n, reads + ["qe%d" % b])
+    def off(d, a, b):
+        return at("off", 32 * d + a // 16, 32 * d + b // 16)
 
-    def layer(b, into, q, sc, n, reads):
-        mm(into, T.wq[:, 128 * b:128 * b + 128], T.wsc[:, 128 * b:128 * b + 128], q, sc, n, reads + ["wq", "wsc"])
-
-    xt, xkeys = T.xs, (["xs.a"], ["xs.b"])
+    tile = "xs"
     for r in range(R + 1):
-        qx, sx = T["qx%d" % r], T["sx%d" % r]
-        ka, kb = "qx%d.a" % r, "qx%d.b" % r
-        side = (T.qup[:], T.sup[:], ["qup", "sup"]) if r < R else (T.qv[:], T.sv[:], ["qv"])
-        quant(qx[:, 0:H], sx[:, 0:H], xt[:, 0:4 * H], xkeys[0], [ka])
-        for bk in ((4, 6) if r < R else (4,)):
-            mm(bk, side[0], side[1], qx[:, 0:H], sx[:, 0:H], H, side[2] + [ka])
-        if r == 0:
-            vset(T.c1[:, 0:1], 3.0 - SH, ["c1"])
-        quant(qx[:, H:C], sx[:, H:C], xt[:, 4 * H:4 * C], xkeys[1], [kb])
-        mm(5, side[0], side[1], qx[:, H:C], sx[:, H:C], H, side[2] + [kb])
+        qx, sx = "qx%d" % r, "sx%d" % r
+        side = ("qup", "sup", 0, 128) if r < R else ("qv", "sv", 0, 128)
+        for k, (a, b) in enumerate(halves):
+            quant(qx, sx, a, b, tile, a)
+            mm(4 + k, side, (qx, sx, a, b))
         if r == R:
             break
         dst, src = T.cores[(rank + STEP[r]) % n_ranks], T.cores[(rank - STEP[r]) % n_ranks]
-        lq, ls, lb, ll, ob, ol = [T["%s%d" % (k, r)] for k in ("lq", "ls", "lb", "ll", "ob", "ol")]
-        pt, qp, sp, mt, qm, sm, xn = [T["%s%d" % (k, r)] for k in ("pt", "qp", "sp", "mt", "qm", "sm", "xn")]
-        send(dst, lq[:].bitcast(dt.uint8), qx[:].bitcast(dt.uint8), "aq%d" % r, [ka, kb])
-        send(dst, ls[:], sx[:], "aq%d" % r, [ka, kb])
-        arrives(src, "aq%d" % r, 2, ["lq"])
-        arrives(src, "ab%d" % r, 1, ["lb"])
-        arrives(src, "al%d" % r, 1, ["ll"])
-        arrives(src, "am%d" % r, 1, ["lm"])
+        lq, ls, lb, ll, ob, ol, qp, sp, qm, sm = ["%s%d" % (k, r) for k in ("lq", "ls", "lb", "ll", "ob", "ol", "qp", "sp", "qm", "sm")]
+        first = [send(dst, at(lq, 0, H), at(qx, 0, H), "aq%d" % r, codes=True), send(dst, at(ls), at(sx), "aq%d" % r)]
+        arrives(src, "aq%d" % r, first, [at(lq, 0, H), at(ls)])
+        arrives(src, "ar%d" % r, [send(dst, at(lq, H, C), at(qx, H, C), "ar%d" % r, codes=True)], [at(lq, H, C)])
 
-        if r == 0:
-            vcp(T.cdf[:, 1:2 * C:2], T.c1[:], ["c1"], ["cdf1"])
-            quant(T.qe[:, 256:384], T.se[:, 256:384], T.ebig[:, 1:513], ["ebig"], ["qe2"])
-        vcp(T.sc[:, 0:H], bank(4, H), ["bank4"], ["sc.a"])
-        act(T.sc2[:, 0:H], bank(6, H), ["bank6"], ["sc2.a"])
-        act(T.sc[:, H:C], bank(5, H), ["bank5"], ["sc.b"])
-        act(T.sc2[:, H:C], bank(5, H), ["bank5"], ["sc2.b"])
-        if r == 0:
-            quant(T.qe[:, 384:512], T.se[:, 384:512], T.ebig[:, 0:512], ["ebig"], ["qe3"])
-        vtt(T.d1[:, 0:H], T.sc[:, 0:H].indirect(T.cdo[:, 0:10]), T.sc2[:, 0:H], ALU.subtract, ["sc.a", "sc2.a", "cdo"], ["d1.a"])
-        vtt(T.d2[:, 0:H], T.sc[:, 0:H].indirect(T.cdo[:, 20:30]), T.sc2[:, 0:H], ALU.subtract, ["sc.a", "sc2.a", "cdo"], ["d2.a"])
-        act(T.g2[:, H:C], T.sc[:].indirect(T.cdo[:, 30:40]), ["sc.a", "sc.b", "cdo"], ["g2"])
-        vtt(T.d1[:, H:C], T.sc[:].indirect(T.cdo[:, 10:20]), T.sc2[:, H:C], ALU.subtract, ["sc.a", "sc.b", "sc2.b", "cdo"], ["d1.b"])
-        vtt(T.d2[:, H:C], T.g2[:, H:C], bank(5, H), ALU.subtract, ["g2", "bank5"], ["d2.b"])
-        for h, a, b in halves:
-            act(T.a1[:, a:b], T.d1[:, a:b], ["d1." + h], ["a1." + h], func=ACT.Abs)
-            act(T.a2[:, a:b], T.d2[:, a:b], ["d2." + h], ["a2." + h], func=ACT.Abs)
-        for b in (0, 2, 3, 1):
-            unpack(b, 4 + b, qx[:], sx[:], C, [ka, kb])
-
-        def mine(b):
-            act(T.fo[:, C * b:C * b + C], bank(4 + b, C), ["bank%d" % (4 + b)], ["fo%d" % b])
-
-        for h, a, b in halves:
-            vtt(T.flg[:, 2 * a + 1:2 * b:2], T.a2[:, a:b], T.a1[:, a:b], ALU.is_lt, ["a1." + h, "a2." + h], ["flg." + h])
-        for b in range(3):
-            mine(b)
-        for h, a, b in halves:
-            scan(T.w1[:, 2 * (Z + a):2 * (Z + b)], T.flg[:, 2 * a:2 * b], T.cdf[:, 2 * a:2 * b], 0.0, ALU.mult, ALU.add,
-                 ["flg." + h, "cdf0", "cdf1"], ["w1.0", "w1.1"] if h == "a" else ["w1.1b", "w1.2"])
-        for h, a, b in halves:
-            wrap(T.hb[:, a:b], T.w1[:, 2 * (Z + a) + 1:2 * (Z + b):2], ["w1.0" if h == "a" else "w1.2"], "hb." + h, H)
-        for h, a, b in halves:
-            vts(T.offa[:, a // 16:b // 16], T.hb[:, a + 15:b:16], cp_pair, 2.0, ALU.add, ALU.mult, ["hb." + h, "cp0"],
-                ["offa.0", "offa.1"] if h == "a" else ["offa.1b", "offa.2"])
-
-        wins = [("w1", T.w1), ("w2", T.w2), ("wa", T.wa), ("wb", T.wb), ("wa", T.wa), ("wb", T.wb)]
-        offs = [("offa", T.offa), ("offb", T.offb)]
-        for d in range(5):
-            (k0, w0), (k1, w1_), (ko, of), (kn, on) = wins[d], wins[d + 1], offs[d % 2], offs[(d + 1) % 2]
-            for what, p in DOUBLING:
-                a, b, e = PARTS[p]
-                if what == "g":
-                    (act if e == "S" else vcp)(w1_[:, Z + a:Z + b], w0[:, 0:(2 if d == 0 else 1) * (Z + b)].indirect(of[:, a // 16:b // 16]),
-                                               ["%s.%d" % (k0, q) for q in range(p + 1)] + [k0 + "z", "%s.%d" % (ko, p)]
-                                               + (["w1.1b", "offa.1b"] if d == 0 and p > 0 else []), ["%s.%d" % (k1, p)])
-                    if d == 0 and p == 0:
-                        vts(ob[:, 0:20], T.hb[:, 15:C:16], cp_base, None, ALU.add, None, ["hb.a", "hb.b", "cp2"], ["ob%d" % r])
-                        send(dst, lb[:, 0:20], ob[:, 0:20], "ab%d" % r, ["ob%d" % r])
-                        vts(T.bq[:, 0:20], T.hb[:, 15:C:16], cp_bq, None, ALU.add, None, ["hb.a", "hb.b", "cp3"], ["bq"])
-                elif what == "w":
-                    wrap(T.hh[:, a:b], w1_[:, Z + a:Z + b], ["%s.%d" % (k1, p)], "hh.%d" % p, b - a)
+        for k, (a, b) in enumerate(halves):
+            copy("VS", at("sc", a, b), bank(4 + k, H))
+            if "V" in CFG["cand"][2 * k:2 * k + 2]:
+                mm(6 + k, side, (qx, sx, a, b))
+                copy("VS", at("sc2", a, b), bank(6 + k, H))
+        for k, (a, b) in enumerate(halves):
+            for c in range(2):
+                theirs = by(at("sc", 0, b), at("cdo", (C * c + a) // 16, (C * c + b) // 16))
+                d = at("dd", C * c + a, C * c + b)
+                if CFG["cand"][2 * k + c] == "V":
+                    vtt(d, theirs, at("sc2", a, b), ALU.subtract)
                 else:
-                    vts(on[:, a // 16:b // 16], T.hh[:, a + 15:b:16], cp_ptr, None, ALU.add, None, ["hh.%d" % p, "cp1"], ["%s.%d" % (kn, p)])
+                    copy("S", at("gc", C * c + a, C * c + b), theirs)
+                    vtt(d, at("gc", C * c + a, C * c + b), bank(4 + k, H), ALU.subtract)
+                act(at("aa", C * c + a, C * c + b), d, ACT.Abs)
+            vtt(at("flg", 2 * a + 1, 2 * b, 2), at("aa", C + a, C + b), at("aa", a, b), ALU.is_lt)
+            scan(at("w1", 2 * (Z + a), 2 * (Z + b)), at("flg", 2 * a, 2 * b), at("cdf", 2 * a, 2 * b), 0.0, ALU.mult, ALU.add)
+            wrap(at("hb", a, b), at("w1", 2 * (Z + a) + 1, 2 * (Z + b), 2))
+            vts(off(0, a, b), held("hb", a, b), cp_pair, 2.0, ALU.add, ALU.mult)
+        vts(at(ob, 0, 20), held("hb", 0, C), cp_base, None, ALU.add)
+        arrives(src, "ab%d" % r, [send(dst, at(lb, 0, 20), at(ob, 0, 20), "ab%d" % r)], [at(lb, 0, 20)])
 
-        def piece(what, k):
-            a, b = ((0, LOW), (LOW, A), (A, C))[k]
-            lab, rd = T.lab[:, Z + a:Z + b], ["lab%d" % j for j, (lo, hi) in enumerate(RUNS) if a <= lo < b]
-            if what == "s":
-                act(T.ef[:, a:b], lab, rd, ["ef0.%d" % k], func=ACT.Relu, bias=1.0, scale=-1.0)
-                act(T.ef[:, 3 * C + a:3 * C + b], lab, rd, ["ef3.%d" % k], func=ACT.Relu, bias=1.0 - 3 * C)
-            elif what == "w":
-                wrap(T.hl[:, a:b], lab, rd, "hl.%d" % k, b - a)
-            else:
-                vts(T.ef[:, what * C + a:what * C + b], lab, float(what * C), None, ALU.is_equal, None, rd, ["ef%d.%d" % (what, k)])
+        if r == 0:
+            queued[0] = 0.0
+            landed = [len(pl["ops"]) - 1]
+            load("Y", at("wq"), T.wc[:], "l_wc", after=landed, codes=True)
+            load("Y", at("wsc"), T.ws[:], "l_ws")
+            load("Y", at("vs"), T.v[:], "l_v")
+            quant("qv", "sv", 0, 128, "vs", 0)
 
-        def theirs(b):
-            act(T.fd[:, 2 * C * b:2 * C * b + C], bank(b, C), ["bank%d" % b], ["fd%d.f" % b])
+        wins = ["w1", "w2", "wa", "wb", "wc2", "wd", "we"]
+        for d in range(6):
+            for a, b, e in CFG["parts"] if d < 5 else [(low, C, "VS")]:
+                copy(e, at(wins[d + 1], Z + a, Z + b), by(at(wins[d], 0, (2 if d == 0 else 1) * (Z + b)), off(d, a, b)))
+                wrap(at("hh", C * d + a, C * d + b), at(wins[d + 1], Z + a, Z + b))
+                vts(off(d + 1, a, b), held("hh", C * d + a, C * d + b), cp_ptr, None, ALU.add)
+        for a, b in runs:
+            copy(CFG["erun"], at("lab", Z + a, Z + b), by(at("lab", 0, Z + a), off(5 if a < low else 6, a, b)))
 
-        def bases(b):
-            act(T.gd[:, C * b:C * b + C], T.fd[:, 2 * C * b:2 * C * b + C].indirect(lb[:, 0:20]), ["fd%d.f" % b, "lb"], ["gd%d" % b])
+        for a, b in CFG["pieces"]:
+            lab = at("lab", Z + a, Z + b)
+            scan(at("li", a, b), lab, at("col16", a, b), 0.0, ALU.min, ALU.add)
+            wrap(at("hl", a, b), at("li", a, b))
+            vts(at("qq", a // 16, b // 16), held("hl", a, b), cp_slot, None, ALU.add)
+            for d in range(4):
+                flag = at("ef", C * d + a, C * d + b)
+                end = {0: (1.0 - LAB, -1.0), 3: (1.0 + LAB - 3 * C, 1.0)}.get(d)
 
-        def minus(b, a=0, e=C):
-            vtt(T.fd[:, 2 * C * b + C + a:2 * C * b + C + e], bank(b, e, a), T.gd[:, C * b + a:C * b + e], ALU.subtract,
-                ["bank%d" % b, "gd%d" % b], ["fd%d.d%d" % (b, a)])
+                def flags(e, flag=flag, lab=lab, d=d, end=end):
+                    if e == "S":
+                        return S.activation(flag["ap"], lab["ap"], ACT.Relu, bias=end[0], scale=end[1])
+                    return V.tensor_scalar(flag["ap"], lab["ap"], float(C * d - LAB), None, ALU.is_equal)
+                call("VS" if end else "V", flags, flag, [lab])
+        scan(at("cum"), at("ef"), at("zer"), -(H + 1.0), ALU.add, ALU.add)
+        for a, b in halves:
+            copy("VS", at("pl", a, b), by(at("cum"), at("qq", a // 16, b // 16)))
+            wrap(at("hp", a, b), at("pl", a, b))
+        vts(at("plo", 0, 20), held("hp", 0, C), cp_place, None, ALU.add)
+        copy("V", by(at("srt"), at("plo", 0, 20)), at("li"))
+        wrap(at("h2"), at("srt", 0, A))
+        vts(at(ol), held("h2", 0, A), cp_slot, None, ALU.add)
+        arrives(src, "al%d" % r, [send(dst, at(ll), at(ol), "al%d" % r)], [at(ll)])
 
         for b in range(4):
-            unpack(b, b, lq[:], ls[:], C, ["lq"])
-        act(T.wa[:, Z + LOW:PW], T.wb[:].indirect(T.offb[:, LOW // 16:20]), ["wb.0", "wb.1", "wb.2", "wbz", "offb.1", "offb.2"], ["wa.1", "wa.2"])
-        if r > 0:
-            theirs(0)
-        else:
-            mine(3)
-        for j, (a, b) in enumerate(RUNS):
-            of, ko = (T.offb, ["offb.0"]) if a < LOW else (T.offa, ["offa.1", "offa.2"])
-            vcp(T.lab[:, Z + a:Z + b], T.lab[:, 0:Z + a].indirect(of[:, a // 16:b // 16]),
-                ["labz"] + ko + ["lab%d" % i for i in range(j)], ["lab%d" % j])
-            if r == 0 and j == 0:
-                vts(T.iw[:, 0:20], T.i16[:, 0:20], col(8), cp_none, ALU.add, ALU.add, ["i16", "cp8", "cp6"], ["iw"])
-            if r == 0 and j == 1:
-                vts(T.kc[:], T.i16[:, 0:16], col(8), -(H + 0.5), ALU.add, ALU.add, ["i16", "cp8"], ["kc"])
-            if j == 2:
-                wrap(T.hh[:, LOW:C], T.wa[:, Z + LOW:PW], ["wa.1", "wa.2"], ["hh.1", "hh.2"], C - LOW)
-            if j == 3:
-                vts(T.offa[:, LOW // 16:20], T.hh[:, LOW + 15:C:16], cp_ptr, None, ALU.add, None, ["hh.1", "hh.2", "cp1"],
-                    ["offa.1", "offa.1b", "offa.2"])
-                piece("s", 0)
-                theirs(1 if r > 0 else 0)
-            if j == 4:
-                piece(1, 0)
-                piece(2, 0)
-            if j == 5:
-                piece("w", 0)
-                piece("s", 1)
-            if j == 6:
-                piece("w", 1)
-                piece(1, 1)
-                piece(2, 1)
+            if CFG["state"][b] == "V":
+                unpack(b, 6 + b % 2, (qx, sx, 0, C))
+                for a, e in fills:
+                    copy("S", at("fo", C * b + a, C * b + e), bank(6 + b % 2, e, a))
 
-        piece("s", 2)
-        bases(0)
-        if r == 0:
-            theirs(1)
-        hl = ["hl.0", "hl.1", "hl.2"]
-        piece("w", 2)
-        piece(1, 2)
-        piece(2, 2)
-        vtt(T.qf[:, 0:20], T.hl[:, 15:C:16], T.iw[:, 0:20], ALU.add, hl + ["iw"], ["qf0"])
-        vtt(T.qf[:, 20:40], T.hl[:, 15:C:16], T.bq[:, 0:20], ALU.add, hl + ["bq"], ["qf1"])
-        scan(T.cum[:], T.ef[:], T.zer[:], -(H + 1.0), ALU.add, ALU.add,
-             ["ef%d.%d" % (d, k) for d in range(4) for k in range(3)] + ["zer"], ["cum"])
-        vcp(T.qq[:, 0:40], T.qf[:], ["qf0", "qf1"], ["qq"])
-        act(T.pl[:, H:C], T.cum[:].indirect(T.qq[:, 10:20]), ["cum", "qq"], ["pl.b"])
-        vcp(T.pl[:, 0:H], T.cum[:].indirect(T.qq[:, 0:10]), ["cum", "qq"], ["pl.a"])
-        act(T.sg[:], T.kc[:], ["kc", "cum"], ["sg"], func=ACT.Sign, bias=T.cum[:, C - 1:C], scale=-1.0)
-        bases(1)
-        act(T.adj[:, 0:16], T.sg[:], ["sg", "cp5"], ["adj0"], func=ACT.Identity, bias=cp_take, scale=-C / 2)
-        act(T.adj[:, 16:32], T.sg[:], ["sg", "cp7"], ["adj1"], func=ACT.Identity, bias=cp_from, scale=A / 2)
-        theirs(2)
-        theirs(3)
-        act(T.pb[:], T.cum[:].indirect(T.qq[:, 20:40]), ["cum", "qq"], ["pb"])
-        bases(2)
-        bases(3)
-        minus(0, 0, H)
-        for h, a, b in halves:
-            wrap(T.hh[:, a:b], T.pl[:, a:b], ["pl." + h], ["hh.0", "hh.1"] if h == "a" else ["hh.2"], H)
-        minus(0, H, C)
-        vts(T.plo[:, 0:20], T.hh[:, 15:C:16], cp_place, None, ALU.add, None, ["hh.0", "hh.1", "hh.2", "cp4"], ["plo"])
-        vcp(T.srt[:].indirect(T.plo[:, 0:20]), T.iot[:], ["iot", "plo"], ["srt"])
-        minus(1, 0, H)
-        wrap(T.h2[:, 0:A], T.srt[:, 0:A], ["srt"], "h2", A)
-        wrap(T.h2[:, A:C], T.srt[:, A:C], ["srt"], "h2t", C - A)
-        minus(1, H, C)
-        vtt(T.vi[:, 0:16], T.h2[:, 15:A:16], T.adj[:, 0:16], ALU.add, ["h2", "adj0"], ["vi0"])
-        vts(T.oo[:, 0:20], T.h2[:, 15:C:16], cp_base, None, ALU.add, None, ["h2", "h2t", "cp2"], ["oo"])
-        vcp(ol[:, 0:16], T.vi[:, 0:16], ["vi0"], ["ol%d" % r])
-        send(dst, ll[:, 0:16], ol[:, 0:16], "al%d" % r, ["ol%d" % r])
+        def mv(b, d, a=0, e=C):
+            return at("mv", 4 * C * b + C * d + a, 4 * C * b + C * d + e)
 
-        def ordered(eng, b):
-            times(eng, T.zx[:, C * b:C * b + C], T.fo[:, C * b:C * b + C].indirect(T.oo[:, 0:20]), 64.0, ["fo%d" % b, "oo"],
-                  ["zx%d.a" % b, "zx%d.b" % b])
+        for b in range(4):
+            vts(at("lb4", 20 * b, 20 * b + 20), at(lb, 0, 20), 4.0, float(b), ALU.mult, ALU.add)
+        for k, (a, e) in enumerate(fills):
+            n, one, two = e - a, 4 * (k % 2), 4 * (1 - k % 2)
+            for b in range(4):
+                unpack(b, one + b, (lq, ls, a, e))
+                copy(CFG["eft"], at("ft", 4 * a + b, 4 * e, 4), bank(one + b, n))
+            quant(qp, sp, a, e, "ft", a)
+            for b in range(4):
+                copy(CFG["egt"], at("gt", 4 * a + b, 4 * e, 4), by(at("ft", 0, 4 * e), at("lb4", 20 * b + a // 16, 20 * b + e // 16)))
+                vtt(at("pt", 4 * a + b, 4 * e, 4), bank(one + b, n), at("gt", 4 * a + b, 4 * e, 4), ALU.subtract)
+            quant(qp, sp, C + a, C + e, "gt", a)
+            quant(qp, sp, 2 * C + a, 2 * C + e, "pt", a)
+        for k, (a, e) in enumerate(fills):
+            n, one, two = e - a, 4 * (k % 2), 4 * (1 - k % 2)
+            for b in range(4):
+                unpack(b, one + b, (qp, sp, C + a, C + e), True, False)
+                unpack(b, one + b, (qp, sp, 2 * C + a, 2 * C + e), False, True)
+                copy(CFG["em"], mv(b, 1, a, e), bank(one + b, n))
+                unpack(b, one + b, (qp, sp, 2 * C + a, 2 * C + e))
+                if "V" in (CFG["steps"][2][b], CFG["steps"][3][b]):
+                    copy(CFG["em"], at("md", C * b + a, C * b + e), bank(one + b, n))
+                for d in (2, 3):
+                    base = by(mv(b, d - 1, 0, e), at(lb, a // 16, e // 16))
+                    if CFG["steps"][d][b] == "V":
+                        vtt(mv(b, d, a, e), base, at("md", C * b + a, C * b + e), ALU.add)
+                    else:
+                        gb = at("gb", C * (4 * (d - 2) + b) + a, C * (4 * (d - 2) + b) + e)
+                        copy("S", gb, base)
+                        vtt(mv(b, d, a, e), bank(one + b, n), gb, ALU.add)
+        for b in range(4):
+            unpack(b, CFG["b0"][b], (qp, sp, 0, C))
+            for a, e in fills:
+                copy(CFG["em"], mv(b, 0, a, e), bank(CFG["b0"][b], e, a))
 
-        ordered("S", 1)
-        if r > 0:
-            mine(3)
-        vcp(T.pbo[:], T.pb[:].indirect(T.oo[:, 0:16]), ["pb", "oo"], ["pbo"])
-        minus(2)
-        wrap(T.h3[:], T.pbo[:], ["pbo"], "h3", A)
-        minus(3)
-        vtt(T.vi[:, 16:32], T.h3[:, 15:A:16], T.adj[:, 16:32], ALU.add, ["h3", "adj1"], ["vi1"])
-        ordered("V", 0)
-        if r == 0:
-            quant(T.qv[:], T.sv[:], T.vs[:], ["vs"], ["qv"])
-        vcp(ol[:, 16:32], T.vi[:, 16:32], ["vi1"], ["om%d" % r])
-        send(dst, ll[:, 16:32], ol[:, 16:32], "am%d" % r, ["om%d" % r])
-
-        for b in (2, 0, 3, 1):
-            f = act if b >= 2 else vcp
-            f(pt[:, b:4 * A:4], T.fd[:, 2 * C * b:2 * C * (b + 1)].indirect(ll[:, 0:16]),
-              ["fd%d.f" % b, "fd%d.d0" % b, "fd%d.d%d" % (b, H), "ll"], ["pt%d" % b])
-        ordered("S", 2)
-        for h, a, bk in (("a", 0, 4), ("b", HA, 5)):
-            quant(qp[:, a:a + HA], sp[:, a:a + HA], pt[:, 4 * a:4 * (a + HA)], ["pt0", "pt1", "pt2", "pt3"], ["qp." + h])
-            unpack(3, bk, qp[:, a:a + HA], sp[:, a:a + HA], HA, ["qp." + h])
-        for b in (2, 1, 0, 3):
-            unpack(b, b, qp[:], sp[:], A, ["qp.a", "qp.b"])
-
-        def plane(st, b):
-            return T.mw[:, MWW * (4 * st + b):MWW * (4 * st + b) + A]
-
-        def based(st, b):
-            return T.mw[:, MWW * (4 * st + b):MWW * (4 * st + b) + A + 1].indirect(ll[:, 16:32])
-
-        def into(st, b):
-            return (plane(st, b), "m%d.%d" % (st, b)) if st < 3 else (mt[:, b:4 * A:4], "mt%d" % b)
-
-        vcp(T.mw[:, 3 * MWW:3 * MWW + HA], bank(4, HA), ["bank4"], ["m0.3a"])
-        vcp(T.mw[:, 3 * MWW + HA:3 * MWW + A], bank(5, HA), ["bank5"], ["m0.3"])
-        for what, b, st in REBUILD:
-            out, ko = into(st, b)
-            gb = T.gb[:, A * b:A * b + A]
-            if what == "cv":
-                vcp(out, bank(b, A), ["bank%d" % b], [ko])
-            elif what == "g":
-                act(gb, based(st - 1, b), ["m%d.%d" % (st - 1, b), "m0.3a", "mwz", "lm"], ["gb%d" % b])
-            elif what == "a":
-                vtt(out, bank(b, A), gb, ALU.add, ["bank%d" % b, "gb%d" % b], [ko])
-            else:
-                vtt(out, based(st - 1, b), plane(0, b), ALU.add, ["m%d.%d" % (st - 1, b), "m0.%d" % b, "m0.3a", "mwz", "lm"], [ko])
-        ordered("S", 3)
-
-        for h, a, bk in (("a", 0, 4), ("b", HA, 5)):
-            quant(qm[:, a:a + HA], sm[:, a:a + HA], mt[:, 4 * a:4 * (a + HA)], ["mt0", "mt1", "mt2", "mt3"], ["qm." + h])
-            layer(0, bk, qm[:, a:a + HA], sm[:, a:a + HA], HA, ["qm." + h])
-        for b in (1, 3, 2):
-            layer(b, b, qm[:], sm[:], A, ["qm.a", "qm.b"])
-        for h, a, bk in (("a", 0, 4), ("b", HA, 5)):
-            vtt(T.zx[:, a:a + HA], bank(bk, HA), T.zx[:, a:a + HA], ALU.add, ["bank%d" % bk, "zx0." + h], ["zx0." + h])
-
-        def fetch(eng, b, a, e):
-            times(eng, xn[:, 4 * a + b:4 * e:4], T.zx[:, C * b:C * b + C].indirect(T.plo[:, a // 16:e // 16]), 0.015625,
-                  ["zx%d.a" % b, "zx%d.b" % b, "plo"], ["xn%d.%d" % (b, a)])
-
-        fetch("S", 0, 0, C)
-        for b in (1, 3, 2):
-            vtt(T.zx[:, C * b:C * b + A], bank(b, A), T.zx[:, C * b:C * b + A], ALU.add, ["bank%d" % b, "zx%d.a" % b], ["zx%d.a" % b])
-            if b == 1:
-                fetch("S", 1, 0, C)
-        fetch("V", 3, 0, C)
-        fetch("S", 2, H, C)
-        fetch("V", 2, 0, H)
-        xt, xkeys = xn, (["xn0.0", "xn1.0", "xn2.0", "xn3.0"], ["xn0.0", "xn1.0", "xn2.%d" % H, "xn3.0"])
+        for a, e in CFG["mparts"]:
+            for b in range(4):
+                copy("VS", at("mt", 4 * a + b, 4 * e, 4), by(at("mv", 4 * C * b, 4 * C * (b + 1)), at(ll, a // 16, e // 16)))
+            quant(qm, sm, a, e, "mt", a)
+        for b in range(4):
+            if CFG["state"][b] == "S":
+                unpack(b, 6 + b % 2, (qx, sx, 0, C))
+        for (a, e), banks in CFG["lparts"]:
+            for b in CFG["lorder"]:
+                mm(banks[b], ("wq", "wsc", 128 * b, 128 * b + 128), (qm, sm, a, e))
+                copy("VS", at("pr", C * b + a, C * b + e), bank(banks[b], e - a), scale=0.015625)
+        for a, e in CFG["xparts"]:
+            for b in range(4):
+                made = by(at("pr", C * b, C * b + C), at("plo", a // 16, e // 16))
+                out = at("xn", 4 * a + b, 4 * e, 4)
+                if CFG["state"][b] == "V":
+                    vtt(out, made, at("fo", C * b + a, C * b + e), ALU.add)
+                else:
+                    copy("S", at("gx", C * b + a, C * b + e), made)
+                    vtt(out, bank(6 + b % 2, e, a), at("gx", C * b + a, C * b + e), ALU.add)
+        tile = "xn"
 
     outs = {"S": 0, "Y": 0}
 
     def store(eng, out, in_, reads):
         outs[eng] += 16
         q = S if eng == "S" else g.sync
-        _add(pl, eng, lambda: q.dma_start(out, in_), reads, [], kind="dma", sem="out" + eng)
+        _add(pl, {eng: 60.0}, lambda e: q.dma_start(out, in_), keys(reads), [], kind="dma", sem="out" + eng, lag=CFG["load"] + 800.0)
 
-    act(T.ys[:, 0:H], bank(4, H), ["bank4"], ["ys.a"])
-    vcp(T.ys[:, H:C], bank(5, H), ["bank5"], ["ys.b"])
-    store("Y", T.oc[:], qx[:].bitcast(dt.uint8), [ka, kb])
-    store("S", T.y[:], T.ys[:], ["ys.a", "ys.b"])
+    for k, (a, b) in enumerate(halves):
+        copy("SV"[k], at("ys", a, b), bank(4 + k, H))
+    store("Y", T.oc[:], T[qx][:].bitcast(dt.uint8), at(qx))
+    store("S", T.y[:], T.ys[:], at("ys"))
     for k in range(4):
-        store("Y" if k < 2 else "S", T.osc[4 * k:4 * k + 4, :], sx[32 * k:32 * k + 4, :], [ka, kb])
+        store("Y" if k < 2 else "S", T.osc[4 * k:4 * k + 4, :], T[sx][32 * k:32 * k + 4, :], at(sx))
     _emit(pl, g, T)
     S.wait_ge(T.sem.outS, outs["S"])
     g.sync.wait_ge(T.sem.outY, outs["Y"])

@@ -1,3 +1,4 @@
+import math
 from concourse.mybir import dt, AluOpType as ALU, ActivationFunctionType as ACT
 
 C, A, R = 320, 256, 3
@@ -12,19 +13,24 @@ LAB = 5 * C
 BANK = 512
 
 CFG = {
+    "mid": 160,
     "low": 128,
-    "parts": [(0, 160, "V"), (160, 320, "S")],
-    "pieces": [(0, 256), (256, 320)],
-    "cand": "VVVS",
+    "parts": [(0, 160), (160, 320)],
+    "pieces": [(0, 192), (192, 320)],
+    "cand": "VSVS",
     "steps": {2: "VSSS", 3: "VSSS"},
-    "state": "VVVS",
-    "xparts": [(0, 160), (160, 320)],
-    "mparts": [(0, 128), (128, 256)],
-    "b0": [0, 1, 2, 3], "lparts": [((0, 128), [0, 1, 2, 3]), ((128, 256), [0, 1, 4, 5])], "lorder": [2, 0, 3, 1],
-    "fill": 160,
-    "wake": 170.0, "f": 1.15, "g": 1.56, "sc": 3.8, "link": 2000.0, "bw": 80.0, "rows": 480.0, "first": 1000.0, "load": 1500.0, "lrows": 240.0, "passes": 5,
-    "ahead": 60.0, "over": 400.0, "give": 300.0, "mix": 1.0, "eft": "VS", "egt": "VS", "em": "VS", "erun": "VS",
+    "state": "VVSS",
+    "sparts": [(0, 320)], "mparts": [(0, 128), (128, 256)], "grun": 2, "plparts": [(0, 160), (160, 320)], "xsplit": True,
+    "lparts": [((0, 128), [0, 1, 2, 3]), ((128, 256), [0, 1, 4, 5])], "lorder": [2, 0, 3, 1],
+    "sb": [4, 5], "db": [0, 1], "fb": [6, 7, 6, 7],
+    "passes": 3, "ahead": 60.0, "over": 400.0, "give": 300.0,
+    "tries": [200000, 60000, 20000], "heat": 15.0, "mean": 0.15,
 }
+PACES = [{"f": 1.05, "wake": 190.0, "g": 1.4, "sc": 3.8, "link": 1800.0, "rows": 480.0, "bw": 90.0, "load": 1500.0, "first": 1000.0,
+          "issue": 400.0},
+         {"f": 1.35, "wake": 120.0, "g": 1.7, "sc": 3.8, "link": 900.0, "rows": 280.0, "bw": 110.0, "load": 1000.0, "first": 1000.0,
+          "issue": 150.0}]
+QUEUES = ["V", "S", "P", "G", "Y", "L", "in"]
 ORDER = []
 
 
@@ -38,17 +44,17 @@ SCRATCH = {
     "qu": _sb(128, CODE), "su": _sb(128, "uint8"), "qup": _sb(128, CODE), "sup": _sb(128, "uint8"),
     "qv": _sb(128, CODE), "sv": _sb(128, "uint8"), "uoff": _sb(16, "uint16"),
     "ebig": _sb(528, "bfloat16"), "ones": _sb(128, "bfloat16"), "qe": _sb(512, CODE), "se": _sb(512, "uint8"),
-    "a16": _sb(24, "int32"), "b16": _sb(24, "int32"), "e0": _sb(16, "float32"), "e1": _sb(16, "float32"),
-    "cps": _sb(16, "float32"), "i16": _sb(8, "float32"),
-    "hk": _sb(C, "bfloat16"), "iot": _sb(C, "bfloat16"), "col32": _sb(C, "float32"), "col16": _sb(C, H16),
+    "a16": _sb(24, "int32"), "b16": _sb(24, "int32"), "e0": _sb(16, "float32"), "e1": _sb(16, "float32"), "e4": _sb(16, "float32"),
+    "cps": _sb(16, "float32"), "i16": _sb(8, "float32"), "a20": _sb(20, "int32"), "b20": _sb(40, "int32"), "rep": _sb(40, "uint16"),
+    "hk0": _sb(32, "bfloat16"),
+    "hk": _sb(C, "bfloat16"), "hk4": _sb(192, "bfloat16"), "iot": _sb(C, "bfloat16"), "col16": _sb(C, H16),
     "c1": _sb(C, "bfloat16"), "cdf": _sb(2 * C, H16), "flg": _sb(2 * C, "bfloat16"), "zer": _sb(4 * C, "bfloat16"),
     "sc": _sb(C, "float32"), "sc2": _sb(C, "float32"), "gc": _sb(2 * C, "float32"), "dd": _sb(2 * C, "float32"), "aa": _sb(2 * C, "float32"),
-    "w1": _sb(2 * PW, "bfloat16"), "w2": _sb(PW, "bfloat16"), "wa": _sb(PW, "bfloat16"), "wb": _sb(PW, "bfloat16"),
-    "wc2": _sb(PW, "bfloat16"), "wd": _sb(PW, "bfloat16"), "we": _sb(PW, "bfloat16"),
-    "lab": _sb(PW, "bfloat16"), "hb": _sb(C, H16), "hh": _sb(6 * C, H16), "li": _sb(C, H16), "hl": _sb(C, H16), "hp": _sb(C, H16),
-    "h2": _sb(A, H16), "off": _sb(7 * 32, "uint16"), "qq": _sb(32, "uint16"),
+    "w1": _sb(2 * PW, "bfloat16"), "ww": _sb(6 * PW, "bfloat16"),
+    "lab": _sb(PW, "bfloat16"), "hb": _sb(C, H16), "h4": _sb(C, H16), "hh": _sb(6 * C, H16), "li": _sb(C, H16), "hl": _sb(C, H16),
+    "hp": _sb(C, H16), "h2": _sb(A, H16), "off": _sb(7 * 32, "uint16"), "qq": _sb(32, "uint16"),
     "ef": _sb(4 * C, "bfloat16"), "cum": _sb(4 * C, "bfloat16"), "pl": _sb(C, "bfloat16"), "plo": _sb(32, "uint16"),
-    "srt": _sb(C, "float32"), "lb4": _sb(80, "uint16"),
+    "srt": _sb(C, "float32"),
     "fo": _sb(4 * C, "bfloat16"), "md": _sb(4 * C, "bfloat16"), "mv": _sb(16 * C, "bfloat16"), "gb": _sb(8 * C, "bfloat16"),
     "pr": _sb(4 * C, "float32"), "gx": _sb(4 * C, "float32"), "ys": _sb(C, "float32"),
     "ft": _sb(4 * C, "bfloat16"), "gt": _sb(4 * C, "bfloat16"), "pt": _sb(4 * C, "bfloat16"), "mt": _sb(4 * A, "bfloat16"),
@@ -61,9 +67,9 @@ for _r in range(R + 1):
 for _r in range(R):
     SCRATCH["lq%d" % _r] = _sb(C, CODE)
     SCRATCH["ls%d" % _r] = _sb(C, "uint8")
-    SCRATCH["lb%d" % _r] = _sb(32, "uint16")
+    SCRATCH["lb%d" % _r] = _sb(112, "uint16")
     SCRATCH["ll%d" % _r] = _sb(16, "uint16")
-    SCRATCH["ob%d" % _r] = _sb(32, "uint16")
+    SCRATCH["ob%d" % _r] = _sb(112, "uint16")
     SCRATCH["ol%d" % _r] = _sb(16, "uint16")
     SCRATCH["qp%d" % _r] = _sb(3 * C, CODE)
     SCRATCH["sp%d" % _r] = _sb(3 * C, "uint8")
@@ -71,7 +77,7 @@ for _r in range(R):
     SCRATCH["sm%d" % _r] = _sb(A, "uint8")
 
 SEMAPHORES = (["cV", "cS", "cP", "cG", "sent", "l_cd", "l_u", "l_xa", "l_xb", "l_v", "l_wc", "l_ws", "outS", "outY"]
-              + ["a%s%d" % (k, r) for k in "qrbl" for r in range(R)])
+              + ["a%s%d" % (k, r) for k in "qrcbl" for r in range(R)])
 
 BYTES = {"float32": 4, "int32": 4, CODE: 4, "bfloat16": 2, H16: 2, "uint16": 2, "uint8": 1}
 
@@ -103,12 +109,22 @@ def _add(pl, costs, fn, reads, writes, kind="c", sem=None, total=0, lag=0.0, aft
     return n
 
 
+def _edges(pl):
+    ops = pl["ops"]
+    pred = [[(j, ops[j]["lag"] + pl["wake"]) for j in sorted(op["deps"] | op["shared"])] + [(j, 0.0) for j in op["behind"]] for op in ops]
+    succ = [[] for _ in ops]
+    for k in range(len(ops)):
+        for j, delay in pred[k]:
+            succ[j].append((k, delay))
+    return pred, succ
+
+
 def _list(ops, pred, succ, worth, first):
     n = len(ops)
     left = [len(p) for p in pred]
     since = list(first)
     ready = {k: since[k] for k in range(n) if not left[k]}
-    free = {e: 0.0 for e in ("V", "S", "P", "G", "Y", "in", "L")}
+    free = {e: 0.0 for e in QUEUES}
     order, eng, end = [], {}, [0.0] * n
 
     def choose(e, mine):
@@ -123,7 +139,7 @@ def _list(ops, pred, succ, worth, first):
     while ready:
         best = None
         ranked = sorted(ready, key=lambda k: (-worth[k], k))
-        for e in free:
+        for e in QUEUES:
             mine = [k for k in ranked if e in ops[k]["costs"]]
             if e == "V":
                 ts, theirs = free["S"], set()
@@ -152,18 +168,9 @@ def _list(ops, pred, succ, worth, first):
     return order, eng, end
 
 
-def _edges(ops):
-    pred = [[(j, ops[j]["lag"] + CFG["wake"]) for j in sorted(op["deps"] | op["shared"])] + [(j, 0.0) for j in op["behind"]] for op in ops]
-    succ = [[] for _ in ops]
-    for k in range(len(ops)):
-        for j, delay in pred[k]:
-            succ[j].append((k, delay))
-    return pred, succ
-
-
-def _order(ops):
-    n = len(ops)
-    pred, succ = _edges(ops)
+def _first_order(pl):
+    ops, n = pl["ops"], len(pl["ops"])
+    pred, succ = _edges(pl)
     worth = [0.0] * n
     for k in range(n - 1, -1, -1):
         worth[k] = min(ops[k]["costs"].values()) + max([delay + worth[j] for j, delay in succ[k]] + [ops[k]["lag"]])
@@ -173,16 +180,123 @@ def _order(ops):
         span = max(end[k] + ops[k]["lag"] for k in range(n))
         if best is None or span < best[0]:
             best = (span, order, eng)
-        back = _list(ops, succ, pred, end, [op["lag"] for op in ops])[2]
-        worth = [CFG["mix"] * back[k] + (1 - CFG["mix"]) * worth[k] for k in range(n)]
-    return best
+        worth = _list(ops, succ, pred, end, [op["lag"] for op in ops])[2]
+    return best[1], best[2]
 
 
-def _emit(pl, g, T):
+def _mend(plans, order, eng, lo, hi, tries):
+    n = hi - lo
+    row = [k - lo for k in order]
+    on = [QUEUES.index(eng[k]) for k in range(lo, hi)]
+    either = [len(plans[0]["ops"][k]["costs"]) > 1 for k in range(lo, hi)]
+    paces = []
+    for pl in plans:
+        pred, succ = _edges(pl)
+        before = [[(j - lo, d, j in pl["ops"][k]["shared"]) for j, d in pred[k] if j >= lo] for k in range(lo, hi)]
+        later = [set(j - lo for j, _ in succ[k] if j < hi) for k in range(lo, hi)]
+        costs = [[pl["ops"][k]["costs"].get(q, 0.0) for q in QUEUES] for k in range(lo, hi)]
+        last = [(k, max(pl["ops"][lo + k]["lag"], 0.0) + pl["wake"]) for k in range(n) if not later[k]]
+        paces.append((before, costs, last))
+    earlier = [set(x[0] for x in p) for p in paces[0][0]]
+    arrival = QUEUES.index("in")
+
+    mean = CFG["mean"] / n
+
+    def span(ends, p0):
+        latest, missing = [-1] * len(QUEUES), arrival
+        for i in range(p0 - 1, -1, -1):
+            q = on[row[i]]
+            if latest[q] < 0 and q != arrival:
+                latest[q] = row[i]
+                missing -= 1
+                if not missing:
+                    break
+        rest, total, new = row[p0:], 0.0, []
+        for (before, costs, last), old in zip(paces, ends):
+            end = old[:]
+            free = [end[k] if k >= 0 else 0.0 for k in latest]
+            for k in rest:
+                q = on[k]
+                t = free[q]
+                for j, delay, soft in before[k]:
+                    x = end[j] + delay
+                    if x > t and not (soft and on[j] == q):
+                        t = x
+                end[k] = free[q] = t + costs[k][q]
+                free[arrival] = 0.0
+            total += max([end[k] + t for k, t in last]) + mean * sum(end)
+            new.append(end)
+        return total / len(paces), new
+
+    seed = [1]
+
+    def draw(m):
+        seed[0] = (seed[0] * 1103515245 + 12345) % 2147483648
+        return (seed[0] >> 8) % m
+
+    now, ends = span([[0.0] * n for _ in paces], 0)
+    best = (now, row[:], on[:])
+    for it in range(tries):
+        p = draw(n)
+        k = row[p]
+        was = on[k]
+        if was == arrival:
+            continue
+        way, steps = 2 * draw(2) - 1, (1, 1, 2, 3, 5, 8)[draw(6)]
+        if either[k] and draw(10) < 3:
+            on[k] = 1 - was
+            steps *= draw(2)
+        q, stop = p, (earlier[k] if way < 0 else later[k])
+        while steps and 0 <= q + way < n and row[q + way] not in stop:
+            q += way
+            if on[row[q]] == on[k]:
+                steps -= 1
+        if q == p and on[k] == was:
+            continue
+        row.insert(q, row.pop(p))
+        s, new = span(ends, min(p, q))
+        if s <= now or draw(4096) < 4096 * math.exp((now - s) / (CFG["heat"] * (1 - it / tries) + 1)):
+            now, ends = s, new
+            if s < best[0]:
+                best = (s, row[:], on[:])
+            if it % 50 == 0:
+                row.sort(key=lambda k: round(ends[0][k] - paces[0][1][k][on[k]], 3))
+        else:
+            row.insert(p, row.pop(q))
+            on[k] = was
+    return [k + lo for k in best[1]], {lo + k: QUEUES[q] for k, q in enumerate(best[2])}
+
+
+def _order(plans):
+    order, eng = _first_order(plans[0])
+    cuts, n = plans[0]["cuts"], len(plans[0]["ops"])
+    like, begin = plans[0]["like"], plans[0]["begin"]
+    row, on = _mend(plans, [k for k in order if cuts[0] <= k < cuts[1]], eng, cuts[0], cuts[1], CFG["tries"][0])
+    place = {k - cuts[0]: i for i, k in enumerate(row)}
+    rows = []
+    for s, (lo, hi) in enumerate(zip([0] + cuts, cuts + [n])):
+        mine = [k for k in order if lo <= k < hi]
+        same = sorted((k for k in mine if k in like), key=lambda k: place[like[k]])
+        for k in same:
+            eng[k] = on[cuts[0] + like[k]]
+        spots = iter(same)
+        wish = [k for k in mine if k < begin] + [next(spots) if k in like else k for k in mine if k >= begin]
+        mine, done = [], set()
+        pred = _edges(plans[0])[0]
+        while wish:
+            k = next(k for k in wish if all(j < lo or j in done for j, _ in pred[k]))
+            wish.remove(k)
+            done.add(k)
+            mine.append(k)
+        if s in (0, len(cuts)):
+            mine, moved = _mend(plans, mine, eng, lo, hi, CFG["tries"][1 if s == 0 else 2])
+            eng.update(moved)
+        rows += mine
+    return rows, eng
+
+
+def _emit(pl, order, eng, g, T):
     ops = pl["ops"]
-    if not ORDER:
-        ORDER.append(_order(ops))
-    _, order, eng = ORDER[0]
     at = {n: k for k, n in enumerate(order)}
     queue = {"V": g.vector, "S": g.scalar, "P": g.tensor, "G": g, "Y": g.sync}
     known = {e: {} for e in queue}
@@ -230,13 +344,25 @@ def rank_program(g, core, T, topo):
     rank = T.rank_of(core)
     if rank is None:
         return
+    pl = _plan(g, core, rank, T, topo, PACES[0])
+    if not ORDER:
+        ORDER.append(_order([pl] + [_plan(g, core, rank, T, topo, pace) for pace in PACES[1:]]))
+    _emit(pl, ORDER[0][0], ORDER[0][1], g, T)
+    g.scalar.wait_ge(T.sem.outS, pl["outs"]["S"])
+    g.sync.wait_ge(T.sem.outY, pl["outs"]["Y"])
+    g.wait_ge(T.sem.sent, pl["sent"])
+
+
+def _plan(g, core, rank, T, topo, pace):
     n_ranks = len(T.cores)
-    pl = {"ops": [], "seen": {}}
+    pl = {"ops": [], "seen": {}, "cuts": [], "like": {}, "wake": pace["wake"], "sent": 0, "outs": {"S": 0, "Y": 0}}
     V, S = g.vector, g.scalar
-    sent, last, loads, queued = [0], [], [], [0.0]
-    H = C // 2
+    last, wire, loads, queued = [], [], [], [0.0]
+    H = CFG["mid"]
+    sb, db, fb = CFG["sb"], CFG["db"], CFG["fb"]
     halves = ((0, H), (H, C))
-    cyc = 0.83 * CFG["f"]
+    f = pace["f"]
+    cyc = 0.83 * f
 
     def at(name, a=0, b=None, st=1):
         where, shape, kind = SCRATCH[name]
@@ -247,7 +373,7 @@ def rank_program(g, core, T, topo):
         elif st == 1:
             cols = ((1 << n) - 1) << a
         else:
-            cols = sum(1 << c for c in range(a, b, st))
+            cols = ((1 << (st * n)) - 1) // ((1 << st) - 1) << a
         return {"ap": T[name][:, a:b:st] if st > 1 else T[name][:, a:b], "keys": [(name, cols)], "n": n, "bytes": BYTES[kind],
                 "psum": where == "psum", "list": False}
 
@@ -267,9 +393,9 @@ def rank_program(g, core, T, topo):
     def cost(e, out, ins, k=None):
         full = [x for x in ins if isinstance(x, dict) and x["n"] == out["n"]]
         if out["list"]:
-            return 50 * CFG["f"] + CFG["sc"] * cyc * out["n"]
+            return 50 * f + pace["sc"] * cyc * out["n"]
         if any(x["list"] for x in full):
-            return (50 if e == "V" else 65) * CFG["f"] + CFG["g"] * cyc * out["n"]
+            return (50 if e == "V" else 65) * f + pace["g"] * cyc * out["n"]
         if k is None:
             k = 0.5 if e == "V" and all(x["bytes"] == 2 for x in full + [out]) else 1.0
         return cyc * max(64, k * out["n"])
@@ -302,23 +428,22 @@ def rank_program(g, core, T, topo):
     def act(out, in_, func, bias=0.0, scale=1.0):
         call("S", lambda e: S.activation(out["ap"], in_["ap"], func, bias=ap(bias), scale=scale), out, [in_, bias])
 
-    def iota(out, pattern, base, cm, small=True):
+    def iota(out, pattern, base, cm, small=True, behind=()):
         if small:
             fn = lambda e: g.iota(out["ap"], pattern, base, cm, allow_small_or_imprecise_dtypes=True)
         else:
             fn = lambda e: g.iota(out["ap"], pattern, base, cm)
-        _add(pl, {"G": 130 * CFG["f"] + 2 * cyc * out["n"]}, fn, [], keys(out))
+        _add(pl, {"G": 130 * f + 2 * cyc * out["n"]}, fn, [], keys(out), behind=behind)
 
-    def wrap(out, data):
-        scan(out, at("hk", 0, data["n"]), data, 0.0, ALU.add, ALU.max)
+    def wrap(out, data, keeper="hk"):
+        scan(out, at(keeper, 0, data["n"]), data, 0.0, ALU.add, ALU.max)
 
-    def held(name, a, b):
-        return at(name, a + 15, b, 16)
+    def held(name, a, b, run=16):
+        return at(name, a + run - 1, b, run)
 
-    def quant(q, sc, a, b, tile, ta):
-        in_ = at(tile, 4 * ta, 4 * (ta + b - a))
-        _add(pl, {"V": CFG["f"] * (12 + 0.22 * in_["n"])}, lambda e: V.quantize_mx(at(q, a, b)["ap"], at(sc, a, b)["ap"], in_["ap"]),
-             keys(in_), keys(at(q, a, b), at(sc, a, b)))
+    def quant(q, sc, a, in_):
+        codes, plane = at(q, a, a + in_["n"] // 4), at(sc, a, a + in_["n"] // 4)
+        _add(pl, {"V": f * (12 + 0.22 * in_["n"])}, lambda e: V.quantize_mx(codes["ap"], plane["ap"], in_["ap"]), keys(in_), keys(codes, plane))
 
     def mm(b, w, x, start=True, stop=True):
         sides = [at(w[0], w[2], w[3]), at(w[1], w[2], w[3]), at(x[0], x[2], x[3]), at(x[1], x[2], x[3])]
@@ -333,32 +458,47 @@ def rank_program(g, core, T, topo):
     def load(eng, out, in_, sem, after=(), codes=False):
         q = S if eng == "S" else g.sync
         o = out["ap"].bitcast(dt.uint8) if codes else out["ap"]
-        queued[0] += CFG["lrows"] + 0.4 * out["n"] * out["bytes"]
-        n = _add(pl, {eng: 60.0}, lambda e: q.dma_start(o, in_), [], keys(out), kind="dma", sem=sem, total=16,
-                 lag=CFG["load"] + queued[0], after=after, behind=loads[-1:])
-        loads.append(n)
-        return n
+        queued[0] += 0.5 * pace["rows"] + 0.4 * out["n"] * out["bytes"]
+        loads.append(_add(pl, {eng: 60.0}, lambda e: q.dma_start(o, in_), [], keys(out), kind="dma", sem=sem, total=16,
+                          lag=pace["load"] + queued[0], after=after, behind=loads[-1:]))
+
+    def store(eng, out, in_, reads, rows=128):
+        pl["outs"][eng] += 16
+        q = S if eng == "S" else g.sync
+        n = _add(pl, {eng: 60.0}, lambda e: q.dma_start(out, in_), keys(reads), [], kind="dma", sem="out" + eng, lag=pace["load"])
+        _add(pl, {"L": rows / 256 * pace["rows"] + rows / 320 * reads["n"] * reads["bytes"]}, None, [], [], kind="in", after=[n])
 
     def send(dst, out, in_, sem, codes=False):
         rid, pid, _ = topo.addr(dst)
-        sent[0] += len(topo.engines(core, dst))
+        pl["sent"] += len(topo.engines(core, dst))
         o, i = (out["ap"].bitcast(dt.uint8), in_["ap"].bitcast(dt.uint8)) if codes else (out["ap"], in_["ap"])
-        n = _add(pl, {"G": 100.0}, lambda e: g.remote_dma(o, i, T.sem[sem], T.sem.sent, pid, rid, topo.mask(core, dst)), keys(in_), [],
-                 kind="send", lag=CFG["link"] + (0.0 if last else CFG["first"]), behind=last[-1:])
+        n = _add(pl, {"G": pace["issue"]}, lambda e: g.remote_dma(o, i, T.sem[sem], T.sem.sent, pid, rid, topo.mask(core, dst)), keys(in_), [],
+                 kind="send", lag=pace["link"] + (0.0 if last else pace["first"]), behind=last[-1:])
         last.append(n)
-        return _add(pl, {"L": CFG["rows"] + 128 * in_["n"] * in_["bytes"] / CFG["bw"]}, None, [], [], kind="in", after=[n])
+        wire.append(_add(pl, {"L": pace["rows"] + 128 * in_["n"] * in_["bytes"] / pace["bw"]}, None, [], [], kind="in", after=[n],
+                         behind=wire[-1:]))
+        return wire[-1]
 
     def arrives(src, sem, sends, outs):
         _add(pl, {"in": 0.0}, None, [], keys(*outs), kind="in", sem=sem, total=len(sends) * len(topo.engines(src, core)),
-             lag=-CFG["wake"], after=sends)
+             lag=-pace["wake"], after=sends)
 
     def col(j):
         return at("cps", j, j + 1)
 
-    load("S", at("us"), T.u[:], "l_u")
+    def win(d, a, b):
+        return at("w1", 2 * a, 2 * b) if d == 0 else at("ww", PW * (d - 1) + a, PW * (d - 1) + b)
+
+    def off(d, a, b):
+        return at("off", 32 * d + a // 16, 32 * d + b // 16)
+
+    def mv(b, d, a=0, e=C):
+        return at("mv", 4 * C * b + C * d + a, 4 * C * b + C * d + e)
+
     load("Y", at("cdi"), T.cd[:], "l_cd")
-    xa = load("Y", at("xs", 0, 4 * H), T.x[:, 0:4 * H], "l_xa")
-    xb = load("Y", at("xs", 4 * H, 4 * C), T.x[:, 4 * H:4 * C], "l_xb")
+    load("Y", at("us"), T.u[:], "l_u")
+    load("Y", at("xs", 0, 4 * H), T.x[:, 0:4 * H], "l_xa")
+    load("Y", at("xs", 4 * H, 4 * C), T.x[:, 4 * H:4 * C], "l_xb")
 
     iota(at("i16"), [[16, 8]], 0, 0)
     iota(at("a16", 0, 16), [[1, 16]], 128, -1, small=False)
@@ -366,33 +506,28 @@ def rank_program(g, core, T, topo):
     vset(at("ones"), 1.0)
     vset(at("ebig"), 0.0)
     diag = at("ebig", 3, 515, 4)
-    _add(pl, {"G": 170 * CFG["f"] + 256 * cyc},
+    _add(pl, {"G": 170 * f + 256 * cyc},
          lambda e: g.affine_select(diag["ap"], T.ones[:], [[-1, 128]], ALU.is_equal, 0.0, 0, 1), keys(at("ones")), keys(diag))
-    iota(at("w1", 0, 2 * Z), [[1, Z], [0, 2]], -SH - 1, 0)
-    iota(at("w2", 0, Z), [[0, 4], [-2, 2], [1, 2]], 2 - SH, 0)
-    for w in ("wa", "wb", "wc2", "wd"):
-        vts(at(w, 0, Z), at("iot", 0, Z), -float(Z), None, ALU.add)
-    iota(at("lab", 0, Z), [[0, 4], [C, 4]], -LAB, 0)
+    iota(win(0, 0, Z), [[1, Z], [0, 2]], -SH - 1, 0)
+    iota(win(1, 0, Z), [[0, 4], [-2, 2], [1, 2]], 2 - SH, 0)
+    iota(win(2, 0, Z), [[1, Z]], -SH, 0)
     vts(at("col16"), at("iot"), float(3 * C + SH - Z), None, ALU.add)
-    vset(at("flg"), 0.0)
+    vset(at("flg", 0, 2 * C, 2), 0.0)
     copy("V", at("uoff", 0, 8), at("i16"))
     vts(at("b16", 0, 16), at("a16", 0, 16), 15, None, ALU.bitwise_and)
-    vset(at("zer"), 0.0)
-    for b in range(4):
-        vset(at("pr", C * b + A, C * b + C), 0.0)
     vts(at("e0"), at("b16", 0, 16), 0.0, -4 * KEEP, ALU.is_equal, ALU.mult)
     vts(at("e1"), at("b16", 0, 16), 1.0, KEEP, ALU.is_equal, ALU.mult)
     copy("V", at("cdo", 0, 40), at("cdi"))
-    vtt(at("hk", 0, 16), at("e0"), at("e1"), ALU.add)
-    for a, b in ((16, 32), (32, 64), (64, 128), (128, 256)):
-        copy("VS", at("hk", a, b), at("hk", 0, b - a))
+    vtt(at("hk0", 0, 16), at("e0"), at("e1"), ALU.add)
+    iota(at("a20"), [[0, 20]], 0, 1, small=False)
+    for j, mask in enumerate((15, 3)):
+        vts(at("b20", 20 * j, 20 * j + 20), at("a20"), mask, None, ALU.bitwise_and)
+    copy("V", at("rep", 0, 40), at("b20"))
+    copy("VS", at("hk", 0, A), by(at("hk0", 0, 16), at("rep", 0, A // 16)))
     copy("VS", at("c1"), by(at("iot"), at("cdo", 0, 20)))
-    quant("qu", "su", 0, 128, "us", 0)
+    quant("qu", "su", 0, at("us"))
     for b in range(4):
-        diag_b = at("ebig", 3 - b, 515 - b)
-        _add(pl, {"V": CFG["f"] * (12 + 0.22 * 512)},
-             lambda e, b=b, t=diag_b: V.quantize_mx(T.qe[:, 128 * b:128 * b + 128], T.se[:, 128 * b:128 * b + 128], t["ap"]),
-             keys(diag_b), keys(at("qe", 128 * b, 128 * b + 128), at("se", 128 * b, 128 * b + 128)))
+        quant("qe", "se", 128 * b, at("ebig", 3 - b, 515 - b))
     picked = by(at("qu"), at("uoff", 0, 8), words=True)
     call("V", lambda e: V.tensor_copy(T.qup[:].bitcast(dt.uint32), picked["ap"]), at("qup"), [picked])
     copy("VS", at("sup"), by(at("su"), at("uoff", 0, 8)))
@@ -400,24 +535,28 @@ def rank_program(g, core, T, topo):
     vset(at("w1", 1, 2), 3.0 - SH)
     copy("V", at("cdf", 3, 2 * C, 2), at("c1", 1, C))
     vset(at("cdf", 1, 2), 3.0 - SH)
-    for j, c0 in enumerate([SH + 0.5, SH, SH - Z, H, 2 * C]):
+    for j, c0 in enumerate([SH + 0.5, SH, SH - Z, C // 2, 2 * C]):
         act(col(j), at("e1", 0, 1), ACT.Identity, bias=float(c0 - KEEP))
-    cp_pair, cp_ptr, cp_base, cp_place, cp_slot = [col(j) for j in range(5)]
+    cp_pair, cp_ptr, cp_base, cp_place, cp_slot, cp_four = [col(j) for j in range(6)]
+    iota(at("a16", 16, 20), [[-4, 4]], 128, 1, small=False)
+    vts(at("b16", 16, 20), at("a16", 16, 20), 12, None, ALU.bitwise_and)
+    vts(at("e4", 0, 4), at("b16", 16, 20), 0.0, -4 * KEEP, ALU.is_equal, ALU.mult)
+    vts(at("e4", 4, 8), at("b16", 16, 20), 12.0, KEEP, ALU.is_equal, ALU.mult)
+    vtt(at("hk0", 16, 20), at("e4", 0, 4), at("e4", 4, 8), ALU.add)
+    copy("VS", at("hk4", 0, H), by(at("hk0", 16, 20), at("rep", 20, 20 + H // 16)))
+    vts(at("e4", 8, 9), at("b20", 20, 21), 0.25, float(SH - Z - KEEP), ALU.mult, ALU.add)
+    vtt(cp_four, at("e4", 8, 9), at("e4", 4, 5), ALU.add)
 
     low = CFG["low"]
     runs = [(a, a + 32) for a in range(0, low, 32)] + [(a, a + 64) for a in range(low, C, 64)]
-    fills = [(a, min(C, a + CFG["fill"])) for a in range(0, C, CFG["fill"])]
-
-    def off(d, a, b):
-        return at("off", 32 * d + a // 16, 32 * d + b // 16)
-
-    tile = "xs"
+    tile, begins, extra = "xs", [], []
     for r in range(R + 1):
+        begins.append(len(pl["ops"]))
         qx, sx = "qx%d" % r, "sx%d" % r
         side = ("qup", "sup", 0, 128) if r < R else ("qv", "sv", 0, 128)
         for k, (a, b) in enumerate(halves):
-            quant(qx, sx, a, b, tile, a)
-            mm(4 + k, side, (qx, sx, a, b))
+            quant(qx, sx, a, at(tile, 4 * a, 4 * b))
+            mm(sb[k], side, (qx, sx, a, b))
         if r == R:
             break
         dst, src = T.cores[(rank + STEP[r]) % n_ranks], T.cores[(rank - STEP[r]) % n_ranks]
@@ -427,10 +566,10 @@ def rank_program(g, core, T, topo):
         arrives(src, "ar%d" % r, [send(dst, at(lq, H, C), at(qx, H, C), "ar%d" % r, codes=True)], [at(lq, H, C)])
 
         for k, (a, b) in enumerate(halves):
-            copy("VS", at("sc", a, b), bank(4 + k, H))
+            copy("VS", at("sc", a, b), bank(sb[k], b - a))
             if "V" in CFG["cand"][2 * k:2 * k + 2]:
-                mm(6 + k, side, (qx, sx, a, b))
-                copy("VS", at("sc2", a, b), bank(6 + k, H))
+                mm(db[k], side, (qx, sx, a, b))
+                copy("VS", at("sc2", a, b), bank(db[k], b - a))
         for k, (a, b) in enumerate(halves):
             for c in range(2):
                 theirs = by(at("sc", 0, b), at("cdo", (C * c + a) // 16, (C * c + b) // 16))
@@ -438,32 +577,42 @@ def rank_program(g, core, T, topo):
                 if CFG["cand"][2 * k + c] == "V":
                     vtt(d, theirs, at("sc2", a, b), ALU.subtract)
                 else:
-                    copy("S", at("gc", C * c + a, C * c + b), theirs)
-                    vtt(d, at("gc", C * c + a, C * c + b), bank(4 + k, H), ALU.subtract)
+                    copy("VS", at("gc", C * c + a, C * c + b), theirs)
+                    vtt(d, at("gc", C * c + a, C * c + b), bank(sb[k], b - a), ALU.subtract)
                 act(at("aa", C * c + a, C * c + b), d, ACT.Abs)
             vtt(at("flg", 2 * a + 1, 2 * b, 2), at("aa", C + a, C + b), at("aa", a, b), ALU.is_lt)
-            scan(at("w1", 2 * (Z + a), 2 * (Z + b)), at("flg", 2 * a, 2 * b), at("cdf", 2 * a, 2 * b), 0.0, ALU.mult, ALU.add)
-            wrap(at("hb", a, b), at("w1", 2 * (Z + a) + 1, 2 * (Z + b), 2))
+            scan(win(0, Z + a, Z + b), at("flg", 2 * a, 2 * b), at("cdf", 2 * a, 2 * b), 0.0, ALU.mult, ALU.add)
+            base = at("w1", 2 * (Z + a) + 1, 2 * (Z + b), 2)
+            wrap(at("hb", a, b), base)
             vts(off(0, a, b), held("hb", a, b), cp_pair, 2.0, ALU.add, ALU.mult)
-        vts(at(ob, 0, 20), held("hb", 0, C), cp_base, None, ALU.add)
-        arrives(src, "ab%d" % r, [send(dst, at(lb, 0, 20), at(ob, 0, 20), "ab%d" % r)], [at(lb, 0, 20)])
+            wrap(at("h4", a, b), base, "hk4")
+            vts(at(ob, a // 4, b // 4), held("h4", a, b, 4), cp_four, 4.0, ALU.add, ALU.mult)
+            if k == 1:
+                vts(at(ob, C // 4, C // 4 + C // 16), held("hb", 0, C), cp_base, None, ALU.add)
+            lo, hi, sem = a // 4, b // 4 + k * C // 16, "a%s%d" % ("cb"[k], r)
+            arrives(src, sem, [send(dst, at(lb, lo, hi), at(ob, lo, hi), sem)], [at(lb, lo, hi)])
 
         if r == 0:
-            queued[0] = 0.0
-            landed = [len(pl["ops"]) - 1]
-            load("Y", at("wq"), T.wc[:], "l_wc", after=landed, codes=True)
+            queued[0], n0 = 0.0, len(pl["ops"])
+            load("Y", at("wq"), T.wc[:], "l_wc", after=[n0 - 1], codes=True)
             load("Y", at("wsc"), T.ws[:], "l_ws")
             load("Y", at("vs"), T.v[:], "l_v")
-            quant("qv", "sv", 0, 128, "vs", 0)
+            quant("qv", "sv", 0, at("vs"))
+            for d in range(3, 6):
+                iota(win(d, 0, Z), [[1, Z]], -SH, 0, behind=last[2:3])
+            iota(at("lab", 0, Z), [[0, 4], [C, 4]], -LAB, 0, behind=last[2:3])
+            iota(at("zer"), [[0, 4 * C]], 0, 0, behind=last[-1:])
+            for b in range(4):
+                iota(at("pr", C * b + A, C * b + C), [[0, C - A]], 0, 0, behind=last[-1:])
+            extra += range(n0, len(pl["ops"]))
 
-        wins = ["w1", "w2", "wa", "wb", "wc2", "wd", "we"]
         for d in range(6):
-            for a, b, e in CFG["parts"] if d < 5 else [(low, C, "VS")]:
-                copy(e, at(wins[d + 1], Z + a, Z + b), by(at(wins[d], 0, (2 if d == 0 else 1) * (Z + b)), off(d, a, b)))
-                wrap(at("hh", C * d + a, C * d + b), at(wins[d + 1], Z + a, Z + b))
+            for a, b in CFG["parts"] if d < 5 else [(low, C)]:
+                copy("VS", win(d + 1, Z + a, Z + b), by(win(d, 0, Z + b), off(d, a, b)))
+                wrap(at("hh", C * d + a, C * d + b), win(d + 1, Z + a, Z + b))
                 vts(off(d + 1, a, b), held("hh", C * d + a, C * d + b), cp_ptr, None, ALU.add)
         for a, b in runs:
-            copy(CFG["erun"], at("lab", Z + a, Z + b), by(at("lab", 0, Z + a), off(5 if a < low else 6, a, b)))
+            copy("VS", at("lab", Z + a, Z + b), by(at("lab", 0, Z + a), off(5 if a < low else 6, a, b)))
 
         for a, b in CFG["pieces"]:
             lab = at("lab", Z + a, Z + b)
@@ -479,8 +628,8 @@ def rank_program(g, core, T, topo):
                         return S.activation(flag["ap"], lab["ap"], ACT.Relu, bias=end[0], scale=end[1])
                     return V.tensor_scalar(flag["ap"], lab["ap"], float(C * d - LAB), None, ALU.is_equal)
                 call("VS" if end else "V", flags, flag, [lab])
-        scan(at("cum"), at("ef"), at("zer"), -(H + 1.0), ALU.add, ALU.add)
-        for a, b in halves:
+        scan(at("cum"), at("ef"), at("zer"), -(C // 2 + 1.0), ALU.add, ALU.add)
+        for a, b in CFG["plparts"]:
             copy("VS", at("pl", a, b), by(at("cum"), at("qq", a // 16, b // 16)))
             wrap(at("hp", a, b), at("pl", a, b))
         vts(at("plo", 0, 20), held("hp", 0, C), cp_place, None, ALU.add)
@@ -491,84 +640,79 @@ def rank_program(g, core, T, topo):
 
         for b in range(4):
             if CFG["state"][b] == "V":
-                unpack(b, 6 + b % 2, (qx, sx, 0, C))
-                for a, e in fills:
-                    copy("S", at("fo", C * b + a, C * b + e), bank(6 + b % 2, e, a))
+                unpack(b, fb[b], (qx, sx, 0, C))
+                for a, e in halves:
+                    copy("VS", at("fo", C * b + a, C * b + e), bank(fb[b], e, a))
 
-        def mv(b, d, a=0, e=C):
-            return at("mv", 4 * C * b + C * d + a, 4 * C * b + C * d + e)
-
-        for b in range(4):
-            vts(at("lb4", 20 * b, 20 * b + 20), at(lb, 0, 20), 4.0, float(b), ALU.mult, ALU.add)
-        for k, (a, e) in enumerate(fills):
-            n, one, two = e - a, 4 * (k % 2), 4 * (1 - k % 2)
+        for k, (a, e) in enumerate(halves):
+            n = e - a
             for b in range(4):
-                unpack(b, one + b, (lq, ls, a, e))
-                copy(CFG["eft"], at("ft", 4 * a + b, 4 * e, 4), bank(one + b, n))
-            quant(qp, sp, a, e, "ft", a)
+                unpack(b, 4 * k + b, (lq, ls, a, e))
+                copy("VS", at("ft", 4 * a + b, 4 * e, 4), bank(4 * k + b, n))
+            quant(qp, sp, 2 * a + n, at("ft", 4 * a, 4 * e))
+            for lo in range(a, e, n // CFG["grun"]):
+                hi = lo + n // CFG["grun"]
+                copy("VS", at("gt", 4 * lo, 4 * hi), by(at("ft", 0, 4 * hi), at(lb, lo // 4, hi // 4)))
             for b in range(4):
-                copy(CFG["egt"], at("gt", 4 * a + b, 4 * e, 4), by(at("ft", 0, 4 * e), at("lb4", 20 * b + a // 16, 20 * b + e // 16)))
-                vtt(at("pt", 4 * a + b, 4 * e, 4), bank(one + b, n), at("gt", 4 * a + b, 4 * e, 4), ALU.subtract)
-            quant(qp, sp, C + a, C + e, "gt", a)
-            quant(qp, sp, 2 * C + a, 2 * C + e, "pt", a)
-        for k, (a, e) in enumerate(fills):
-            n, one, two = e - a, 4 * (k % 2), 4 * (1 - k % 2)
+                vtt(at("pt", 4 * a + b, 4 * e, 4), bank(4 * k + b, n), at("gt", 4 * a + b, 4 * e, 4), ALU.subtract)
+            quant(qp, sp, 2 * C + a, at("gt", 4 * a, 4 * e))
+            quant(qp, sp, 2 * a, at("pt", 4 * a, 4 * e))
             for b in range(4):
-                unpack(b, one + b, (qp, sp, C + a, C + e), True, False)
-                unpack(b, one + b, (qp, sp, 2 * C + a, 2 * C + e), False, True)
-                copy(CFG["em"], mv(b, 1, a, e), bank(one + b, n))
-                unpack(b, one + b, (qp, sp, 2 * C + a, 2 * C + e))
+                unpack(b, 4 * k + b, (qp, sp, 2 * C + a, 2 * C + e), True, False)
+                unpack(b, 4 * k + b, (qp, sp, 2 * a, 2 * a + n), False, True)
+                copy("VS", mv(b, 1, a, e), bank(4 * k + b, n))
+                unpack(b, 4 * k + b, (qp, sp, 2 * a, 2 * e))
                 if "V" in (CFG["steps"][2][b], CFG["steps"][3][b]):
-                    copy(CFG["em"], at("md", C * b + a, C * b + e), bank(one + b, n))
-                for d in (2, 3):
-                    base = by(mv(b, d - 1, 0, e), at(lb, a // 16, e // 16))
+                    copy("VS", at("md", C * b + a, C * b + e), bank(4 * k + b, n))
+        for b in range(4):
+            for d in (2, 3):
+                for a, e in CFG["sparts"]:
+                    base = by(mv(b, d - 1, 0, e), at(lb, C // 4 + a // 16, C // 4 + e // 16))
                     if CFG["steps"][d][b] == "V":
                         vtt(mv(b, d, a, e), base, at("md", C * b + a, C * b + e), ALU.add)
-                    else:
-                        gb = at("gb", C * (4 * (d - 2) + b) + a, C * (4 * (d - 2) + b) + e)
-                        copy("S", gb, base)
-                        vtt(mv(b, d, a, e), bank(one + b, n), gb, ALU.add)
-        for b in range(4):
-            unpack(b, CFG["b0"][b], (qp, sp, 0, C))
-            for a, e in fills:
-                copy(CFG["em"], mv(b, 0, a, e), bank(CFG["b0"][b], e, a))
+                        continue
+                    g0 = C * (4 * (d - 2) + b)
+                    copy("VS", at("gb", g0 + a, g0 + e), base)
+                    for k, (lo, hi) in enumerate(halves):
+                        if a <= lo < e:
+                            vtt(mv(b, d, lo, hi), bank(4 * k + b, hi - lo), at("gb", g0 + lo, g0 + hi), ALU.add)
+                if d == 2:
+                    for k, (a, e) in enumerate(halves):
+                        copy("VS", mv(b, 0, a, e), bank(4 * k + b, 2 * (e - a), e - a))
 
+        pl["cuts"].append(len(pl["ops"]))
         for a, e in CFG["mparts"]:
             for b in range(4):
                 copy("VS", at("mt", 4 * a + b, 4 * e, 4), by(at("mv", 4 * C * b, 4 * C * (b + 1)), at(ll, a // 16, e // 16)))
-            quant(qm, sm, a, e, "mt", a)
+        for a in (0, A // 2):
+            quant(qm, sm, a, at("mt", 4 * a, 4 * a + 2 * A))
         for b in range(4):
             if CFG["state"][b] == "S":
-                unpack(b, 6 + b % 2, (qx, sx, 0, C))
+                unpack(b, fb[b], (qx, sx, 0, C))
         for (a, e), banks in CFG["lparts"]:
             for b in CFG["lorder"]:
                 mm(banks[b], ("wq", "wsc", 128 * b, 128 * b + 128), (qm, sm, a, e))
                 copy("VS", at("pr", C * b + a, C * b + e), bank(banks[b], e - a), scale=0.015625)
-        for a, e in CFG["xparts"]:
+        for a, e in halves if CFG["xsplit"] else [(0, C)]:
             for b in range(4):
                 made = by(at("pr", C * b, C * b + C), at("plo", a // 16, e // 16))
                 out = at("xn", 4 * a + b, 4 * e, 4)
                 if CFG["state"][b] == "V":
                     vtt(out, made, at("fo", C * b + a, C * b + e), ALU.add)
                 else:
-                    copy("S", at("gx", C * b + a, C * b + e), made)
-                    vtt(out, bank(6 + b % 2, e, a), at("gx", C * b + a, C * b + e), ALU.add)
+                    copy("VS", at("gx", C * b + a, C * b + e), made)
+                    vtt(out, bank(fb[b], e, a), at("gx", C * b + a, C * b + e), ALU.add)
         tile = "xn"
 
-    outs = {"S": 0, "Y": 0}
-
-    def store(eng, out, in_, reads):
-        outs[eng] += 16
-        q = S if eng == "S" else g.sync
-        _add(pl, {eng: 60.0}, lambda e: q.dma_start(out, in_), keys(reads), [], kind="dma", sem="out" + eng, lag=CFG["load"] + 800.0)
+    cuts, pl["begin"] = pl["cuts"], begins[0]
+    head = [k for k in range(begins[0], cuts[0]) if k not in extra]
+    pl["like"].update({k: begins[1] - cuts[0] + i for i, k in enumerate(head)})
+    pl["like"].update({k: (k - cuts[0]) % (cuts[1] - cuts[0]) for k in range(cuts[0], len(pl["ops"]))})
 
     for k, (a, b) in enumerate(halves):
-        copy("SV"[k], at("ys", a, b), bank(4 + k, H))
-    store("Y", T.oc[:], T[qx][:].bitcast(dt.uint8), at(qx))
-    store("S", T.y[:], T.ys[:], at("ys"))
+        store("Y", T.oc[:, 4 * a:4 * b], T[qx][:, a:b].bitcast(dt.uint8), at(qx, a, b))
+        copy("VS", at("ys", a, b), bank(sb[k], b - a))
+        store("YS"[k], T.y[:, a:b], T.ys[:, a:b], at("ys", a, b))
     for k in range(4):
-        store("Y" if k < 2 else "S", T.osc[4 * k:4 * k + 4, :], T[sx][32 * k:32 * k + 4, :], at(sx))
-    _emit(pl, g, T)
-    S.wait_ge(T.sem.outS, outs["S"])
-    g.sync.wait_ge(T.sem.outY, outs["Y"])
-    g.wait_ge(T.sem.sent, sent[0])
+        store("Y" if k < 2 else "S", T.osc[4 * k:4 * k + 4, :], T[sx][32 * k:32 * k + 4, :], at(sx), 16)
+    return pl

@@ -11,25 +11,28 @@ SH = PW // 2
 KEEP = 1280.0
 LAB = 5 * C
 BANK = 512
+HALVES = [(0, C // 2), (C // 2, C)]
 
 CFG = {
-    "mid": 160,
-    "low": 128,
-    "parts": [(0, 160), (160, 320)],
+    "mid": 160, "final": 192,
+    "loads": "uacb",
+    "jumps": [(1, 1, HALVES, HALVES), (2, 1, HALVES, HALVES), (3, 2, HALVES, []), (5, 3, HALVES, HALVES), (8, 8, HALVES, HALVES),
+              (16, 16, [(32, 192), (192, 320)], [(32, 192), (192, 320)]), (32, 32, [(128, 192), (192, 320)], [(128, 192), (192, 320)])],
+    "runs": ([(0, 16, 16, "lab0", "lab0", 0), (0, 32, 16, "lab0", "lab", 16)] + [(a, a + 32, 32, "lab", "lab", a) for a in (32, 64, 96)]
+             + [(a, a + 64, 64, "lab", "lab", a) for a in (128, 192, 256)]),
     "pieces": [(0, 192), (192, 320)],
     "cand": "VSVS",
     "steps": {2: "VSSS", 3: "VSSS"},
-    "state": "VVSS",
-    "sparts": [(0, 320)], "mparts": [(0, 128), (128, 256)], "grun": 2, "plparts": [(0, 160), (160, 320)], "xsplit": True,
-    "lparts": [((0, 128), [0, 1, 2, 3]), ((128, 256), [0, 1, 4, 5])], "lorder": [2, 0, 3, 1],
-    "sb": [4, 5], "db": [0, 1], "fb": [6, 7, 6, 7],
-    "passes": 3, "ahead": 60.0, "over": 400.0, "give": 300.0,
-    "tries": [200000, 60000, 20000], "heat": 15.0, "mean": 0.15,
+    "state": "VSSS",
+    "lparts": [((0, 128), [0, 1, 2, 3]), ((128, 256), [4, 5, 6, 7])], "lorder": [2, 3, 1, 0],
+    "sb": [0, 4], "db": [5, 7], "fb": [6, 1, 2, 3],
+    "passes": 3, "ahead": 60.0, "over": 100.0, "give": 100.0,
+    "tries": [90000, 100000, 30000], "seeds": [6, 2, 1], "heat": 30.0, "mean": 0.25,
 }
-PACES = [{"f": 1.05, "wake": 190.0, "g": 1.4, "sc": 3.8, "link": 1800.0, "rows": 480.0, "bw": 90.0, "load": 1500.0, "first": 1000.0,
-          "issue": 400.0},
-         {"f": 1.35, "wake": 120.0, "g": 1.7, "sc": 3.8, "link": 900.0, "rows": 280.0, "bw": 110.0, "load": 1000.0, "first": 1000.0,
-          "issue": 150.0}]
+PACES = [{"f": 1.0, "wake": 200.0, "g": 1.5, "sc": 3.8, "link": 1700.0, "rows": 450.0, "bw": 90.0, "load": 1400.0, "first": 1000.0,
+          "issue": 350.0},
+         {"f": 1.4, "wake": 170.0, "g": 1.85, "sc": 4.2, "link": 1200.0, "rows": 330.0, "bw": 110.0, "load": 1100.0, "first": 1000.0,
+          "issue": 220.0}]
 QUEUES = ["V", "S", "P", "G", "Y", "L", "in"]
 ORDER = []
 
@@ -38,6 +41,7 @@ def _sb(n, d):
     return ("sbuf", [128, n], d)
 
 
+JUMPS = len(CFG["jumps"])
 SCRATCH = {
     "xs": _sb(4 * C, "bfloat16"), "us": _sb(512, "bfloat16"), "vs": _sb(512, "bfloat16"),
     "wq": _sb(512, CODE), "wsc": _sb(512, "uint8"), "cdi": _sb(40, "int32"), "cdo": _sb(48, "uint16"),
@@ -47,13 +51,13 @@ SCRATCH = {
     "a16": _sb(24, "int32"), "b16": _sb(24, "int32"), "e0": _sb(16, "float32"), "e1": _sb(16, "float32"), "e4": _sb(16, "float32"),
     "cps": _sb(16, "float32"), "i16": _sb(8, "float32"), "a20": _sb(20, "int32"), "b20": _sb(40, "int32"), "rep": _sb(40, "uint16"),
     "hk0": _sb(32, "bfloat16"),
-    "hk": _sb(C, "bfloat16"), "hk4": _sb(192, "bfloat16"), "iot": _sb(C, "bfloat16"), "col16": _sb(C, H16),
-    "c1": _sb(C, "bfloat16"), "cdf": _sb(2 * C, H16), "flg": _sb(2 * C, "bfloat16"), "zer": _sb(4 * C, "bfloat16"),
+    "hk": _sb(A, "bfloat16"), "hk4": _sb(192, "bfloat16"), "iot": _sb(C, "bfloat16"), "col16": _sb(C, H16),
+    "c1": _sb(C, "bfloat16"), "cdf": _sb(2 * C, H16), "flg": _sb(2 * C, "bfloat16"),
     "sc": _sb(C, "float32"), "sc2": _sb(C, "float32"), "gc": _sb(2 * C, "float32"), "dd": _sb(2 * C, "float32"), "aa": _sb(2 * C, "float32"),
-    "w1": _sb(2 * PW, "bfloat16"), "ww": _sb(6 * PW, "bfloat16"),
-    "lab": _sb(PW, "bfloat16"), "hb": _sb(C, H16), "h4": _sb(C, H16), "hh": _sb(6 * C, H16), "li": _sb(C, H16), "hl": _sb(C, H16),
-    "hp": _sb(C, H16), "h2": _sb(A, H16), "off": _sb(7 * 32, "uint16"), "qq": _sb(32, "uint16"),
-    "ef": _sb(4 * C, "bfloat16"), "cum": _sb(4 * C, "bfloat16"), "pl": _sb(C, "bfloat16"), "plo": _sb(32, "uint16"),
+    "w1": _sb(2 * PW, "bfloat16"), "w2": _sb(2 * PW, "bfloat16"), "ww": _sb(JUMPS * PW, "bfloat16"), "lab0": _sb(2 * Z, "bfloat16"),
+    "lab": _sb(PW, "bfloat16"), "hb": _sb(C, H16), "h4": _sb(C, H16), "hh": _sb(JUMPS * C, H16), "li": _sb(C, H16), "hl": _sb(C, H16),
+    "hp": _sb(C, H16), "h2": _sb(A, H16), "off": _sb((JUMPS + 1) * 32, "uint16"), "qq": _sb(32, "uint16"),
+    "ef": _sb(4 * C, "bfloat16"), "cum": _sb(2 * C + 1, "bfloat16"), "pl": _sb(C, "bfloat16"), "plo": _sb(32, "uint16"),
     "srt": _sb(C, "float32"),
     "fo": _sb(4 * C, "bfloat16"), "md": _sb(4 * C, "bfloat16"), "mv": _sb(16 * C, "bfloat16"), "gb": _sb(8 * C, "bfloat16"),
     "pr": _sb(4 * C, "float32"), "gx": _sb(4 * C, "float32"), "ys": _sb(C, "float32"),
@@ -96,7 +100,7 @@ def _add(pl, costs, fn, reads, writes, kind="c", sem=None, total=0, lag=0.0, aft
         kept = []
         for j, c, wrote in pl["seen"].get(name, []):
             if c & cols:
-                deps.add(j)
+                (shared if kind == "c" == ops[j]["kind"] else deps).add(j)
             if c & ~cols:
                 kept.append((j, c & ~cols, wrote))
         pl["seen"][name] = kept
@@ -184,85 +188,101 @@ def _first_order(pl):
     return best[1], best[2]
 
 
-def _mend(plans, order, eng, lo, hi, tries):
-    n = hi - lo
+def _mend(plans, order, eng, lo, hi, tries, start):
+    n, ops = hi - lo, plans[0]["ops"]
     row = [k - lo for k in order]
     on = [QUEUES.index(eng[k]) for k in range(lo, hi)]
-    either = [len(plans[0]["ops"][k]["costs"]) > 1 for k in range(lo, hi)]
-    paces = []
-    for pl in plans:
-        pred, succ = _edges(pl)
-        before = [[(j - lo, d, j in pl["ops"][k]["shared"]) for j, d in pred[k] if j >= lo] for k in range(lo, hi)]
-        later = [set(j - lo for j, _ in succ[k] if j < hi) for k in range(lo, hi)]
-        costs = [[pl["ops"][k]["costs"].get(q, 0.0) for q in QUEUES] for k in range(lo, hi)]
-        last = [(k, max(pl["ops"][lo + k]["lag"], 0.0) + pl["wake"]) for k in range(n) if not later[k]]
-        paces.append((before, costs, last))
-    earlier = [set(x[0] for x in p) for p in paces[0][0]]
+    either = [len(ops[k]["costs"]) > 1 for k in range(lo, hi)]
+    pred, succ = _edges(plans[0])
+    later = [set(j - lo for j, _ in succ[k] if j < hi) for k in range(lo, hi)]
+    earlier = [set(j - lo for j, _ in pred[k] if j >= lo) for k in range(lo, hi)]
+    hard = [set(j - lo for j in ops[k]["deps"] if j >= lo) for k in range(lo, hi)]
+    above = []
+    for k in range(n):
+        above.append(set().union(*[above[j] | {j} for j in hard[k] if ops[lo + j]["lag"] >= 0]))
+    hard = [[j for j in sorted(h) if not any(j in above[m] for m in h if ops[lo + m]["lag"] >= 0)] for h in hard]
+    soft = [[j - lo for j in sorted(ops[k]["shared"]) if j >= lo and j - lo not in above[k - lo]] for k in range(lo, hi)]
+    tied = [[j - lo for j in ops[k]["behind"] if j >= lo] for k in range(lo, hi)]
+    (c0, d0), (c1, d1) = [([[pl["ops"][k]["costs"].get(q, 0.0) for q in QUEUES] for k in range(lo, hi)],
+                           [pl["ops"][k]["lag"] + pl["wake"] for k in range(lo, hi)]) for pl in plans]
+    last = [(k, max(d0[k], plans[0]["wake"]) - d0[k], max(d1[k], plans[1]["wake"]) - d1[k]) for k in range(n) if not later[k]]
     arrival = QUEUES.index("in")
-
     mean = CFG["mean"] / n
 
-    def span(ends, p0):
-        latest, missing = [-1] * len(QUEUES), arrival
+    def span(seen, p0):
+        a, b = seen[0][:], seen[1][:]
+        fa, fb = [0.0] * len(QUEUES), [0.0] * len(QUEUES)
+        met, missing = [False] * len(QUEUES), arrival
         for i in range(p0 - 1, -1, -1):
-            q = on[row[i]]
-            if latest[q] < 0 and q != arrival:
-                latest[q] = row[i]
+            k = row[i]
+            q = on[k]
+            if not met[q] and q != arrival:
+                met[q], fa[q], fb[q] = True, a[k] - d0[k], b[k] - d1[k]
                 missing -= 1
                 if not missing:
                     break
-        rest, total, new = row[p0:], 0.0, []
-        for (before, costs, last), old in zip(paces, ends):
-            end = old[:]
-            free = [end[k] if k >= 0 else 0.0 for k in latest]
-            for k in rest:
-                q = on[k]
-                t = free[q]
-                for j, delay, soft in before[k]:
-                    x = end[j] + delay
-                    if x > t and not (soft and on[j] == q):
-                        t = x
-                end[k] = free[q] = t + costs[k][q]
-                free[arrival] = 0.0
-            total += max([end[k] + t for k, t in last]) + mean * sum(end)
-            new.append(end)
-        return total / len(paces), new
+        for k in row[p0:]:
+            q = on[k]
+            s, t = fa[q], fb[q]
+            for j in hard[k]:
+                if a[j] > s:
+                    s = a[j]
+                if b[j] > t:
+                    t = b[j]
+            if soft[k]:
+                for j in soft[k]:
+                    if on[j] != q:
+                        if a[j] > s:
+                            s = a[j]
+                        if b[j] > t:
+                            t = b[j]
+            if q > 2:
+                for j in tied[k]:
+                    s, t = max(s, a[j] - d0[j]), max(t, b[j] - d1[j])
+                if q == arrival:
+                    a[k], b[k] = s + d0[k], t + d1[k]
+                    continue
+            fa[q] = s = s + c0[k][q]
+            fb[q] = t = t + c1[k][q]
+            a[k] = s + d0[k]
+            b[k] = t + d1[k]
+        return (max([a[k] + x for k, x, _ in last]) + max([b[k] + x for k, _, x in last]) + mean * (sum(a) + sum(b))) / 2, (a, b)
 
-    seed = [1]
+    seed, far = [start], (1, 1, 2, 3, 5, 8) + ((13, 25) if lo == 0 else ())
 
     def draw(m):
         seed[0] = (seed[0] * 1103515245 + 12345) % 2147483648
         return (seed[0] >> 8) % m
 
-    now, ends = span([[0.0] * n for _ in paces], 0)
+    now, seen = span([[0.0] * n, [0.0] * n], 0)
     best = (now, row[:], on[:])
     for it in range(tries):
         p = draw(n)
         k = row[p]
         was = on[k]
-        if was == arrival:
+        if was > 1 and (was == arrival or draw(2)):
             continue
-        way, steps = 2 * draw(2) - 1, (1, 1, 2, 3, 5, 8)[draw(6)]
+        way, steps = 2 * draw(2) - 1, far[draw(len(far))]
         if either[k] and draw(10) < 3:
             on[k] = 1 - was
             steps *= draw(2)
-        q, stop = p, (earlier[k] if way < 0 else later[k])
+        q, to, stop = p, p, (earlier[k] if way < 0 else later[k])
         while steps and 0 <= q + way < n and row[q + way] not in stop:
             q += way
             if on[row[q]] == on[k]:
-                steps -= 1
-        if q == p and on[k] == was:
+                steps, to = steps - 1, q
+        if to == p and on[k] == was:
             continue
-        row.insert(q, row.pop(p))
-        s, new = span(ends, min(p, q))
+        row.insert(to, row.pop(p))
+        s, new = span(seen, min(p, to))
         if s <= now or draw(4096) < 4096 * math.exp((now - s) / (CFG["heat"] * (1 - it / tries) + 1)):
-            now, ends = s, new
+            now, seen = s, new
             if s < best[0]:
                 best = (s, row[:], on[:])
             if it % 50 == 0:
-                row.sort(key=lambda k: round(ends[0][k] - paces[0][1][k][on[k]], 3))
+                row.sort(key=lambda k: round(seen[0][k] - d0[k] - c0[k][on[k]], 3))
         else:
-            row.insert(p, row.pop(q))
+            row.insert(p, row.pop(to))
             on[k] = was
     return [k + lo for k in best[1]], {lo + k: QUEUES[q] for k, q in enumerate(best[2])}
 
@@ -271,7 +291,7 @@ def _order(plans):
     order, eng = _first_order(plans[0])
     cuts, n = plans[0]["cuts"], len(plans[0]["ops"])
     like, begin = plans[0]["like"], plans[0]["begin"]
-    row, on = _mend(plans, [k for k in order if cuts[0] <= k < cuts[1]], eng, cuts[0], cuts[1], CFG["tries"][0])
+    row, on = _mend(plans, [k for k in order if cuts[0] <= k < cuts[1]], eng, cuts[0], cuts[1], CFG["tries"][0], CFG["seeds"][0])
     place = {k - cuts[0]: i for i, k in enumerate(row)}
     rows = []
     for s, (lo, hi) in enumerate(zip([0] + cuts, cuts + [n])):
@@ -289,7 +309,8 @@ def _order(plans):
             done.add(k)
             mine.append(k)
         if s in (0, len(cuts)):
-            mine, moved = _mend(plans, mine, eng, lo, hi, CFG["tries"][1 if s == 0 else 2])
+            i = 1 if s == 0 else 2
+            mine, moved = _mend(plans, mine, eng, lo, hi, CFG["tries"][i], CFG["seeds"][i])
             eng.update(moved)
         rows += mine
     return rows, eng
@@ -401,7 +422,7 @@ def _plan(g, core, rank, T, topo, pace):
         return cyc * max(64, k * out["n"])
 
     def call(engs, fn, out, ins, k=None):
-        return _add(pl, {e: cost(e, out, ins, k) for e in engs}, fn, keys(*ins), keys(out))
+        return _add(pl, {e: cost(e, out, ins, k) for e in engs}, fn, keys(*ins) + keys(out)[1:], keys(out)[:1])
 
     def copy(engs, out, in_, scale=None):
         def fn(e):
@@ -486,19 +507,37 @@ def _plan(g, core, rank, T, topo, pace):
     def col(j):
         return at("cps", j, j + 1)
 
-    def win(d, a, b):
-        return at("w1", 2 * a, 2 * b) if d == 0 else at("ww", PW * (d - 1) + a, PW * (d - 1) + b)
+    steps = [1] + [w + o for w, o, _, _ in CFG["jumps"]]
+    paired = {w: "w%d" % w for w, o, _, _ in CFG["jumps"] if o == 1}
 
-    def off(d, a, b):
-        return at("off", 32 * d + a // 16, 32 * d + b // 16)
+    def win(k, a, b):
+        i = steps.index(k) - 1
+        return at(paired[k], 2 * a, 2 * b) if k in paired else at("ww", PW * i + a, PW * i + b)
+
+    def made(k, a, b):
+        return at(paired[k], 2 * a + 1, 2 * b, 2) if k in paired else win(k, a, b)
+
+    def off(k, a, b):
+        i = steps.index(k)
+        return at("off", 32 * i + a // 16, 32 * i + b // 16)
+
+    def fixed(k, behind=()):
+        low = CFG["jumps"][steps.index(k) - 1][2][0][0]
+        if k % 4 == 2:
+            iota(made(k, 0, Z), [[0, 4], [-2, 2], [1, 2]], 2 - SH, 0, behind=behind)
+            return
+        iota(made(k, 0, Z + low), [[1, Z + low]], (0, -1, 0, 1)[k % 4] - SH, 0, behind=behind)
+        if k % 2:
+            s = (0, 0, 0, 3)[k % 4]
+            vset(made(k, s, s + 1), float(3 - s - SH))
 
     def mv(b, d, a=0, e=C):
         return at("mv", 4 * C * b + C * d + a, 4 * C * b + C * d + e)
 
-    load("Y", at("cdi"), T.cd[:], "l_cd")
-    load("Y", at("us"), T.u[:], "l_u")
-    load("Y", at("xs", 0, 4 * H), T.x[:, 0:4 * H], "l_xa")
-    load("Y", at("xs", 4 * H, 4 * C), T.x[:, 4 * H:4 * C], "l_xb")
+    inputs = {"c": (at("cdi"), T.cd[:], "l_cd"), "u": (at("us"), T.u[:], "l_u"), "a": (at("xs", 0, 4 * H), T.x[:, 0:4 * H], "l_xa"),
+              "b": (at("xs", 4 * H, 4 * C), T.x[:, 4 * H:4 * C], "l_xb")}
+    for name in CFG["loads"]:
+        load("Y", *inputs[name])
 
     iota(at("i16"), [[16, 8]], 0, 0)
     iota(at("a16", 0, 16), [[1, 16]], 128, -1, small=False)
@@ -508,9 +547,10 @@ def _plan(g, core, rank, T, topo, pace):
     diag = at("ebig", 3, 515, 4)
     _add(pl, {"G": 170 * f + 256 * cyc},
          lambda e: g.affine_select(diag["ap"], T.ones[:], [[-1, 128]], ALU.is_equal, 0.0, 0, 1), keys(at("ones")), keys(diag))
-    iota(win(0, 0, Z), [[1, Z], [0, 2]], -SH - 1, 0)
-    iota(win(1, 0, Z), [[0, 4], [-2, 2], [1, 2]], 2 - SH, 0)
-    iota(win(2, 0, Z), [[1, Z]], -SH, 0)
+    iota(win(1, 0, Z), [[1, Z], [0, 2]], -SH - 1, 0)
+    vset(at("w2", 0, 2 * PW, 2), 0.0)
+    for k in steps[1:3]:
+        fixed(k)
     vts(at("col16"), at("iot"), float(3 * C + SH - Z), None, ALU.add)
     vset(at("flg", 0, 2 * C, 2), 0.0)
     copy("V", at("uoff", 0, 8), at("i16"))
@@ -523,7 +563,7 @@ def _plan(g, core, rank, T, topo, pace):
     for j, mask in enumerate((15, 3)):
         vts(at("b20", 20 * j, 20 * j + 20), at("a20"), mask, None, ALU.bitwise_and)
     copy("V", at("rep", 0, 40), at("b20"))
-    copy("VS", at("hk", 0, A), by(at("hk0", 0, 16), at("rep", 0, A // 16)))
+    copy("VS", at("hk"), by(at("hk0", 0, 16), at("rep", 0, A // 16)))
     copy("VS", at("c1"), by(at("iot"), at("cdo", 0, 20)))
     quant("qu", "su", 0, at("us"))
     for b in range(4):
@@ -535,9 +575,9 @@ def _plan(g, core, rank, T, topo, pace):
     vset(at("w1", 1, 2), 3.0 - SH)
     copy("V", at("cdf", 3, 2 * C, 2), at("c1", 1, C))
     vset(at("cdf", 1, 2), 3.0 - SH)
-    for j, c0 in enumerate([SH + 0.5, SH, SH - Z, C // 2, 2 * C]):
+    for j, c0 in enumerate([SH + 0.5, SH, SH - Z, C // 2 + 1, 2 * C]):
         act(col(j), at("e1", 0, 1), ACT.Identity, bias=float(c0 - KEEP))
-    cp_pair, cp_ptr, cp_base, cp_place, cp_slot, cp_four = [col(j) for j in range(6)]
+    cp_pair, cp_ptr, cp_base, cp_even, cp_slot, cp_four, cp_half, cp_place = [col(j) for j in range(8)]
     iota(at("a16", 16, 20), [[-4, 4]], 128, 1, small=False)
     vts(at("b16", 16, 20), at("a16", 16, 20), 12, None, ALU.bitwise_and)
     vts(at("e4", 0, 4), at("b16", 16, 20), 0.0, -4 * KEEP, ALU.is_equal, ALU.mult)
@@ -547,8 +587,6 @@ def _plan(g, core, rank, T, topo, pace):
     vts(at("e4", 8, 9), at("b20", 20, 21), 0.25, float(SH - Z - KEEP), ALU.mult, ALU.add)
     vtt(cp_four, at("e4", 8, 9), at("e4", 4, 5), ALU.add)
 
-    low = CFG["low"]
-    runs = [(a, a + 32) for a in range(0, low, 32)] + [(a, a + 64) for a in range(low, C, 64)]
     tile, begins, extra = "xs", [], []
     for r in range(R + 1):
         begins.append(len(pl["ops"]))
@@ -581,10 +619,10 @@ def _plan(g, core, rank, T, topo, pace):
                     vtt(d, at("gc", C * c + a, C * c + b), bank(sb[k], b - a), ALU.subtract)
                 act(at("aa", C * c + a, C * c + b), d, ACT.Abs)
             vtt(at("flg", 2 * a + 1, 2 * b, 2), at("aa", C + a, C + b), at("aa", a, b), ALU.is_lt)
-            scan(win(0, Z + a, Z + b), at("flg", 2 * a, 2 * b), at("cdf", 2 * a, 2 * b), 0.0, ALU.mult, ALU.add)
-            base = at("w1", 2 * (Z + a) + 1, 2 * (Z + b), 2)
+            scan(win(1, Z + a, Z + b), at("flg", 2 * a, 2 * b), at("cdf", 2 * a, 2 * b), 0.0, ALU.mult, ALU.add)
+            base = made(1, Z + a, Z + b)
             wrap(at("hb", a, b), base)
-            vts(off(0, a, b), held("hb", a, b), cp_pair, 2.0, ALU.add, ALU.mult)
+            vts(off(1, a, b), held("hb", a, b), cp_pair, 2.0, ALU.add, ALU.mult)
             wrap(at("h4", a, b), base, "hk4")
             vts(at(ob, a // 4, b // 4), held("h4", a, b, 4), cp_four, 4.0, ALU.add, ALU.mult)
             if k == 1:
@@ -598,27 +636,32 @@ def _plan(g, core, rank, T, topo, pace):
             load("Y", at("wsc"), T.ws[:], "l_ws")
             load("Y", at("vs"), T.v[:], "l_v")
             quant("qv", "sv", 0, at("vs"))
-            for d in range(3, 6):
-                iota(win(d, 0, Z), [[1, Z]], -SH, 0, behind=last[2:3])
-            iota(at("lab", 0, Z), [[0, 4], [C, 4]], -LAB, 0, behind=last[2:3])
-            iota(at("zer"), [[0, 4 * C]], 0, 0, behind=last[-1:])
+            for k in steps[3:-1]:
+                fixed(k, last[2:3])
+            for name in ("lab", "lab0"):
+                iota(at(name, 0, Z), [[0, 4], [C, 4]], -LAB, 0, behind=last[2:3])
+            vset(at("cum", 0, 1), -(C // 2 + 1.0))
+            vts(at("b16", 20, 21), at("a20", 0, 1), 1, None, ALU.bitwise_and)
+            vts(cp_half, at("b16", 20, 21), cp_slot, None, ALU.add)
+            vts(cp_place, at("b16", 20, 21), -1.0, cp_even, ALU.mult, ALU.add)
             for b in range(4):
                 iota(at("pr", C * b + A, C * b + C), [[0, C - A]], 0, 0, behind=last[-1:])
             extra += range(n0, len(pl["ops"]))
 
-        for d in range(6):
-            for a, b in CFG["parts"] if d < 5 else [(low, C)]:
-                copy("VS", win(d + 1, Z + a, Z + b), by(win(d, 0, Z + b), off(d, a, b)))
-                wrap(at("hh", C * d + a, C * d + b), win(d + 1, Z + a, Z + b))
-                vts(off(d + 1, a, b), held("hh", C * d + a, C * d + b), cp_ptr, None, ALU.add)
-        for a, b in runs:
-            copy("VS", at("lab", Z + a, Z + b), by(at("lab", 0, Z + a), off(5 if a < low else 6, a, b)))
+        for i, (w, o, parts, listed) in enumerate(CFG["jumps"]):
+            for a, b in parts:
+                copy("VS", made(w + o, Z + a, Z + b), by(win(w, 0, Z + b), off(o, a, b)))
+            for a, b in listed:
+                wrap(at("hh", C * i + a, C * i + b), made(w + o, Z + a, Z + b))
+                vts(off(w + o, a, b), held("hh", C * i + a, C * i + b), cp_ptr, None, ALU.add)
+        for a, b, k, known, into, end in CFG["runs"]:
+            copy("VS", at(into, Z + a, Z + b), by(at(known, 0, Z + end), off(k, a, b)))
 
         for a, b in CFG["pieces"]:
             lab = at("lab", Z + a, Z + b)
             scan(at("li", a, b), lab, at("col16", a, b), 0.0, ALU.min, ALU.add)
             wrap(at("hl", a, b), at("li", a, b))
-            vts(at("qq", a // 16, b // 16), held("hl", a, b), cp_slot, None, ALU.add)
+            vts(at("qq", a // 16, b // 16), held("hl", a, b), cp_half, 0.5, ALU.add, ALU.mult)
             for d in range(4):
                 flag = at("ef", C * d + a, C * d + b)
                 end = {0: (1.0 - LAB, -1.0), 3: (1.0 + LAB - 3 * C, 1.0)}.get(d)
@@ -628,9 +671,10 @@ def _plan(g, core, rank, T, topo, pace):
                         return S.activation(flag["ap"], lab["ap"], ACT.Relu, bias=end[0], scale=end[1])
                     return V.tensor_scalar(flag["ap"], lab["ap"], float(C * d - LAB), None, ALU.is_equal)
                 call("VS" if end else "V", flags, flag, [lab])
-        scan(at("cum"), at("ef"), at("zer"), -(C // 2 + 1.0), ALU.add, ALU.add)
-        for a, b in CFG["plparts"]:
+        scan(at("cum", 1, 2 * C + 1), at("ef", 0, 4 * C, 2), at("ef", 1, 4 * C, 2), -(C // 2 + 1.0), ALU.add, ALU.add)
+        for a, b in HALVES:
             copy("VS", at("pl", a, b), by(at("cum"), at("qq", a // 16, b // 16)))
+        for a, b in HALVES:
             wrap(at("hp", a, b), at("pl", a, b))
         vts(at("plo", 0, 20), held("hp", 0, C), cp_place, None, ALU.add)
         copy("V", by(at("srt"), at("plo", 0, 20)), at("li"))
@@ -650,9 +694,7 @@ def _plan(g, core, rank, T, topo, pace):
                 unpack(b, 4 * k + b, (lq, ls, a, e))
                 copy("VS", at("ft", 4 * a + b, 4 * e, 4), bank(4 * k + b, n))
             quant(qp, sp, 2 * a + n, at("ft", 4 * a, 4 * e))
-            for lo in range(a, e, n // CFG["grun"]):
-                hi = lo + n // CFG["grun"]
-                copy("VS", at("gt", 4 * lo, 4 * hi), by(at("ft", 0, 4 * hi), at(lb, lo // 4, hi // 4)))
+            copy("VS", at("gt", 4 * a, 4 * e), by(at("ft", 0, 4 * e), at(lb, a // 4, e // 4)))
             for b in range(4):
                 vtt(at("pt", 4 * a + b, 4 * e, 4), bank(4 * k + b, n), at("gt", 4 * a + b, 4 * e, 4), ALU.subtract)
             quant(qp, sp, 2 * C + a, at("gt", 4 * a, 4 * e))
@@ -665,42 +707,42 @@ def _plan(g, core, rank, T, topo, pace):
                 if "V" in (CFG["steps"][2][b], CFG["steps"][3][b]):
                     copy("VS", at("md", C * b + a, C * b + e), bank(4 * k + b, n))
         for b in range(4):
-            for d in (2, 3):
-                for a, e in CFG["sparts"]:
-                    base = by(mv(b, d - 1, 0, e), at(lb, C // 4 + a // 16, C // 4 + e // 16))
-                    if CFG["steps"][d][b] == "V":
-                        vtt(mv(b, d, a, e), base, at("md", C * b + a, C * b + e), ALU.add)
-                        continue
+            for d, e in ((2, C), (3, A)):
+                base = by(mv(b, d - 1, 0, e), at(lb, C // 4, C // 4 + e // 16))
+                if CFG["steps"][d][b] == "V":
+                    vtt(mv(b, d, 0, e), base, at("md", C * b, C * b + e), ALU.add)
+                else:
                     g0 = C * (4 * (d - 2) + b)
-                    copy("VS", at("gb", g0 + a, g0 + e), base)
-                    for k, (lo, hi) in enumerate(halves):
-                        if a <= lo < e:
-                            vtt(mv(b, d, lo, hi), bank(4 * k + b, hi - lo), at("gb", g0 + lo, g0 + hi), ALU.add)
+                    copy("VS", at("gb", g0, g0 + e), base)
+                    for k, (lo, hi) in enumerate(((0, H), (H, e))):
+                        vtt(mv(b, d, lo, hi), bank(4 * k + b, hi - lo), at("gb", g0 + lo, g0 + hi), ALU.add)
                 if d == 2:
-                    for k, (a, e) in enumerate(halves):
-                        copy("VS", mv(b, 0, a, e), bank(4 * k + b, 2 * (e - a), e - a))
+                    for k, (lo, hi) in enumerate(halves):
+                        copy("VS", mv(b, 0, lo, hi), bank(4 * k + b, 2 * (hi - lo), hi - lo))
 
         pl["cuts"].append(len(pl["ops"]))
-        for a, e in CFG["mparts"]:
+        for (a, e), _ in CFG["lparts"]:
             for b in range(4):
-                copy("VS", at("mt", 4 * a + b, 4 * e, 4), by(at("mv", 4 * C * b, 4 * C * (b + 1)), at(ll, a // 16, e // 16)))
-        for a in (0, A // 2):
-            quant(qm, sm, a, at("mt", 4 * a, 4 * a + 2 * A))
-        for b in range(4):
-            if CFG["state"][b] == "S":
-                unpack(b, fb[b], (qx, sx, 0, C))
+                copy("VS", at("mt", 4 * a + b, 4 * e, 4), by(at("mv", 4 * C * b, 4 * C * b + 3 * C + A), at(ll, a // 16, e // 16)))
+        for (a, e), _ in CFG["lparts"]:
+            quant(qm, sm, a, at("mt", 4 * a, 4 * e))
         for (a, e), banks in CFG["lparts"]:
             for b in CFG["lorder"]:
                 mm(banks[b], ("wq", "wsc", 128 * b, 128 * b + 128), (qm, sm, a, e))
                 copy("VS", at("pr", C * b + a, C * b + e), bank(banks[b], e - a), scale=0.015625)
-        for a, e in halves if CFG["xsplit"] else [(0, C)]:
+        for b in range(4):
+            if CFG["state"][b] == "S":
+                unpack(b, fb[b], (qx, sx, 0, C))
+        if r == R - 1:
+            halves = ((0, CFG["final"]), (CFG["final"], C))
+        for a, e in halves:
             for b in range(4):
-                made = by(at("pr", C * b, C * b + C), at("plo", a // 16, e // 16))
+                product = by(at("pr", C * b, C * b + C), at("plo", a // 16, e // 16))
                 out = at("xn", 4 * a + b, 4 * e, 4)
                 if CFG["state"][b] == "V":
-                    vtt(out, made, at("fo", C * b + a, C * b + e), ALU.add)
+                    vtt(out, product, at("fo", C * b + a, C * b + e), ALU.add)
                 else:
-                    copy("VS", at("gx", C * b + a, C * b + e), made)
+                    copy("VS", at("gx", C * b + a, C * b + e), product)
                     vtt(out, bank(fb[b], e, a), at("gx", C * b + a, C * b + e), ALU.add)
         tile = "xn"
 

import math
from concourse.mybir import dt, AluOpType as ALU, ActivationFunctionType as ACT

C, A, R = 320, 256, 3
STEP = [1, 2, 3]
CODE = "float8_e4m3fn_x4"
H16 = "float16"
Z = 16
PW = Z + C
SH = PW // 2
KEEP = 1280.0
LAB = 5 * C
BANK = 512
HALVES = [(0, C // 2), (C // 2, C)]

CFG = {
    "mid": 160, "final": 192,
    "loads": "uacb",
    "jumps": [(1, 1, HALVES, HALVES), (2, 1, HALVES, HALVES), (3, 2, HALVES, []), (5, 3, HALVES, HALVES), (8, 8, HALVES, HALVES),
              (16, 16, [(32, 192), (192, 320)], [(32, 192), (192, 320)]), (32, 32, [(128, 192), (192, 320)], [(128, 192), (192, 320)])],
    "runs": ([(0, 16, 16, "lab0", "lab0", 0), (0, 32, 16, "lab0", "lab", 16)] + [(a, a + 32, 32, "lab", "lab", a) for a in (32, 64, 96)]
             + [(a, a + 64, 64, "lab", "lab", a) for a in (128, 192, 256)]),
    "pieces": [(0, 192), (192, 320)],
    "cand": "VSVS",
    "steps": {2: "VSSS", 3: "VSSS"},
    "state": "VSSS",
    "lparts": [((0, 128), [0, 1, 2, 3]), ((128, 256), [4, 5, 6, 7])], "lorder": [2, 3, 1, 0],
    "sb": [0, 4], "db": [5, 7], "fb": [6, 1, 2, 3],
    "passes": 3, "ahead": 60.0, "over": 100.0, "give": 100.0,
    "tries": [90000, 100000, 30000], "seeds": [6, 2, 1], "heat": 30.0, "mean": 0.25,
}
PACES = [{"f": 1.0, "wake": 200.0, "g": 1.5, "sc": 3.8, "link": 1700.0, "rows": 450.0, "bw": 90.0, "load": 1400.0, "first": 1000.0,
          "issue": 350.0},
         {"f": 1.4, "wake": 170.0, "g": 1.85, "sc": 4.2, "link": 1200.0, "rows": 330.0, "bw": 110.0, "load": 1100.0, "first": 1000.0,
          "issue": 220.0}]
QUEUES = ["V", "S", "P", "G", "Y", "L", "in"]
ORDER = []


def _sb(n, d):
    return ("sbuf", [128, n], d)


JUMPS = len(CFG["jumps"])
SCRATCH = {
    "xs": _sb(4 * C, "bfloat16"), "us": _sb(512, "bfloat16"), "vs": _sb(512, "bfloat16"),
    "wq": _sb(512, CODE), "wsc": _sb(512, "uint8"), "cdi": _sb(40, "int32"), "cdo": _sb(48, "uint16"),
    "qu": _sb(128, CODE), "su": _sb(128, "uint8"), "qup": _sb(128, CODE), "sup": _sb(128, "uint8"),
    "qv": _sb(128, CODE), "sv": _sb(128, "uint8"), "uoff": _sb(16, "uint16"),
    "ebig": _sb(528, "bfloat16"), "ones": _sb(128, "bfloat16"), "qe": _sb(512, CODE), "se": _sb(512, "uint8"),
    "a16": _sb(24, "int32"), "b16": _sb(24, "int32"), "e0": _sb(16, "float32"), "e1": _sb(16, "float32"), "e4": _sb(16, "float32"),
    "cps": _sb(16, "float32"), "i16": _sb(8, "float32"), "a20": _sb(20, "int32"), "b20": _sb(40, "int32"), "rep": _sb(40, "uint16"),
    "hk0": _sb(32, "bfloat16"),
    "hk": _sb(A, "bfloat16"), "hk4": _sb(192, "bfloat16"), "iot": _sb(C, "bfloat16"), "col16": _sb(C, H16),
    "c1": _sb(C, "bfloat16"), "cdf": _sb(2 * C, H16), "flg": _sb(2 * C, "bfloat16"),
    "sc": _sb(C, "float32"), "sc2": _sb(C, "float32"), "gc": _sb(2 * C, "float32"), "dd": _sb(2 * C, "float32"), "aa": _sb(2 * C, "float32"),
    "w1": _sb(2 * PW, "bfloat16"), "w2": _sb(2 * PW, "bfloat16"), "ww": _sb(JUMPS * PW, "bfloat16"), "lab0": _sb(2 * Z, "bfloat16"),
    "lab": _sb(PW, "bfloat16"), "hb": _sb(C, H16), "h4": _sb(C, H16), "hh": _sb(JUMPS * C, H16), "li": _sb(C, H16), "hl": _sb(C, H16),
    "hp": _sb(C, H16), "h2": _sb(A, H16), "off": _sb((JUMPS + 1) * 32, "uint16"), "qq": _sb(32, "uint16"),
    "ef": _sb(4 * C, "bfloat16"), "cum": _sb(2 * C + 1, "bfloat16"), "pl": _sb(C, "bfloat16"), "plo": _sb(32, "uint16"),
    "srt": _sb(C, "float32"),
    "fo": _sb(4 * C, "bfloat16"), "md": _sb(4 * C, "bfloat16"), "mv": _sb(16 * C, "bfloat16"), "gb": _sb(8 * C, "bfloat16"),
    "pr": _sb(4 * C, "float32"), "gx": _sb(4 * C, "float32"), "ys": _sb(C, "float32"),
    "ft": _sb(4 * C, "bfloat16"), "gt": _sb(4 * C, "bfloat16"), "pt": _sb(4 * C, "bfloat16"), "mt": _sb(4 * A, "bfloat16"),
    "xn": _sb(4 * C, "bfloat16"),
    "ps": ("psum", [128, BANK * 8], "float32"),
}
for _r in range(R + 1):
    SCRATCH["qx%d" % _r] = _sb(C, CODE)
    SCRATCH["sx%d" % _r] = _sb(C, "uint8")
for _r in range(R):
    SCRATCH["lq%d" % _r] = _sb(C, CODE)
    SCRATCH["ls%d" % _r] = _sb(C, "uint8")
    SCRATCH["lb%d" % _r] = _sb(112, "uint16")
    SCRATCH["ll%d" % _r] = _sb(16, "uint16")
    SCRATCH["ob%d" % _r] = _sb(112, "uint16")
    SCRATCH["ol%d" % _r] = _sb(16, "uint16")
    SCRATCH["qp%d" % _r] = _sb(3 * C, CODE)
    SCRATCH["sp%d" % _r] = _sb(3 * C, "uint8")
    SCRATCH["qm%d" % _r] = _sb(A, CODE)
    SCRATCH["sm%d" % _r] = _sb(A, "uint8")

SEMAPHORES = (["cV", "cS", "cP", "cG", "sent", "l_cd", "l_u", "l_xa", "l_xb", "l_v", "l_wc", "l_ws", "outS", "outY"]
              + ["a%s%d" % (k, r) for k in "qrcbl" for r in range(R)])

BYTES = {"float32": 4, "int32": 4, CODE: 4, "bfloat16": 2, H16: 2, "uint16": 2, "uint8": 1}


def _add(pl, costs, fn, reads, writes, kind="c", sem=None, total=0, lag=0.0, after=(), behind=()):
    ops, n = pl["ops"], len(pl["ops"])
    deps, shared = set(after), set()
    for name, cols in reads:
        for j, c, wrote in pl["seen"].get(name, []):
            if c & cols:
                if wrote:
                    deps.add(j)
                elif name == "ps":
                    shared.add(j)
    for name, cols in writes:
        kept = []
        for j, c, wrote in pl["seen"].get(name, []):
            if c & cols:
                (shared if kind == "c" == ops[j]["kind"] else deps).add(j)
            if c & ~cols:
                kept.append((j, c & ~cols, wrote))
        pl["seen"][name] = kept
    for name, cols in reads:
        pl["seen"].setdefault(name, []).append((n, cols, False))
    for name, cols in writes:
        pl["seen"].setdefault(name, []).append((n, cols, True))
    ops.append({"costs": costs, "fn": fn, "deps": deps, "shared": shared - deps, "kind": kind, "sem": sem, "total": total, "lag": lag,
                "behind": list(behind)})
    return n


def _edges(pl):
    ops = pl["ops"]
    pred = [[(j, ops[j]["lag"] + pl["wake"]) for j in sorted(op["deps"] | op["shared"])] + [(j, 0.0) for j in op["behind"]] for op in ops]
    succ = [[] for _ in ops]
    for k in range(len(ops)):
        for j, delay in pred[k]:
            succ[j].append((k, delay))
    return pred, succ


def _list(ops, pred, succ, worth, first):
    n = len(ops)
    left = [len(p) for p in pred]
    since = list(first)
    ready = {k: since[k] for k in range(n) if not left[k]}
    free = {e: 0.0 for e in QUEUES}
    order, eng, end = [], {}, [0.0] * n

    def choose(e, mine):
        t = max(free[e], min(ready[k] for k in mine))
        for i, k in enumerate(mine):
            s = max(t, ready[k])
            if ready[k] <= t + CFG["ahead"] and all(s + ops[k]["costs"][e] <= ready[j] + CFG["over"] for j in mine[:i]):
                return s, k
        k = min(mine, key=lambda k: (ready[k] if ready[k] > t else 1e18, -worth[k]))
        return max(t, ready[k]), k

    while ready:
        best = None
        ranked = sorted(ready, key=lambda k: (-worth[k], k))
        for e in QUEUES:
            mine = [k for k in ranked if e in ops[k]["costs"]]
            if e == "V":
                ts, theirs = free["S"], set()
                for k in ranked:
                    if "S" in ops[k]["costs"] and max(ts, ready[k]) <= max(free["V"], ready[k]) + CFG["give"]:
                        theirs.add(k)
                        ts = max(ts, ready[k]) + ops[k]["costs"]["S"]
                mine = [k for k in mine if k not in theirs]
            if not mine:
                continue
            t, k = choose(e, mine)
            if best is None or t < best[0]:
                best = (t, e, k)
        t, e, k = best
        end[k] = t + ops[k]["costs"][e]
        if e != "in":
            free[e] = end[k]
        eng[k] = e
        order.append(k)
        del ready[k]
        for j, delay in succ[k]:
            since[j] = max(since[j], end[k] + delay)
            left[j] -= 1
            if not left[j]:
                ready[j] = since[j]
    return order, eng, end


def _first_order(pl):
    ops, n = pl["ops"], len(pl["ops"])
    pred, succ = _edges(pl)
    worth = [0.0] * n
    for k in range(n - 1, -1, -1):
        worth[k] = min(ops[k]["costs"].values()) + max([delay + worth[j] for j, delay in succ[k]] + [ops[k]["lag"]])
    best = None
    for _ in range(CFG["passes"]):
        order, eng, end = _list(ops, pred, succ, worth, [0.0] * n)
        span = max(end[k] + ops[k]["lag"] for k in range(n))
        if best is None or span < best[0]:
            best = (span, order, eng)
        worth = _list(ops, succ, pred, end, [op["lag"] for op in ops])[2]
    return best[1], best[2]


def _mend(plans, order, eng, lo, hi, tries, start):
    n, ops = hi - lo, plans[0]["ops"]
    row = [k - lo for k in order]
    on = [QUEUES.index(eng[k]) for k in range(lo, hi)]
    either = [len(ops[k]["costs"]) > 1 for k in range(lo, hi)]
    pred, succ = _edges(plans[0])
    later = [set(j - lo for j, _ in succ[k] if j < hi) for k in range(lo, hi)]
    earlier = [set(j - lo for j, _ in pred[k] if j >= lo) for k in range(lo, hi)]
    hard = [set(j - lo for j in ops[k]["deps"] if j >= lo) for k in range(lo, hi)]
    above = []
    for k in range(n):
        above.append(set().union(*[above[j] | {j} for j in hard[k] if ops[lo + j]["lag"] >= 0]))
    hard = [[j for j in sorted(h) if not any(j in above[m] for m in h if ops[lo + m]["lag"] >= 0)] for h in hard]
    soft = [[j - lo for j in sorted(ops[k]["shared"]) if j >= lo and j - lo not in above[k - lo]] for k in range(lo, hi)]
    tied = [[j - lo for j in ops[k]["behind"] if j >= lo] for k in range(lo, hi)]
    (c0, d0), (c1, d1) = [([[pl["ops"][k]["costs"].get(q, 0.0) for q in QUEUES] for k in range(lo, hi)],
                           [pl["ops"][k]["lag"] + pl["wake"] for k in range(lo, hi)]) for pl in plans]
    last = [(k, max(d0[k], plans[0]["wake"]) - d0[k], max(d1[k], plans[1]["wake"]) - d1[k]) for k in range(n) if not later[k]]
    arrival = QUEUES.index("in")
    mean = CFG["mean"] / n

    def span(seen, p0):
        a, b = seen[0][:], seen[1][:]
        fa, fb = [0.0] * len(QUEUES), [0.0] * len(QUEUES)
        met, missing = [False] * len(QUEUES), arrival
        for i in range(p0 - 1, -1, -1):
            k = row[i]
            q = on[k]
            if not met[q] and q != arrival:
                met[q], fa[q], fb[q] = True, a[k] - d0[k], b[k] - d1[k]
                missing -= 1
                if not missing:
                    break
        for k in row[p0:]:
            q = on[k]
            s, t = fa[q], fb[q]
            for j in hard[k]:
                if a[j] > s:
                    s = a[j]
                if b[j] > t:
                    t = b[j]
            if soft[k]:
                for j in soft[k]:
                    if on[j] != q:
                        if a[j] > s:
                            s = a[j]
                        if b[j] > t:
                            t = b[j]
            if q > 2:
                for j in tied[k]:
                    s, t = max(s, a[j] - d0[j]), max(t, b[j] - d1[j])
                if q == arrival:
                    a[k], b[k] = s + d0[k], t + d1[k]
                    continue
            fa[q] = s = s + c0[k][q]
            fb[q] = t = t + c1[k][q]
            a[k] = s + d0[k]
            b[k] = t + d1[k]
        return (max([a[k] + x for k, x, _ in last]) + max([b[k] + x for k, _, x in last]) + mean * (sum(a) + sum(b))) / 2, (a, b)

    seed, far = [start], (1, 1, 2, 3, 5, 8) + ((13, 25) if lo == 0 else ())

    def draw(m):
        seed[0] = (seed[0] * 1103515245 + 12345) % 2147483648
        return (seed[0] >> 8) % m

    now, seen = span([[0.0] * n, [0.0] * n], 0)
    best = (now, row[:], on[:])
    for it in range(tries):
        p = draw(n)
        k = row[p]
        was = on[k]
        if was > 1 and (was == arrival or draw(2)):
            continue
        way, steps = 2 * draw(2) - 1, far[draw(len(far))]
        if either[k] and draw(10) < 3:
            on[k] = 1 - was
            steps *= draw(2)
        q, to, stop = p, p, (earlier[k] if way < 0 else later[k])
        while steps and 0 <= q + way < n and row[q + way] not in stop:
            q += way
            if on[row[q]] == on[k]:
                steps, to = steps - 1, q
        if to == p and on[k] == was:
            continue
        row.insert(to, row.pop(p))
        s, new = span(seen, min(p, to))
        if s <= now or draw(4096) < 4096 * math.exp((now - s) / (CFG["heat"] * (1 - it / tries) + 1)):
            now, seen = s, new
            if s < best[0]:
                best = (s, row[:], on[:])
            if it % 50 == 0:
                row.sort(key=lambda k: round(seen[0][k] - d0[k] - c0[k][on[k]], 3))
        else:
            row.insert(p, row.pop(to))
            on[k] = was
    return [k + lo for k in best[1]], {lo + k: QUEUES[q] for k, q in enumerate(best[2])}


def _order(plans):
    order, eng = _first_order(plans[0])
    cuts, n = plans[0]["cuts"], len(plans[0]["ops"])
    like, begin = plans[0]["like"], plans[0]["begin"]
    row, on = _mend(plans, [k for k in order if cuts[0] <= k < cuts[1]], eng, cuts[0], cuts[1], CFG["tries"][0], CFG["seeds"][0])
    place = {k - cuts[0]: i for i, k in enumerate(row)}
    rows = []
    for s, (lo, hi) in enumerate(zip([0] + cuts, cuts + [n])):
        mine = [k for k in order if lo <= k < hi]
        same = sorted((k for k in mine if k in like), key=lambda k: place[like[k]])
        for k in same:
            eng[k] = on[cuts[0] + like[k]]
        spots = iter(same)
        wish = [k for k in mine if k < begin] + [next(spots) if k in like else k for k in mine if k >= begin]
        mine, done = [], set()
        pred = _edges(plans[0])[0]
        while wish:
            k = next(k for k in wish if all(j < lo or j in done for j, _ in pred[k]))
            wish.remove(k)
            done.add(k)
            mine.append(k)
        if s in (0, len(cuts)):
            i = 1 if s == 0 else 2
            mine, moved = _mend(plans, mine, eng, lo, hi, CFG["tries"][i], CFG["seeds"][i])
            eng.update(moved)
        rows += mine
    return rows, eng


def _emit(pl, order, eng, g, T):
    ops = pl["ops"]
    at = {n: k for k, n in enumerate(order)}
    queue = {"V": g.vector, "S": g.scalar, "P": g.tensor, "G": g, "Y": g.sync}
    known = {e: {} for e in queue}
    for n in order:
        op = ops[n]
        op["eng"] = eng[n]
        op["line"] = op["eng"] if op["kind"] == "c" else "d%d" % n
        op["waits"] = []
        if op["kind"] == "in":
            op["clock"] = {op["line"]: at[n]}
            continue
        kn = known[op["eng"]]
        need = set(op["deps"]) | set(j for j in op["shared"] if eng[j] != eng[n])
        for j in sorted(need, key=lambda j: -at[j]):
            d = ops[j]
            if d["kind"] == "send" or kn.get(d["line"], -1) >= at[j]:
                continue
            op["waits"].append(j)
            d["signals"] = True
            for line, m in d["clock"].items():
                kn[line] = max(kn.get(line, -1), m)
        op["clock"] = dict(kn)
        op["clock"][op["line"]] = at[n]
    count = {e: 0 for e in queue}
    for n in order:
        op = ops[n]
        if op["kind"] == "c" and op.get("signals"):
            count[op["eng"]] += 1
            op["sem"], op["total"] = "c" + op["eng"], count[op["eng"]]
    for n in order:
        op = ops[n]
        if op["kind"] == "in":
            continue
        q = queue[op["eng"]]
        for j in op["waits"]:
            q.wait_ge(T.sem[ops[j]["sem"]], ops[j]["total"])
        ins = op["fn"](op["eng"])
        if op["kind"] == "dma":
            ins.then_inc(T.sem[op["sem"]], 16)
        elif op["kind"] == "c" and op.get("signals"):
            ins.then_inc(T.sem[op["sem"]], 1)


def rank_program(g, core, T, topo):
    rank = T.rank_of(core)
    if rank is None:
        return
    pl = _plan(g, core, rank, T, topo, PACES[0])
    if not ORDER:
        ORDER.append(_order([pl] + [_plan(g, core, rank, T, topo, pace) for pace in PACES[1:]]))
    _emit(pl, ORDER[0][0], ORDER[0][1], g, T)
    g.scalar.wait_ge(T.sem.outS, pl["outs"]["S"])
    g.sync.wait_ge(T.sem.outY, pl["outs"]["Y"])
    g.wait_ge(T.sem.sent, pl["sent"])


def _plan(g, core, rank, T, topo, pace):
    n_ranks = len(T.cores)
    pl = {"ops": [], "seen": {}, "cuts": [], "like": {}, "wake": pace["wake"], "sent": 0, "outs": {"S": 0, "Y": 0}}
    V, S = g.vector, g.scalar
    last, wire, loads, queued = [], [], [], [0.0]
    H = CFG["mid"]
    sb, db, fb = CFG["sb"], CFG["db"], CFG["fb"]
    halves = ((0, H), (H, C))
    f = pace["f"]
    cyc = 0.83 * f

    def at(name, a=0, b=None, st=1):
        where, shape, kind = SCRATCH[name]
        b = shape[1] if b is None else b
        n = len(range(a, b, st))
        if where == "psum":
            cols = 1 << (a // BANK)
        elif st == 1:
            cols = ((1 << n) - 1) << a
        else:
            cols = ((1 << (st * n)) - 1) // ((1 << st) - 1) << a
        return {"ap": T[name][:, a:b:st] if st > 1 else T[name][:, a:b], "keys": [(name, cols)], "n": n, "bytes": BYTES[kind],
                "psum": where == "psum", "list": False}

    def by(win, off, words=False):
        ap = win["ap"].bitcast(dt.uint32) if words else win["ap"]
        return dict(win, ap=ap.indirect(off["ap"]), keys=win["keys"] + off["keys"], n=16 * off["n"], list=True)

    def bank(b, n, a=0):
        return at("ps", BANK * b + a, BANK * b + n)

    def keys(*xs):
        return [k for x in xs if isinstance(x, dict) for k in x["keys"]]

    def ap(x):
        return x["ap"] if isinstance(x, dict) else x

    def cost(e, out, ins, k=None):
        full = [x for x in ins if isinstance(x, dict) and x["n"] == out["n"]]
        if out["list"]:
            return 50 * f + pace["sc"] * cyc * out["n"]
        if any(x["list"] for x in full):
            return (50 if e == "V" else 65) * f + pace["g"] * cyc * out["n"]
        if k is None:
            k = 0.5 if e == "V" and all(x["bytes"] == 2 for x in full + [out]) else 1.0
        return cyc * max(64, k * out["n"])

    def call(engs, fn, out, ins, k=None):
        return _add(pl, {e: cost(e, out, ins, k) for e in engs}, fn, keys(*ins) + keys(out)[1:], keys(out)[:1])

    def copy(engs, out, in_, scale=None):
        def fn(e):
            if e == "S":
                return S.activation(out["ap"], in_["ap"], ACT.Copy) if scale is None else S.activation(out["ap"], in_["ap"], ACT.Copy, scale=scale)
            return V.tensor_copy(out["ap"], in_["ap"]) if scale is None else V.tensor_scalar(out["ap"], in_["ap"], scale, None, ALU.mult)
        call(engs, fn, out, [in_])

    def vts(out, in0, s1, s2, op0, op1=None):
        if op1 is None:
            call("V", lambda e: V.tensor_scalar(out["ap"], in0["ap"], ap(s1), None, op0), out, [in0, s1])
        else:
            call("V", lambda e: V.tensor_scalar(out["ap"], in0["ap"], ap(s1), ap(s2), op0, op1), out, [in0, s1, s2])

    def vtt(out, in0, in1, op):
        call("V", lambda e: V.tensor_tensor(out["ap"], in0["ap"], in1["ap"], op), out, [in0, in1], 1.0 if in0["psum"] or in1["psum"] else 2.0)

    def vset(out, c):
        call("V", lambda e: V.memset(out["ap"], c), out, [])

    def scan(out, d0, d1, first, op0, op1):
        call("V", lambda e: V.tensor_tensor_scan(out["ap"], d0["ap"], d1["ap"], first, op0, op1), out, [d0, d1])

    def act(out, in_, func, bias=0.0, scale=1.0):
        call("S", lambda e: S.activation(out["ap"], in_["ap"], func, bias=ap(bias), scale=scale), out, [in_, bias])

    def iota(out, pattern, base, cm, small=True, behind=()):
        if small:
            fn = lambda e: g.iota(out["ap"], pattern, base, cm, allow_small_or_imprecise_dtypes=True)
        else:
            fn = lambda e: g.iota(out["ap"], pattern, base, cm)
        _add(pl, {"G": 130 * f + 2 * cyc * out["n"]}, fn, [], keys(out), behind=behind)

    def wrap(out, data, keeper="hk"):
        scan(out, at(keeper, 0, data["n"]), data, 0.0, ALU.add, ALU.max)

    def held(name, a, b, run=16):
        return at(name, a + run - 1, b, run)

    def quant(q, sc, a, in_):
        codes, plane = at(q, a, a + in_["n"] // 4), at(sc, a, a + in_["n"] // 4)
        _add(pl, {"V": f * (12 + 0.22 * in_["n"])}, lambda e: V.quantize_mx(codes["ap"], plane["ap"], in_["ap"]), keys(in_), keys(codes, plane))

    def mm(b, w, x, start=True, stop=True):
        sides = [at(w[0], w[2], w[3]), at(w[1], w[2], w[3]), at(x[0], x[2], x[3]), at(x[1], x[2], x[3])]
        out = bank(b, x[3] - x[2])
        _add(pl, {"P": 0.65 * (x[3] - x[2] + 16)},
             lambda e: g.tensor.matmul_mx(out["ap"], sides[0]["ap"], sides[1]["ap"], sides[2]["ap"], sides[3]["ap"], start, stop),
             keys(*sides), keys(out))

    def unpack(b, into, x, start=True, stop=True):
        mm(into, ("qe", "se", 128 * b, 128 * b + 128), x, start, stop)

    def load(eng, out, in_, sem, after=(), codes=False):
        q = S if eng == "S" else g.sync
        o = out["ap"].bitcast(dt.uint8) if codes else out["ap"]
        queued[0] += 0.5 * pace["rows"] + 0.4 * out["n"] * out["bytes"]
        loads.append(_add(pl, {eng: 60.0}, lambda e: q.dma_start(o, in_), [], keys(out), kind="dma", sem=sem, total=16,
                          lag=pace["load"] + queued[0], after=after, behind=loads[-1:]))

    def store(eng, out, in_, reads, rows=128):
        pl["outs"][eng] += 16
        q = S if eng == "S" else g.sync
        n = _add(pl, {eng: 60.0}, lambda e: q.dma_start(out, in_), keys(reads), [], kind="dma", sem="out" + eng, lag=pace["load"])
        _add(pl, {"L": rows / 256 * pace["rows"] + rows / 320 * reads["n"] * reads["bytes"]}, None, [], [], kind="in", after=[n])

    def send(dst, out, in_, sem, codes=False):
        rid, pid, _ = topo.addr(dst)
        pl["sent"] += len(topo.engines(core, dst))
        o, i = (out["ap"].bitcast(dt.uint8), in_["ap"].bitcast(dt.uint8)) if codes else (out["ap"], in_["ap"])
        n = _add(pl, {"G": pace["issue"]}, lambda e: g.remote_dma(o, i, T.sem[sem], T.sem.sent, pid, rid, topo.mask(core, dst)), keys(in_), [],
                 kind="send", lag=pace["link"] + (0.0 if last else pace["first"]), behind=last[-1:])
        last.append(n)
        wire.append(_add(pl, {"L": pace["rows"] + 128 * in_["n"] * in_["bytes"] / pace["bw"]}, None, [], [], kind="in", after=[n],
                         behind=wire[-1:]))
        return wire[-1]

    def arrives(src, sem, sends, outs):
        _add(pl, {"in": 0.0}, None, [], keys(*outs), kind="in", sem=sem, total=len(sends) * len(topo.engines(src, core)),
             lag=-pace["wake"], after=sends)

    def col(j):
        return at("cps", j, j + 1)

    steps = [1] + [w + o for w, o, _, _ in CFG["jumps"]]
    paired = {w: "w%d" % w for w, o, _, _ in CFG["jumps"] if o == 1}

    def win(k, a, b):
        i = steps.index(k) - 1
        return at(paired[k], 2 * a, 2 * b) if k in paired else at("ww", PW * i + a, PW * i + b)

    def made(k, a, b):
        return at(paired[k], 2 * a + 1, 2 * b, 2) if k in paired else win(k, a, b)

    def off(k, a, b):
        i = steps.index(k)
        return at("off", 32 * i + a // 16, 32 * i + b // 16)

    def fixed(k, behind=()):
        low = CFG["jumps"][steps.index(k) - 1][2][0][0]
        if k % 4 == 2:
            iota(made(k, 0, Z), [[0, 4], [-2, 2], [1, 2]], 2 - SH, 0, behind=behind)
            return
        iota(made(k, 0, Z + low), [[1, Z + low]], (0, -1, 0, 1)[k % 4] - SH, 0, behind=behind)
        if k % 2:
            s = (0, 0, 0, 3)[k % 4]
            vset(made(k, s, s + 1), float(3 - s - SH))

    def mv(b, d, a=0, e=C):
        return at("mv", 4 * C * b + C * d + a, 4 * C * b + C * d + e)

    inputs = {"c": (at("cdi"), T.cd[:], "l_cd"), "u": (at("us"), T.u[:], "l_u"), "a": (at("xs", 0, 4 * H), T.x[:, 0:4 * H], "l_xa"),
              "b": (at("xs", 4 * H, 4 * C), T.x[:, 4 * H:4 * C], "l_xb")}
    for name in CFG["loads"]:
        load("Y", *inputs[name])

    iota(at("i16"), [[16, 8]], 0, 0)
    iota(at("a16", 0, 16), [[1, 16]], 128, -1, small=False)
    iota(at("iot"), [[1, C]], Z - SH, 0)
    vset(at("ones"), 1.0)
    vset(at("ebig"), 0.0)
    diag = at("ebig", 3, 515, 4)
    _add(pl, {"G": 170 * f + 256 * cyc},
         lambda e: g.affine_select(diag["ap"], T.ones[:], [[-1, 128]], ALU.is_equal, 0.0, 0, 1), keys(at("ones")), keys(diag))
    iota(win(1, 0, Z), [[1, Z], [0, 2]], -SH - 1, 0)
    vset(at("w2", 0, 2 * PW, 2), 0.0)
    for k in steps[1:3]:
        fixed(k)
    vts(at("col16"), at("iot"), float(3 * C + SH - Z), None, ALU.add)
    vset(at("flg", 0, 2 * C, 2), 0.0)
    copy("V", at("uoff", 0, 8), at("i16"))
    vts(at("b16", 0, 16), at("a16", 0, 16), 15, None, ALU.bitwise_and)
    vts(at("e0"), at("b16", 0, 16), 0.0, -4 * KEEP, ALU.is_equal, ALU.mult)
    vts(at("e1"), at("b16", 0, 16), 1.0, KEEP, ALU.is_equal, ALU.mult)
    copy("V", at("cdo", 0, 40), at("cdi"))
    vtt(at("hk0", 0, 16), at("e0"), at("e1"), ALU.add)
    iota(at("a20"), [[0, 20]], 0, 1, small=False)
    for j, mask in enumerate((15, 3)):
        vts(at("b20", 20 * j, 20 * j + 20), at("a20"), mask, None, ALU.bitwise_and)
    copy("V", at("rep", 0, 40), at("b20"))
    copy("VS", at("hk"), by(at("hk0", 0, 16), at("rep", 0, A // 16)))
    copy("VS", at("c1"), by(at("iot"), at("cdo", 0, 20)))
    quant("qu", "su", 0, at("us"))
    for b in range(4):
        quant("qe", "se", 128 * b, at("ebig", 3 - b, 515 - b))
    picked = by(at("qu"), at("uoff", 0, 8), words=True)
    call("V", lambda e: V.tensor_copy(T.qup[:].bitcast(dt.uint32), picked["ap"]), at("qup"), [picked])
    copy("VS", at("sup"), by(at("su"), at("uoff", 0, 8)))
    vtt(at("cdf", 0, 2 * C, 2), by(at("iot"), at("cdo", 20, 40)), at("c1"), ALU.subtract)
    vset(at("w1", 1, 2), 3.0 - SH)
    copy("V", at("cdf", 3, 2 * C, 2), at("c1", 1, C))
    vset(at("cdf", 1, 2), 3.0 - SH)
    for j, c0 in enumerate([SH + 0.5, SH, SH - Z, C // 2 + 1, 2 * C]):
        act(col(j), at("e1", 0, 1), ACT.Identity, bias=float(c0 - KEEP))
    cp_pair, cp_ptr, cp_base, cp_even, cp_slot, cp_four, cp_half, cp_place = [col(j) for j in range(8)]
    iota(at("a16", 16, 20), [[-4, 4]], 128, 1, small=False)
    vts(at("b16", 16, 20), at("a16", 16, 20), 12, None, ALU.bitwise_and)
    vts(at("e4", 0, 4), at("b16", 16, 20), 0.0, -4 * KEEP, ALU.is_equal, ALU.mult)
    vts(at("e4", 4, 8), at("b16", 16, 20), 12.0, KEEP, ALU.is_equal, ALU.mult)
    vtt(at("hk0", 16, 20), at("e4", 0, 4), at("e4", 4, 8), ALU.add)
    copy("VS", at("hk4", 0, H), by(at("hk0", 16, 20), at("rep", 20, 20 + H // 16)))
    vts(at("e4", 8, 9), at("b20", 20, 21), 0.25, float(SH - Z - KEEP), ALU.mult, ALU.add)
    vtt(cp_four, at("e4", 8, 9), at("e4", 4, 5), ALU.add)

    tile, begins, extra = "xs", [], []
    for r in range(R + 1):
        begins.append(len(pl["ops"]))
        qx, sx = "qx%d" % r, "sx%d" % r
        side = ("qup", "sup", 0, 128) if r < R else ("qv", "sv", 0, 128)
        for k, (a, b) in enumerate(halves):
            quant(qx, sx, a, at(tile, 4 * a, 4 * b))
            mm(sb[k], side, (qx, sx, a, b))
        if r == R:
            break
        dst, src = T.cores[(rank + STEP[r]) % n_ranks], T.cores[(rank - STEP[r]) % n_ranks]
        lq, ls, lb, ll, ob, ol, qp, sp, qm, sm = ["%s%d" % (k, r) for k in ("lq", "ls", "lb", "ll", "ob", "ol", "qp", "sp", "qm", "sm")]
        first = [send(dst, at(lq, 0, H), at(qx, 0, H), "aq%d" % r, codes=True), send(dst, at(ls), at(sx), "aq%d" % r)]
        arrives(src, "aq%d" % r, first, [at(lq, 0, H), at(ls)])
        arrives(src, "ar%d" % r, [send(dst, at(lq, H, C), at(qx, H, C), "ar%d" % r, codes=True)], [at(lq, H, C)])

        for k, (a, b) in enumerate(halves):
            copy("VS", at("sc", a, b), bank(sb[k], b - a))
            if "V" in CFG["cand"][2 * k:2 * k + 2]:
                mm(db[k], side, (qx, sx, a, b))
                copy("VS", at("sc2", a, b), bank(db[k], b - a))
        for k, (a, b) in enumerate(halves):
            for c in range(2):
                theirs = by(at("sc", 0, b), at("cdo", (C * c + a) // 16, (C * c + b) // 16))
                d = at("dd", C * c + a, C * c + b)
                if CFG["cand"][2 * k + c] == "V":
                    vtt(d, theirs, at("sc2", a, b), ALU.subtract)
                else:
                    copy("VS", at("gc", C * c + a, C * c + b), theirs)
                    vtt(d, at("gc", C * c + a, C * c + b), bank(sb[k], b - a), ALU.subtract)
                act(at("aa", C * c + a, C * c + b), d, ACT.Abs)
            vtt(at("flg", 2 * a + 1, 2 * b, 2), at("aa", C + a, C + b), at("aa", a, b), ALU.is_lt)
            scan(win(1, Z + a, Z + b), at("flg", 2 * a, 2 * b), at("cdf", 2 * a, 2 * b), 0.0, ALU.mult, ALU.add)
            base = made(1, Z + a, Z + b)
            wrap(at("hb", a, b), base)
            vts(off(1, a, b), held("hb", a, b), cp_pair, 2.0, ALU.add, ALU.mult)
            wrap(at("h4", a, b), base, "hk4")
            vts(at(ob, a // 4, b // 4), held("h4", a, b, 4), cp_four, 4.0, ALU.add, ALU.mult)
            if k == 1:
                vts(at(ob, C // 4, C // 4 + C // 16), held("hb", 0, C), cp_base, None, ALU.add)
            lo, hi, sem = a // 4, b // 4 + k * C // 16, "a%s%d" % ("cb"[k], r)
            arrives(src, sem, [send(dst, at(lb, lo, hi), at(ob, lo, hi), sem)], [at(lb, lo, hi)])

        if r == 0:
            queued[0], n0 = 0.0, len(pl["ops"])
            load("Y", at("wq"), T.wc[:], "l_wc", after=[n0 - 1], codes=True)
            load("Y", at("wsc"), T.ws[:], "l_ws")
            load("Y", at("vs"), T.v[:], "l_v")
            quant("qv", "sv", 0, at("vs"))
            for k in steps[3:-1]:
                fixed(k, last[2:3])
            for name in ("lab", "lab0"):
                iota(at(name, 0, Z), [[0, 4], [C, 4]], -LAB, 0, behind=last[2:3])
            vset(at("cum", 0, 1), -(C // 2 + 1.0))
            vts(at("b16", 20, 21), at("a20", 0, 1), 1, None, ALU.bitwise_and)
            vts(cp_half, at("b16", 20, 21), cp_slot, None, ALU.add)
            vts(cp_place, at("b16", 20, 21), -1.0, cp_even, ALU.mult, ALU.add)
            for b in range(4):
                iota(at("pr", C * b + A, C * b + C), [[0, C - A]], 0, 0, behind=last[-1:])
            extra += range(n0, len(pl["ops"]))

        for i, (w, o, parts, listed) in enumerate(CFG["jumps"]):
            for a, b in parts:
                copy("VS", made(w + o, Z + a, Z + b), by(win(w, 0, Z + b), off(o, a, b)))
            for a, b in listed:
                wrap(at("hh", C * i + a, C * i + b), made(w + o, Z + a, Z + b))
                vts(off(w + o, a, b), held("hh", C * i + a, C * i + b), cp_ptr, None, ALU.add)
        for a, b, k, known, into, end in CFG["runs"]:
            copy("VS", at(into, Z + a, Z + b), by(at(known, 0, Z + end), off(k, a, b)))

        for a, b in CFG["pieces"]:
            lab = at("lab", Z + a, Z + b)
            scan(at("li", a, b), lab, at("col16", a, b), 0.0, ALU.min, ALU.add)
            wrap(at("hl", a, b), at("li", a, b))
            vts(at("qq", a // 16, b // 16), held("hl", a, b), cp_half, 0.5, ALU.add, ALU.mult)
            for d in range(4):
                flag = at("ef", C * d + a, C * d + b)
                end = {0: (1.0 - LAB, -1.0), 3: (1.0 + LAB - 3 * C, 1.0)}.get(d)

                def flags(e, flag=flag, lab=lab, d=d, end=end):
                    if e == "S":
                        return S.activation(flag["ap"], lab["ap"], ACT.Relu, bias=end[0], scale=end[1])
                    return V.tensor_scalar(flag["ap"], lab["ap"], float(C * d - LAB), None, ALU.is_equal)
                call("VS" if end else "V", flags, flag, [lab])
        scan(at("cum", 1, 2 * C + 1), at("ef", 0, 4 * C, 2), at("ef", 1, 4 * C, 2), -(C // 2 + 1.0), ALU.add, ALU.add)
        for a, b in HALVES:
            copy("VS", at("pl", a, b), by(at("cum"), at("qq", a // 16, b // 16)))
        for a, b in HALVES:
            wrap(at("hp", a, b), at("pl", a, b))
        vts(at("plo", 0, 20), held("hp", 0, C), cp_place, None, ALU.add)
        copy("V", by(at("srt"), at("plo", 0, 20)), at("li"))
        wrap(at("h2"), at("srt", 0, A))
        vts(at(ol), held("h2", 0, A), cp_slot, None, ALU.add)
        arrives(src, "al%d" % r, [send(dst, at(ll), at(ol), "al%d" % r)], [at(ll)])

        for b in range(4):
            if CFG["state"][b] == "V":
                unpack(b, fb[b], (qx, sx, 0, C))
                for a, e in halves:
                    copy("VS", at("fo", C * b + a, C * b + e), bank(fb[b], e, a))

        for k, (a, e) in enumerate(halves):
            n = e - a
            for b in range(4):
                unpack(b, 4 * k + b, (lq, ls, a, e))
                copy("VS", at("ft", 4 * a + b, 4 * e, 4), bank(4 * k + b, n))
            quant(qp, sp, 2 * a + n, at("ft", 4 * a, 4 * e))
            copy("VS", at("gt", 4 * a, 4 * e), by(at("ft", 0, 4 * e), at(lb, a // 4, e // 4)))
            for b in range(4):
                vtt(at("pt", 4 * a + b, 4 * e, 4), bank(4 * k + b, n), at("gt", 4 * a + b, 4 * e, 4), ALU.subtract)
            quant(qp, sp, 2 * C + a, at("gt", 4 * a, 4 * e))
            quant(qp, sp, 2 * a, at("pt", 4 * a, 4 * e))
            for b in range(4):
                unpack(b, 4 * k + b, (qp, sp, 2 * C + a, 2 * C + e), True, False)
                unpack(b, 4 * k + b, (qp, sp, 2 * a, 2 * a + n), False, True)
                copy("VS", mv(b, 1, a, e), bank(4 * k + b, n))
                unpack(b, 4 * k + b, (qp, sp, 2 * a, 2 * e))
                if "V" in (CFG["steps"][2][b], CFG["steps"][3][b]):
                    copy("VS", at("md", C * b + a, C * b + e), bank(4 * k + b, n))
        for b in range(4):
            for d, e in ((2, C), (3, A)):
                base = by(mv(b, d - 1, 0, e), at(lb, C // 4, C // 4 + e // 16))
                if CFG["steps"][d][b] == "V":
                    vtt(mv(b, d, 0, e), base, at("md", C * b, C * b + e), ALU.add)
                else:
                    g0 = C * (4 * (d - 2) + b)
                    copy("VS", at("gb", g0, g0 + e), base)
                    for k, (lo, hi) in enumerate(((0, H), (H, e))):
                        vtt(mv(b, d, lo, hi), bank(4 * k + b, hi - lo), at("gb", g0 + lo, g0 + hi), ALU.add)
                if d == 2:
                    for k, (lo, hi) in enumerate(halves):
                        copy("VS", mv(b, 0, lo, hi), bank(4 * k + b, 2 * (hi - lo), hi - lo))

        pl["cuts"].append(len(pl["ops"]))
        for (a, e), _ in CFG["lparts"]:
            for b in range(4):
                copy("VS", at("mt", 4 * a + b, 4 * e, 4), by(at("mv", 4 * C * b, 4 * C * b + 3 * C + A), at(ll, a // 16, e // 16)))
        for (a, e), _ in CFG["lparts"]:
            quant(qm, sm, a, at("mt", 4 * a, 4 * e))
        for (a, e), banks in CFG["lparts"]:
            for b in CFG["lorder"]:
                mm(banks[b], ("wq", "wsc", 128 * b, 128 * b + 128), (qm, sm, a, e))
                copy("VS", at("pr", C * b + a, C * b + e), bank(banks[b], e - a), scale=0.015625)
        for b in range(4):
            if CFG["state"][b] == "S":
                unpack(b, fb[b], (qx, sx, 0, C))
        if r == R - 1:
            halves = ((0, CFG["final"]), (CFG["final"], C))
        for a, e in halves:
            for b in range(4):
                product = by(at("pr", C * b, C * b + C), at("plo", a // 16, e // 16))
                out = at("xn", 4 * a + b, 4 * e, 4)
                if CFG["state"][b] == "V":
                    vtt(out, product, at("fo", C * b + a, C * b + e), ALU.add)
                else:
                    copy("VS", at("gx", C * b + a, C * b + e), product)
                    vtt(out, bank(fb[b], e, a), at("gx", C * b + a, C * b + e), ALU.add)
        tile = "xn"

    cuts, pl["begin"] = pl["cuts"], begins[0]
    head = [k for k in range(begins[0], cuts[0]) if k not in extra]
    pl["like"].update({k: begins[1] - cuts[0] + i for i, k in enumerate(head)})
    pl["like"].update({k: (k - cuts[0]) % (cuts[1] - cuts[0]) for k in range(cuts[0], len(pl["ops"]))})

    for k, (a, b) in enumerate(halves):
        store("Y", T.oc[:, 4 * a:4 * b], T[qx][:, a:b].bitcast(dt.uint8), at(qx, a, b))
        copy("VS", at("ys", a, b), bank(sb[k], b - a))
        store("YS"[k], T.y[:, a:b], T.ys[:, a:b], at("ys", a, b))
    for k in range(4):
        store("Y" if k < 2 else "S", T.osc[4 * k:4 * k + 4, :], T[sx][32 * k:32 * k + 4, :], at(sx), 16)
    return pl
